import numpy as np
import ml_dtypes


def mxq(x, axis, fmt="e4m3"):
    dtype, down = {"e4m3": (ml_dtypes.float8_e4m3fn, 7), "e5m2": (ml_dtypes.float8_e5m2, 14)}[fmt]
    v = np.moveaxis(np.asarray(x, np.float32).astype(ml_dtypes.bfloat16).astype(np.float64), axis, -1)
    blocks = v.reshape(v.shape[:-1] + (-1, 32))
    amax = np.abs(blocks).max(-1, keepdims=True)
    byte = np.maximum(np.where(amax > 0, np.frexp(amax)[1] - 1 + 127, 0) - down, 1)
    scale = np.exp2(byte - 127.0)
    codes = (blocks / scale).astype(np.float32).astype(dtype).astype(np.float64)
    return np.moveaxis((codes * scale).reshape(v.shape), -1, axis)


WIDE = False


def mx_kscale(k):
    if not WIDE:
        return np.ones(k)
    levels = np.array([10, -10, 5, -5, 0])
    if k % 512:
        return np.exp2(np.random.permutation(np.resize(levels, k // 32))).repeat(32)
    a = np.empty((k // 512, 16))
    for p in range(k // 512):
        a[p, :8] = np.random.permutation(np.resize(levels, 8))
        for g in range(8):
            far = levels[np.abs(levels - a[p, g]) >= 10]
            a[p, g + 8] = far[np.random.randint(len(far))]
    return np.exp2(a.ravel()).repeat(32)


def f64(x):
    return np.asarray(x).astype(np.float64)


def striped(idx):
    return np.tile(idx.reshape(-1, 16).T, (8, 1)).astype(np.uint16)


def unstriped(offs):
    return offs[:16].T.reshape(-1).astype(np.int64)


E2M1 = np.array([0.0, 0.5, 1.0, 1.5, 2.0, 3.0, 4.0, 6.0, -0.0, -0.5, -1.0, -1.5, -2.0, -3.0, -4.0, -6.0])


def pack_weight(w, fmt):
    k, n = w.shape
    w = f64(np.asarray(w, np.float32).astype(ml_dtypes.bfloat16)).reshape(k // 32, 32, n)
    amax = np.abs(w).max(1)
    if fmt == "e4m3":
        byte = np.frexp(amax)[1] - 1 + 127 - 7
    else:
        mant, ex = np.frexp(amax / 6.0)
        byte = np.where(mant > 0.5, ex, ex - 1) + 127
    byte = np.clip(np.where(amax > 0, byte, 1), 1, 254)
    scaled = (w * np.exp2(127.0 - byte)[:, None, :]).reshape(k, n).astype(np.float32)
    by_word = np.ascontiguousarray(scaled.reshape(k // 512, 128, 4, n).transpose(0, 1, 3, 2))
    if fmt == "e4m3":
        words = by_word.astype(ml_dtypes.float8_e4m3fn).view(np.uint8)
    else:
        c = by_word.astype(ml_dtypes.float4_e2m1fn).view(np.uint8) & 0xF
        words = (c[..., 0::2] | (c[..., 1::2] << 4)).reshape(k // 512, 128, 2 * n)
    return np.ascontiguousarray(words), np.ascontiguousarray(byte.astype(np.uint8).reshape(k // 512, 16, n))


def unpack_weight(words, scales, fmt):
    g, _, n = scales.shape
    words = np.ascontiguousarray(words).reshape(g, 128, n, -1)
    if fmt == "e4m3":
        vals = words.view(ml_dtypes.float8_e4m3fn).astype(np.float64)
    else:
        nib = np.empty((g, 128, n, 4), np.uint8)
        nib[..., 0::2] = words & 0xF
        nib[..., 1::2] = words >> 4
        vals = E2M1[nib]
    vals = vals * np.repeat(np.exp2(scales.astype(np.float64) - 127.0), 8, axis=1)[..., None]
    return vals.transpose(0, 1, 3, 2).reshape(g * 512, n)


def relu2(v):
    return np.maximum(v, 0.0) ** 2


K, T, E, C, H, N = 512, 768, 12, 128, 512, 512


def by_expert(wq, xq):
    return np.concatenate([wq[e].T @ xq[:, e * C:(e + 1) * C] for e in range(E)], axis=1)


def setup_inputs():
    n = np.random.standard_normal
    s = mx_kscale(K)
    u = mx_kscale(H)
    first = np.random.permutation(np.repeat(np.arange(E), T // E))
    second = (first + 1 + np.random.permutation(np.repeat(np.arange(E - 1), -(-T // (E - 1)))[:T])) % E
    while np.bincount(second, minlength=E).max() != T // E:
        load = np.bincount(second, minlength=E); hi, lo = int(load.argmax()), int(load.argmin())
        t = np.flatnonzero((second == hi) & (first != lo))[0]; second[t] = lo
    slot_token = np.empty(E * C, np.int64); pos = np.empty((2, T), np.int64); fill = np.zeros(E, np.int64)
    place = np.stack([np.random.permutation(C) for _ in range(E)])
    for r, deal in enumerate((first, second)):
        for t in np.random.permutation(T):
            e = deal[t]; j = e * C + place[e, fill[e]]; fill[e] += 1; slot_token[j] = t; pos[r, t] = j
    g = np.random.uniform(0.2, 0.8, T)
    partner = np.concatenate([np.random.permutation(T) for _ in range(-(-E * C // T))])[:E * C]
    x = pack_weight(n((K, T)) * s[:, None], "e4m3")
    w1 = [pack_weight(m, "e2m1") for m in n((E, K, H)) / np.sqrt(K) / s[None, :, None] * u]
    w2 = [pack_weight(m, "e2m1") for m in n((E, H, N)) / np.sqrt(H) / u[None, :, None] ** 2]
    return {
        "x_words": x[0],
        "x_scales": x[1],
        "w1_words": np.stack([m[0] for m in w1]),
        "w1_scales": np.stack([m[1] for m in w1]),
        "wp": (n((E, K, H)) / np.sqrt(K) / s[None, :, None] * u).astype(np.float32),
        "w2_words": np.stack([m[0] for m in w2]),
        "w2_scales": np.stack([m[1] for m in w2]),
        "gate": np.stack([np.tile(g, (128, 1)), np.tile(1.0 - g, (128, 1))]).astype(np.float32),
        "offs": striped(slot_token),
        "pos1": striped(pos[0]),
        "pos2": striped(pos[1]),
        "offs2": striped(partner),
    }


def reference(x_words, x_scales, w1_words, w1_scales, wp, w2_words, w2_scales, gate, offs, pos1, pos2, offs2):
    w1 = np.stack([unpack_weight(w1_words[e], w1_scales[e], "e2m1") for e in range(E)])
    wpq = mxq(f64(wp), 1, "e4m3")
    w2 = np.stack([unpack_weight(w2_words[e], w2_scales[e], "e2m1") for e in range(E)])
    idx, idx2 = unstriped(offs), unstriped(offs2)
    x = unpack_weight(x_words, x_scales, "e4m3")
    h = relu2(by_expert(w1, x[:, idx]) + by_expert(wpq, x[:, idx2]))
    y = by_expert(w2, mxq(h, 0, "e4m3"))
    out = sum(f64(gate[r, :1]) * y[:, unstriped(p)] for r, p in enumerate((pos1, pos2)))
    return out

@@ -1,0 +1,186 @@
+from contextlib import ExitStack
+
+import concourse.mybir as mybir
+from concourse.masks import make_identity
+
+K, T, E, C, H, N = 512, 768, 12, 128, 512, 512
+S = E * C
+P = 128
+PACK = 4
+FLOPS = 2 * S * (2 * K * H + H * N)
+
+F32 = mybir.dt.float32
+BF16 = mybir.dt.bfloat16
+I32 = mybir.dt.int32
+U32 = mybir.dt.uint32
+U16 = mybir.dt.uint16
+U8 = mybir.dt.uint8
+FP8X4 = mybir.dt.float8_e4m3fn_x4
+FP4X4 = mybir.dt.float4_e2m1fn_x4
+ACT = mybir.ActivationFunctionType
+ALU = mybir.AluOpType
+
+PAIR = 2
+GROUP = 4
+CAST_ON_VECTOR = 224
+
+
+def load_scale_rows(nc, plane, rows):
+    by_row = rows.bitcast(I32).rearrange("m (q r) w -> r q m w", r=4)
+    for r in range(4):
+        nc.sync.dma_start(out=plane.bitcast(I32)[r:P:32, :, :], in_=by_row[r])
+
+
+def tile_moe_duo_relu2_kernel(tc, x_words, x_scales, w1_words, w1_scales, wp, w2_words, w2_scales, gate, offs, pos1, pos2, offs2, out):
+    nc = tc.nc
+    with ExitStack() as ctx:
+        keep = ctx.enter_context(tc.tile_pool(name="keep", bufs=1))
+        ring = ctx.enter_context(tc.tile_pool(name="ring", bufs=3))
+        psum = ctx.enter_context(tc.psum_pool(name="psum", bufs=2))
+
+        token_list = keep.tile([P, S // 16], U16, name="token_list")
+        partner_list = keep.tile([P, S // 16], U16, name="partner_list")
+        slot_lists = [keep.tile([P, T // 16], U16, name="slot_list%d" % r) for r in range(2)]
+        x_w = keep.tile([P, T], I32, name="x_w", align_bytes=64)
+        x_s = keep.tile([P, 1, T], U8, name="x_s", align_bytes=64)
+        w1_s = keep.tile([P, E, H], U8, name="w1_s", align_bytes=64)
+        w2_s = keep.tile([P, E, N], U8, name="w2_s", align_bytes=64)
+        w1_w = [keep.tile([P, PAIR, 2 * H], U8, name="w1_w%d" % i, align_bytes=64) for i in range(E // PAIR)]
+        w2_w = [keep.tile([P, GROUP, 2 * N], U8, name="w2_w%d" % i, align_bytes=64) for i in range(E // GROUP)]
+        wp_raw = [keep.tile([P, PACK, H], F32, name="wp_raw%d" % e) for e in range(E)]
+        gates = [keep.tile([P, T], F32, name="gate%d" % r) for r in range(2)]
+        ident = keep.tile([P, P], F32, name="ident")
+        h_w = keep.tile([P, S], U32, name="h_w", align_bytes=64)
+        h_s = keep.tile([P, S], U8, name="h_s", align_bytes=64)
+        y = [keep.tile([P, S], F32, name="y%d" % b) for b in range(N // P)]
+
+        nc.vector.memset(x_s[:].bitcast(I32), 0)
+        nc.vector.memset(w1_s[:].bitcast(I32), 0)
+        nc.gpsimd.memset(w2_s[:].bitcast(I32), 0)
+        make_identity(nc, ident[:])
+
+        def load_packed(tile, words, e0, count):
+            nc.sync.dma_start(out=tile[:].bitcast(I32), in_=words[e0 : e0 + count, 0].bitcast(I32).rearrange("e p w -> p e w"))
+
+        nc.sync.dma_start(token_list[:], offs)
+        nc.sync.dma_start(out=x_w[:], in_=x_words[0].rearrange("p t d -> p (t d)").bitcast(I32))
+        load_scale_rows(nc, x_s[:], x_scales)
+        nc.sync.dma_start(partner_list[:], offs2)
+        for e in range(E):
+            nc.sync.dma_start(out=wp_raw[e][:], in_=wp[e].rearrange("(p j) c -> p j c", j=PACK))
+            if e == 0:
+                load_scale_rows(nc, w1_s[:], w1_scales[:, 0])
+            if e % PAIR == 0:
+                load_packed(w1_w[e // PAIR], w1_words, e, PAIR)
+        load_scale_rows(nc, w2_s[:], w2_scales[:, 0])
+        for g in range(E // GROUP):
+            load_packed(w2_w[g], w2_words, g * GROUP, GROUP)
+        nc.sync.dma_start(slot_lists[0][:], pos1)
+        nc.sync.dma_start(slot_lists[1][:], pos2)
+        for r in range(2):
+            nc.sync.dma_start(out=gates[r][:], in_=gate[r])
+
+        gathered = {}
+
+        def gather(i, which):
+            lst = (token_list, partner_list)[which][:, i * PAIR * C // 16 : (i + 1) * PAIR * C // 16]
+            words = ring.tile([P, PAIR * C], U32, name="g_w%d" % which, bufs=2, align_bytes=64)
+            scales = ring.tile([P, PAIR * C], U8, name="g_s%d" % which, bufs=2, align_bytes=64)
+            nc.vector.tensor_copy(words[:], x_w[:].bitcast(U32).indirect(lst))
+            nc.vector.tensor_copy(scales[:], x_s[:, 0, :].indirect(lst))
+            gathered[(which, i)] = (words, scales)
+
+        wp_bf, wp_q, pre, relu, turned, h_bf = {}, {}, {}, {}, {}, {}
+
+        def cast(e):
+            wp_bf[e] = ring.tile([P, H, PACK], BF16, name="wp_bf", align_bytes=64)
+            for engine_copy, c0, c1 in ((nc.scalar.copy, CAST_ON_VECTOR, H), (nc.vector.tensor_copy, 0, CAST_ON_VECTOR)):
+                engine_copy(
+                    wp_bf[e][:, c0:c1, :].rearrange("p (c i) j -> p c j i", i=4),
+                    wp_raw[e][:, :, c0:c1].rearrange("p j (c i) -> p c j i", i=4),
+                )
+
+        def quantize_wp(e):
+            words = ring.tile([P, H], U32, name="wp_w", align_bytes=64)
+            scales = ring.tile([P, H], U8, name="wp_s", align_bytes=64)
+            nc.vector.quantize_mx(out=words[:].bitcast(FP8X4), scales=scales[:], in_=wp_bf[e][:].rearrange("p c j -> p (c j)"))
+            wp_q[e] = (words, scales)
+
+        def first_layer(e):
+            pre[e] = psum.tile([P, H], F32, name="pre")
+            cols = slice((e % PAIR) * C, (e % PAIR + 1) * C)
+            tok_w, tok_s = gathered[(0, e // PAIR)]
+            par_w, par_s = gathered[(1, e // PAIR)]
+            nc.tensor.matmul_mx(
+                out=pre[e][:], lhsT=tok_w[:, cols].bitcast(FP8X4), lhsT_scale=tok_s[:, cols],
+                rhs=w1_w[e // PAIR][:, e % PAIR, :].bitcast(FP4X4), rhs_scale=w1_s[:, e, :], start=True, stop=False,
+            )
+            nc.tensor.matmul_mx(
+                out=pre[e][:], lhsT=par_w[:, cols].bitcast(FP8X4), lhsT_scale=par_s[:, cols],
+                rhs=wp_q[e][0][:].bitcast(FP8X4), rhs_scale=wp_q[e][1][:], start=False, stop=True,
+            )
+
+        def relu_and_turn(e):
+            relu[e] = ring.tile([P, PACK, P], F32, name="relu")
+            nc.scalar.activation(relu[e][:], pre[e][:].rearrange("s (p t) -> s t p", t=PACK), ACT.Relu)
+            turned[e] = psum.tile([P, PACK, C], F32, name="turned")
+            for t in range(PACK):
+                nc.tensor.transpose(turned[e][:, t, :], relu[e][:, t, :], ident[:])
+
+        def square(e):
+            h_bf[e] = ring.tile([P, C, PACK], BF16, name="h_bf", align_bytes=64)
+            nc.scalar.activation(h_bf[e][:], turned[e][:].rearrange("p t s -> p s t"), ACT.Square)
+
+        def quantize_h(e):
+            cols = slice(e * C, (e + 1) * C)
+            nc.vector.quantize_mx(out=h_w[:, cols].bitcast(FP8X4), scales=h_s[:, cols], in_=h_bf[e][:].rearrange("p s t -> p (s t)"))
+
+        gather(0, 0)
+        gather(0, 1)
+        for step in range(E + 3):
+            if step < E:
+                cast(step)
+            if 0 <= step - 3 < E:
+                quantize_h(step - 3)
+            if step // PAIR + 1 < E // PAIR:
+                gather(step // PAIR + 1, step % PAIR)
+            if step < E:
+                quantize_wp(step)
+                first_layer(step)
+            if 0 <= step - 1 < E:
+                relu_and_turn(step - 1)
+            if 0 <= step - 2 < E:
+                square(step - 2)
+
+        def second_layer(b):
+            for g in range(E // GROUP):
+                bank = psum.tile([P, GROUP * C], F32, name="y_bank", bufs=4)
+                for u in range(GROUP):
+                    e = g * GROUP + u
+                    nc.tensor.matmul_mx(
+                        out=bank[:, u * C : (u + 1) * C],
+                        lhsT=w2_w[g][:, u, 2 * P * b : 2 * P * (b + 1)].bitcast(FP4X4), lhsT_scale=w2_s[:, e, P * b : P * (b + 1)],
+                        rhs=h_w[:, e * C : (e + 1) * C].bitcast(FP8X4), rhs_scale=h_s[:, e * C : (e + 1) * C], start=True, stop=True,
+                    )
+                nc.scalar.copy(y[b][:, g * GROUP * C : (g + 1) * GROUP * C], bank[:])
+
+        parts = {}
+
+        def weigh(b, r):
+            parts[(b, r)] = ring.tile([P, T], F32, name="part%d" % r, bufs=2)
+            nc.vector.tensor_tensor(parts[(b, r)][:], y[b][:].indirect(slot_lists[r][:]), gates[r][:], ALU.mult)
+
+        def add_and_store(b):
+            total = ring.tile([P, T], F32, name="total", bufs=2)
+            nc.vector.tensor_tensor(total[:], parts[(b, 0)][:], parts[(b, 1)][:], ALU.add)
+            nc.sync.dma_start(out=out[b * P : (b + 1) * P, :], in_=total[:])
+
+        for b in range(N // P):
+            second_layer(b)
+        for b in range(N // P + 1):
+            if b < N // P:
+                weigh(b, 0)
+            if b >= 1:
+                add_and_store(b - 1)
+            if b < N // P:
+                weigh(b, 1)

@@ -22,7 +22,13 @@ ALU = mybir.AluOpType
 
 PAIR = 2
 GROUP = 4
-CAST_ON_VECTOR = 224
+CAST_ON_VECTOR = 192
+CAST_ON_VECTOR_LATE = 384
+AHEAD = 2
+HALF = T // 2
+LAST_SPLIT = 512
+REGION = PACK * H * 4
+RELU_AT, HIDDEN_AT, WORDS_AT, SCALES_AT = 0, 2048, 3072, 4096
 
 
 def load_scale_rows(nc, plane, rows):
@@ -36,6 +42,7 @@ def tile_moe_duo_relu2_kernel(tc, x_words, x_scales, w1_words, w1_scales, wp, w2
     with ExitStack() as ctx:
         keep = ctx.enter_context(tc.tile_pool(name="keep", bufs=1))
         ring = ctx.enter_context(tc.tile_pool(name="ring", bufs=3))
+        stage = ctx.enter_context(tc.tile_pool(name="stage", bufs=1))
         psum = ctx.enter_context(tc.psum_pool(name="psum", bufs=2))
 
         token_list = keep.tile([P, S // 16], U16, name="token_list")
@@ -47,17 +54,22 @@ def tile_moe_duo_relu2_kernel(tc, x_words, x_scales, w1_words, w1_scales, wp, w2
         w2_s = keep.tile([P, E, N], U8, name="w2_s", align_bytes=64)
         w1_w = [keep.tile([P, PAIR, 2 * H], U8, name="w1_w%d" % i, align_bytes=64) for i in range(E // PAIR)]
         w2_w = [keep.tile([P, GROUP, 2 * N], U8, name="w2_w%d" % i, align_bytes=64) for i in range(E // GROUP)]
-        wp_raw = [keep.tile([P, PACK, H], F32, name="wp_raw%d" % e) for e in range(E)]
+        wp_raw = [stage.tile([P, PACK, H], F32, name="wp_raw%d" % e, align_bytes=64, offset=e * REGION) for e in range(E)]
         gates = [keep.tile([P, T], F32, name="gate%d" % r) for r in range(2)]
         ident = keep.tile([P, P], F32, name="ident")
         h_w = keep.tile([P, S], U32, name="h_w", align_bytes=64)
         h_s = keep.tile([P, S], U8, name="h_s", align_bytes=64)
         y = [keep.tile([P, S], F32, name="y%d" % b) for b in range(N // P)]
 
-        nc.vector.memset(x_s[:].bitcast(I32), 0)
+        nc.gpsimd.memset(x_s[:].bitcast(I32), 0)
         nc.vector.memset(w1_s[:].bitcast(I32), 0)
-        nc.gpsimd.memset(w2_s[:].bitcast(I32), 0)
         make_identity(nc, ident[:])
+        nc.gpsimd.memset(w2_s[:].bitcast(I32), 0)
+
+        def staged(name, shape, dtype, step, at):
+            if 0 <= step < E:
+                return stage.tile(shape, dtype, name=name, align_bytes=64, offset=step * REGION + at)
+            return keep.tile(shape, dtype, name=name, align_bytes=64)
 
         def load_packed(tile, words, e0, count):
             nc.sync.dma_start(out=tile[:].bitcast(I32), in_=words[e0 : e0 + count, 0].bitcast(I32).rearrange("e p w -> p e w"))
@@ -73,28 +85,32 @@ def tile_moe_duo_relu2_kernel(tc, x_words, x_scales, w1_words, w1_scales, wp, w2
             if e % PAIR == 0:
                 load_packed(w1_w[e // PAIR], w1_words, e, PAIR)
         load_scale_rows(nc, w2_s[:], w2_scales[:, 0])
-        for g in range(E // GROUP):
-            load_packed(w2_w[g], w2_words, g * GROUP, GROUP)
         nc.sync.dma_start(slot_lists[0][:], pos1)
         nc.sync.dma_start(slot_lists[1][:], pos2)
+        for g in range(E // GROUP):
+            load_packed(w2_w[g], w2_words, g * GROUP, GROUP)
         for r in range(2):
             nc.sync.dma_start(out=gates[r][:], in_=gate[r])
 
         gathered = {}
 
-        def gather(i, which):
-            lst = (token_list, partner_list)[which][:, i * PAIR * C // 16 : (i + 1) * PAIR * C // 16]
-            words = ring.tile([P, PAIR * C], U32, name="g_w%d" % which, bufs=2, align_bytes=64)
-            scales = ring.tile([P, PAIR * C], U8, name="g_s%d" % which, bufs=2, align_bytes=64)
+        def gather(which, e0, step):
+            experts = [e for e in range(e0, e0 + PAIR) if 0 <= e < E]
+            count = len(experts) * C
+            lst = (token_list, partner_list)[which][:, experts[0] * C // 16 : (experts[-1] + 1) * C // 16]
+            words = staged("g_w%d_%d" % (which, experts[0]), [P, count], U32, step, WORDS_AT)
+            scales = staged("g_s%d_%d" % (which, experts[0]), [P, count], U8, step, SCALES_AT)
             nc.vector.tensor_copy(words[:], x_w[:].bitcast(U32).indirect(lst))
             nc.vector.tensor_copy(scales[:], x_s[:, 0, :].indirect(lst))
-            gathered[(which, i)] = (words, scales)
+            for u, e in enumerate(experts):
+                gathered[(which, e)] = (words[:, u * C : (u + 1) * C], scales[:, u * C : (u + 1) * C])
 
         wp_bf, wp_q, pre, relu, turned, h_bf = {}, {}, {}, {}, {}, {}
 
         def cast(e):
             wp_bf[e] = ring.tile([P, H, PACK], BF16, name="wp_bf", align_bytes=64)
-            for engine_copy, c0, c1 in ((nc.scalar.copy, CAST_ON_VECTOR, H), (nc.vector.tensor_copy, 0, CAST_ON_VECTOR)):
+            split = CAST_ON_VECTOR if e + AHEAD < E else CAST_ON_VECTOR_LATE
+            for engine_copy, c0, c1 in ((nc.scalar.copy, split, H), (nc.vector.tensor_copy, 0, split)):
                 engine_copy(
                     wp_bf[e][:, c0:c1, :].rearrange("p (c i) j -> p c j i", i=4),
                     wp_raw[e][:, :, c0:c1].rearrange("p j (c i) -> p c j i", i=4),
@@ -107,80 +123,91 @@ def tile_moe_duo_relu2_kernel(tc, x_words, x_scales, w1_words, w1_scales, wp, w2
             wp_q[e] = (words, scales)
 
         def first_layer(e):
-            pre[e] = psum.tile([P, H], F32, name="pre")
-            cols = slice((e % PAIR) * C, (e % PAIR + 1) * C)
-            tok_w, tok_s = gathered[(0, e // PAIR)]
-            par_w, par_s = gathered[(1, e // PAIR)]
+            pre[e] = psum.tile([P, H], F32, name="pre", bufs=3)
+            tok_w, tok_s = gathered[(0, e)]
+            par_w, par_s = gathered[(1, e)]
             nc.tensor.matmul_mx(
-                out=pre[e][:], lhsT=tok_w[:, cols].bitcast(FP8X4), lhsT_scale=tok_s[:, cols],
+                out=pre[e][:], lhsT=tok_w.bitcast(FP8X4), lhsT_scale=tok_s,
                 rhs=w1_w[e // PAIR][:, e % PAIR, :].bitcast(FP4X4), rhs_scale=w1_s[:, e, :], start=True, stop=False,
             )
             nc.tensor.matmul_mx(
-                out=pre[e][:], lhsT=par_w[:, cols].bitcast(FP8X4), lhsT_scale=par_s[:, cols],
+                out=pre[e][:], lhsT=par_w.bitcast(FP8X4), lhsT_scale=par_s,
                 rhs=wp_q[e][0][:].bitcast(FP8X4), rhs_scale=wp_q[e][1][:], start=False, stop=True,
             )
 
         def relu_and_turn(e):
-            relu[e] = ring.tile([P, PACK, P], F32, name="relu")
+            relu[e] = staged("relu%d" % e, [P, PACK, P], F32, e + 1, RELU_AT)
             nc.scalar.activation(relu[e][:], pre[e][:].rearrange("s (p t) -> s t p", t=PACK), ACT.Relu)
             turned[e] = psum.tile([P, PACK, C], F32, name="turned")
             for t in range(PACK):
                 nc.tensor.transpose(turned[e][:, t, :], relu[e][:, t, :], ident[:])
 
         def square(e):
-            h_bf[e] = ring.tile([P, C, PACK], BF16, name="h_bf", align_bytes=64)
+            h_bf[e] = staged("h_bf%d" % e, [P, C, PACK], BF16, e + 2, HIDDEN_AT)
             nc.scalar.activation(h_bf[e][:], turned[e][:].rearrange("p t s -> p s t"), ACT.Square)
 
         def quantize_h(e):
             cols = slice(e * C, (e + 1) * C)
             nc.vector.quantize_mx(out=h_w[:, cols].bitcast(FP8X4), scales=h_s[:, cols], in_=h_bf[e][:].rearrange("p s t -> p (s t)"))
 
-        gather(0, 0)
-        gather(0, 1)
-        for step in range(E + 3):
+        gather(0, 0, -1)
+        gather(1, -1, -1)
+        gather(1, 1, -1)
+        for step in range(E + 2):
             if step < E:
                 cast(step)
-            if 0 <= step - 3 < E:
-                quantize_h(step - 3)
-            if step // PAIR + 1 < E // PAIR:
-                gather(step // PAIR + 1, step % PAIR)
-            if step < E:
                 quantize_wp(step)
                 first_layer(step)
+            if step + AHEAD < E:
+                gather(step % PAIR, step + AHEAD, step)
             if 0 <= step - 1 < E:
                 relu_and_turn(step - 1)
             if 0 <= step - 2 < E:
                 square(step - 2)
+                quantize_h(step - 2)
 
-        def second_layer(b):
+        def second_layer(b, experts, engine_copy):
+            bank = psum.tile([P, len(experts) * C], F32, name="y_bank", bufs=3)
+            for u, e in enumerate(experts):
+                nc.tensor.matmul_mx(
+                    out=bank[:, u * C : (u + 1) * C],
+                    lhsT=w2_w[e // GROUP][:, e % GROUP, 2 * P * b : 2 * P * (b + 1)].bitcast(FP4X4), lhsT_scale=w2_s[:, e, P * b : P * (b + 1)],
+                    rhs=h_w[:, e * C : (e + 1) * C].bitcast(FP8X4), rhs_scale=h_s[:, e * C : (e + 1) * C], start=True, stop=True,
+                )
+            engine_copy(y[b][:, experts[0] * C : (experts[-1] + 1) * C], bank[:])
+
+        for experts in (range(0, 4), range(4, 8), range(8, E - 1)):
+            second_layer(0, experts, nc.vector.tensor_copy)
+        second_layer(0, range(E - 1, E), nc.scalar.copy)
+        for b in range(1, N // P):
             for g in range(E // GROUP):
-                bank = psum.tile([P, GROUP * C], F32, name="y_bank", bufs=4)
-                for u in range(GROUP):
-                    e = g * GROUP + u
-                    nc.tensor.matmul_mx(
-                        out=bank[:, u * C : (u + 1) * C],
-                        lhsT=w2_w[g][:, u, 2 * P * b : 2 * P * (b + 1)].bitcast(FP4X4), lhsT_scale=w2_s[:, e, P * b : P * (b + 1)],
-                        rhs=h_w[:, e * C : (e + 1) * C].bitcast(FP8X4), rhs_scale=h_s[:, e * C : (e + 1) * C], start=True, stop=True,
-                    )
-                nc.scalar.copy(y[b][:, g * GROUP * C : (g + 1) * GROUP * C], bank[:])
+                second_layer(b, range(g * GROUP, (g + 1) * GROUP), nc.scalar.copy)
 
-        parts = {}
+        def weigh(b, r, t0, t1):
+            part = ring.tile([P, t1 - t0], F32, name="part%d" % r, bufs=2)
+            nc.vector.tensor_tensor(part[:], y[b][:].indirect(slot_lists[r][:, t0 // 16 : t1 // 16]), gates[r][:, t0:t1], ALU.mult)
+            return part
 
-        def weigh(b, r):
-            parts[(b, r)] = ring.tile([P, T], F32, name="part%d" % r, bufs=2)
-            nc.vector.tensor_tensor(parts[(b, r)][:], y[b][:].indirect(slot_lists[r][:]), gates[r][:], ALU.mult)
-
-        def add_and_store(b):
+        def add_on_tensor(b, parts):
             total = ring.tile([P, T], F32, name="total", bufs=2)
-            nc.vector.tensor_tensor(total[:], parts[(b, 0)][:], parts[(b, 1)][:], ALU.add)
+            for t0 in range(0, T, HALF):
+                sum_bank = psum.tile([P, HALF], F32, name="y_bank", bufs=3)
+                for c in range(0, HALF, P):
+                    for r in range(2):
+                        nc.tensor.matmul(sum_bank[:, c : c + P], parts[r][:, t0 + c : t0 + c + P], ident[:], start=(r == 0), stop=(r == 1), is_transpose=True)
+                by_token = ring.tile([P, HALF], F32, name="by_token", bufs=3)
+                nc.scalar.copy(by_token[:], sum_bank[:])
+                back_bank = psum.tile([P, HALF], F32, name="pre", bufs=3)
+                for c in range(0, HALF, P):
+                    nc.tensor.transpose(back_bank[:, c : c + P], by_token[:, c : c + P], ident[:])
+                nc.scalar.copy(total[:, t0 : t0 + HALF], back_bank[:])
             nc.sync.dma_start(out=out[b * P : (b + 1) * P, :], in_=total[:])
 
-        for b in range(N // P):
-            second_layer(b)
-        for b in range(N // P + 1):
-            if b < N // P:
-                weigh(b, 0)
-            if b >= 1:
-                add_and_store(b - 1)
-            if b < N // P:
-                weigh(b, 1)
+        last = N // P - 1
+        for b in range(last):
+            add_on_tensor(b, [weigh(b, r, 0, T) for r in range(2)])
+        for t0, t1 in ((0, LAST_SPLIT), (LAST_SPLIT, T)):
+            parts = [weigh(last, r, t0, t1) for r in range(2)]
+            total = ring.tile([P, t1 - t0], F32, name="total", bufs=2)
+            nc.vector.tensor_tensor(total[:], parts[0][:], parts[1][:], ALU.add)
+            nc.sync.dma_start(out=out[last * P : (last + 1) * P, t0:t1], in_=total[:])

@@ -22,13 +22,15 @@ ALU = mybir.AluOpType
 
 PAIR = 2
 GROUP = 4
-CAST_ON_VECTOR = 192
-CAST_ON_VECTOR_LATE = 384
-AHEAD = 2
+CAST_BESIDE_GATHERS = 192
+W2_SCALES_AFTER = 8
+CAST_ALONE = 320
+BANK = 2048
+PRE_BANKS, TURNED_BANKS, Y_BANKS = (0, 1, 2), (3, 4), (5, 6, 7)
 HALF = T // 2
 LAST_SPLIT = 512
 REGION = PACK * H * 4
-RELU_AT, HIDDEN_AT, WORDS_AT, SCALES_AT = 0, 2048, 3072, 4096
+RELU_AT, HIDDEN_AT, GATHERED_AT = 0, 2048, 3072
 
 
 def load_scale_rows(nc, plane, rows):
@@ -43,17 +45,17 @@ def tile_moe_duo_relu2_kernel(tc, x_words, x_scales, w1_words, w1_scales, wp, w2
         keep = ctx.enter_context(tc.tile_pool(name="keep", bufs=1))
         ring = ctx.enter_context(tc.tile_pool(name="ring", bufs=3))
         stage = ctx.enter_context(tc.tile_pool(name="stage", bufs=1))
-        psum = ctx.enter_context(tc.psum_pool(name="psum", bufs=2))
+        psum = ctx.enter_context(tc.psum_pool(name="psum", bufs=1))
 
         token_list = keep.tile([P, S // 16], U16, name="token_list")
         partner_list = keep.tile([P, S // 16], U16, name="partner_list")
         slot_lists = [keep.tile([P, T // 16], U16, name="slot_list%d" % r) for r in range(2)]
         x_w = keep.tile([P, T], I32, name="x_w", align_bytes=64)
         x_s = keep.tile([P, 1, T], U8, name="x_s", align_bytes=64)
-        w1_s = keep.tile([P, E, H], U8, name="w1_s", align_bytes=64)
-        w2_s = keep.tile([P, E, N], U8, name="w2_s", align_bytes=64)
+        w1_s = [keep.tile([P, GROUP, H], U8, name="w1_s%d" % g, align_bytes=64) for g in range(E // GROUP)]
+        w2_s = [keep.tile([P, E, N // 2], U8, name="w2_s%d" % h, align_bytes=64) for h in range(2)]
         w1_w = [keep.tile([P, PAIR, 2 * H], U8, name="w1_w%d" % i, align_bytes=64) for i in range(E // PAIR)]
-        w2_w = [keep.tile([P, GROUP, 2 * N], U8, name="w2_w%d" % i, align_bytes=64) for i in range(E // GROUP)]
+        w2_w = [[keep.tile([P, GROUP, N], U8, name="w2_w%d_%d" % (h, g), align_bytes=64) for g in range(E // GROUP)] for h in range(2)]
         wp_raw = [stage.tile([P, PACK, H], F32, name="wp_raw%d" % e, align_bytes=64, offset=e * REGION) for e in range(E)]
         gates = [keep.tile([P, T], F32, name="gate%d" % r) for r in range(2)]
         ident = keep.tile([P, P], F32, name="ident")
@@ -62,17 +64,22 @@ def tile_moe_duo_relu2_kernel(tc, x_words, x_scales, w1_words, w1_scales, wp, w2
         y = [keep.tile([P, S], F32, name="y%d" % b) for b in range(N // P)]
 
         nc.gpsimd.memset(x_s[:].bitcast(I32), 0)
-        nc.vector.memset(w1_s[:].bitcast(I32), 0)
+        for plane in w1_s:
+            nc.vector.memset(plane[:].bitcast(I32), 0)
         make_identity(nc, ident[:])
-        nc.gpsimd.memset(w2_s[:].bitcast(I32), 0)
+        for plane in w2_s:
+            nc.gpsimd.memset(plane[:].bitcast(I32), 0)
 
         def staged(name, shape, dtype, step, at):
             if 0 <= step < E:
                 return stage.tile(shape, dtype, name=name, align_bytes=64, offset=step * REGION + at)
             return keep.tile(shape, dtype, name=name, align_bytes=64)
 
-        def load_packed(tile, words, e0, count):
-            nc.sync.dma_start(out=tile[:].bitcast(I32), in_=words[e0 : e0 + count, 0].bitcast(I32).rearrange("e p w -> p e w"))
+        def in_bank(name, shape, bank):
+            return psum.tile(shape, F32, name=name, offset=bank * BANK)
+
+        def load_packed(tile, words):
+            nc.sync.dma_start(out=tile[:].bitcast(I32), in_=words.bitcast(I32).rearrange("e p w -> p e w"))
 
         nc.sync.dma_start(token_list[:], offs)
         nc.sync.dma_start(out=x_w[:], in_=x_words[0].rearrange("p t d -> p (t d)").bitcast(I32))
@@ -80,37 +87,40 @@ def tile_moe_duo_relu2_kernel(tc, x_words, x_scales, w1_words, w1_scales, wp, w2
         nc.sync.dma_start(partner_list[:], offs2)
         for e in range(E):
             nc.sync.dma_start(out=wp_raw[e][:], in_=wp[e].rearrange("(p j) c -> p j c", j=PACK))
-            if e == 0:
-                load_scale_rows(nc, w1_s[:], w1_scales[:, 0])
+            if e % GROUP == 2 and e + 2 < E or e == 0:
+                g = (e + 2) // GROUP
+                load_scale_rows(nc, w1_s[g][:], w1_scales[g * GROUP : (g + 1) * GROUP, 0])
             if e % PAIR == 0:
-                load_packed(w1_w[e // PAIR], w1_words, e, PAIR)
-        load_scale_rows(nc, w2_s[:], w2_scales[:, 0])
+                load_packed(w1_w[e // PAIR], w1_words[e : e + PAIR, 0])
+            if e == W2_SCALES_AFTER:
+                load_scale_rows(nc, w2_s[0][:], w2_scales[:, 0, :, 0 : N // 2])
         nc.sync.dma_start(slot_lists[0][:], pos1)
         nc.sync.dma_start(slot_lists[1][:], pos2)
         for g in range(E // GROUP):
-            load_packed(w2_w[g], w2_words, g * GROUP, GROUP)
+            load_packed(w2_w[0][g], w2_words[g * GROUP : (g + 1) * GROUP, 0, :, 0:N])
         for r in range(2):
             nc.sync.dma_start(out=gates[r][:], in_=gate[r])
+        load_scale_rows(nc, w2_s[1][:], w2_scales[:, 0, :, N // 2 : N])
+        for g in range(E // GROUP):
+            load_packed(w2_w[1][g], w2_words[g * GROUP : (g + 1) * GROUP, 0, :, N : 2 * N])
 
         gathered = {}
 
-        def gather(which, e0, step):
-            experts = [e for e in range(e0, e0 + PAIR) if 0 <= e < E]
-            count = len(experts) * C
-            lst = (token_list, partner_list)[which][:, experts[0] * C // 16 : (experts[-1] + 1) * C // 16]
-            words = staged("g_w%d_%d" % (which, experts[0]), [P, count], U32, step, WORDS_AT)
-            scales = staged("g_s%d_%d" % (which, experts[0]), [P, count], U8, step, SCALES_AT)
-            nc.vector.tensor_copy(words[:], x_w[:].bitcast(U32).indirect(lst))
-            nc.vector.tensor_copy(scales[:], x_s[:, 0, :].indirect(lst))
-            for u, e in enumerate(experts):
-                gathered[(which, e)] = (words[:, u * C : (u + 1) * C], scales[:, u * C : (u + 1) * C])
+        def gather(g, sort, step):
+            which, is_scale = divmod(sort, 2)
+            lst = (token_list, partner_list)[which][:, g * GROUP * C // 16 : (g + 1) * GROUP * C // 16]
+            window = x_s[:, 0, :] if is_scale else x_w[:].bitcast(U32)
+            picked = staged("gathered%d_%d" % (g, sort), [P, GROUP * C], U8 if is_scale else U32, step, GATHERED_AT)
+            nc.vector.tensor_copy(picked[:], window.indirect(lst))
+            gathered[(g, sort)] = picked
 
         wp_bf, wp_q, pre, relu, turned, h_bf = {}, {}, {}, {}, {}, {}
 
         def cast(e):
             wp_bf[e] = ring.tile([P, H, PACK], BF16, name="wp_bf", align_bytes=64)
-            split = CAST_ON_VECTOR if e + AHEAD < E else CAST_ON_VECTOR_LATE
-            for engine_copy, c0, c1 in ((nc.scalar.copy, split, H), (nc.vector.tensor_copy, 0, split)):
+            split = 0 if e == 0 else CAST_BESIDE_GATHERS if e + GROUP < E else CAST_ALONE
+            shares = [(nc.scalar.copy, split, H), (nc.vector.tensor_copy, 0, split)]
+            for engine_copy, c0, c1 in shares[: 2 if split else 1]:
                 engine_copy(
                     wp_bf[e][:, c0:c1, :].rearrange("p (c i) j -> p c j i", i=4),
                     wp_raw[e][:, :, c0:c1].rearrange("p j (c i) -> p c j i", i=4),
@@ -123,12 +133,12 @@ def tile_moe_duo_relu2_kernel(tc, x_words, x_scales, w1_words, w1_scales, wp, w2
             wp_q[e] = (words, scales)
 
         def first_layer(e):
-            pre[e] = psum.tile([P, H], F32, name="pre", bufs=3)
-            tok_w, tok_s = gathered[(0, e)]
-            par_w, par_s = gathered[(1, e)]
+            pre[e] = in_bank("pre%d" % e, [P, H], PRE_BANKS[e % len(PRE_BANKS)])
+            cols = slice(e % GROUP * C, (e % GROUP + 1) * C)
+            tok_w, tok_s, par_w, par_s = [gathered[(e // GROUP, sort)][:, cols] for sort in range(4)]
             nc.tensor.matmul_mx(
                 out=pre[e][:], lhsT=tok_w.bitcast(FP8X4), lhsT_scale=tok_s,
-                rhs=w1_w[e // PAIR][:, e % PAIR, :].bitcast(FP4X4), rhs_scale=w1_s[:, e, :], start=True, stop=False,
+                rhs=w1_w[e // PAIR][:, e % PAIR, :].bitcast(FP4X4), rhs_scale=w1_s[e // GROUP][:, e % GROUP, :], start=True, stop=False,
             )
             nc.tensor.matmul_mx(
                 out=pre[e][:], lhsT=par_w.bitcast(FP8X4), lhsT_scale=par_s,
@@ -138,7 +148,7 @@ def tile_moe_duo_relu2_kernel(tc, x_words, x_scales, w1_words, w1_scales, wp, w2
         def relu_and_turn(e):
             relu[e] = staged("relu%d" % e, [P, PACK, P], F32, e + 1, RELU_AT)
             nc.scalar.activation(relu[e][:], pre[e][:].rearrange("s (p t) -> s t p", t=PACK), ACT.Relu)
-            turned[e] = psum.tile([P, PACK, C], F32, name="turned")
+            turned[e] = in_bank("turned%d" % e, [P, PACK, C], TURNED_BANKS[e % len(TURNED_BANKS)])
             for t in range(PACK):
                 nc.tensor.transpose(turned[e][:, t, :], relu[e][:, t, :], ident[:])
 
@@ -150,54 +160,64 @@ def tile_moe_duo_relu2_kernel(tc, x_words, x_scales, w1_words, w1_scales, wp, w2
             cols = slice(e * C, (e + 1) * C)
             nc.vector.quantize_mx(out=h_w[:, cols].bitcast(FP8X4), scales=h_s[:, cols], in_=h_bf[e][:].rearrange("p s t -> p (s t)"))
 
-        gather(0, 0, -1)
-        gather(1, -1, -1)
-        gather(1, 1, -1)
+        for sort in range(4):
+            gather(0, sort, -1)
         for step in range(E + 2):
             if step < E:
                 cast(step)
                 quantize_wp(step)
                 first_layer(step)
-            if step + AHEAD < E:
-                gather(step % PAIR, step + AHEAD, step)
+            if step + GROUP < E:
+                gather(step // GROUP + 1, step % GROUP, step)
             if 0 <= step - 1 < E:
                 relu_and_turn(step - 1)
             if 0 <= step - 2 < E:
                 square(step - 2)
                 quantize_h(step - 2)
 
-        def second_layer(b, experts, engine_copy):
-            bank = psum.tile([P, len(experts) * C], F32, name="y_bank", bufs=3)
+        def second_layer(turn, b, experts, engine_copy):
+            bank = in_bank("y_bank%d" % turn, [P, len(experts) * C], Y_BANKS[turn % len(Y_BANKS)])
             for u, e in enumerate(experts):
                 nc.tensor.matmul_mx(
                     out=bank[:, u * C : (u + 1) * C],
-                    lhsT=w2_w[e // GROUP][:, e % GROUP, 2 * P * b : 2 * P * (b + 1)].bitcast(FP4X4), lhsT_scale=w2_s[:, e, P * b : P * (b + 1)],
+                    lhsT=w2_w[b // 2][e // GROUP][:, e % GROUP, 2 * P * (b % 2) : 2 * P * (b % 2 + 1)].bitcast(FP4X4), lhsT_scale=w2_s[b // 2][:, e, P * (b % 2) : P * (b % 2 + 1)],
                     rhs=h_w[:, e * C : (e + 1) * C].bitcast(FP8X4), rhs_scale=h_s[:, e * C : (e + 1) * C], start=True, stop=True,
                 )
             engine_copy(y[b][:, experts[0] * C : (experts[-1] + 1) * C], bank[:])
 
-        for experts in (range(0, 4), range(4, 8), range(8, E - 1)):
-            second_layer(0, experts, nc.vector.tensor_copy)
-        second_layer(0, range(E - 1, E), nc.scalar.copy)
-        for b in range(1, N // P):
-            for g in range(E // GROUP):
-                second_layer(b, range(g * GROUP, (g + 1) * GROUP), nc.scalar.copy)
+        products = [
+            (0, range(0, GROUP), nc.vector.tensor_copy),
+            (0, range(GROUP, 2 * GROUP), nc.scalar.copy),
+            (0, range(2 * GROUP, E - 1), nc.vector.tensor_copy),
+            (0, range(E - 1, E), nc.scalar.copy),
+        ]
+        products.extend((b, range(e0, e0 + GROUP), nc.scalar.copy) for b in range(1, N // P) for e0 in range(0, E, GROUP))
+        for turn, product in enumerate(products):
+            second_layer(turn, *product)
+
+        taken = [0]
+
+        def spare(name, width):
+            tile = stage.tile([P, width], F32, name=name, align_bytes=64, offset=sum(taken))
+            taken.append(4 * width)
+            return tile
 
         def weigh(b, r, t0, t1):
-            part = ring.tile([P, t1 - t0], F32, name="part%d" % r, bufs=2)
+            part = spare("part%d_%d_%d" % (b, r, t0), t1 - t0)
             nc.vector.tensor_tensor(part[:], y[b][:].indirect(slot_lists[r][:, t0 // 16 : t1 // 16]), gates[r][:, t0:t1], ALU.mult)
             return part
 
         def add_on_tensor(b, parts):
-            total = ring.tile([P, T], F32, name="total", bufs=2)
+            total = spare("total%d" % b, T)
             for t0 in range(0, T, HALF):
-                sum_bank = psum.tile([P, HALF], F32, name="y_bank", bufs=3)
+                bank = Y_BANKS[(len(products) - 2 + t0 // HALF) % len(Y_BANKS)]
+                sum_bank = in_bank("sum%d_%d" % (b, t0), [P, HALF], bank)
                 for c in range(0, HALF, P):
                     for r in range(2):
                         nc.tensor.matmul(sum_bank[:, c : c + P], parts[r][:, t0 + c : t0 + c + P], ident[:], start=(r == 0), stop=(r == 1), is_transpose=True)
-                by_token = ring.tile([P, HALF], F32, name="by_token", bufs=3)
+                by_token = spare("by_token%d_%d" % (b, t0), HALF)
                 nc.scalar.copy(by_token[:], sum_bank[:])
-                back_bank = psum.tile([P, HALF], F32, name="pre", bufs=3)
+                back_bank = in_bank("back%d_%d" % (b, t0), [P, HALF], bank)
                 for c in range(0, HALF, P):
                     nc.tensor.transpose(back_bank[:, c : c + P], by_token[:, c : c + P], ident[:])
                 nc.scalar.copy(total[:, t0 : t0 + HALF], back_bank[:])
@@ -208,6 +228,6 @@ def tile_moe_duo_relu2_kernel(tc, x_words, x_scales, w1_words, w1_scales, wp, w2
             add_on_tensor(b, [weigh(b, r, 0, T) for r in range(2)])
         for t0, t1 in ((0, LAST_SPLIT), (LAST_SPLIT, T)):
             parts = [weigh(last, r, t0, t1) for r in range(2)]
-            total = ring.tile([P, t1 - t0], F32, name="total", bufs=2)
+            total = spare("total%d_%d" % (last, t0), t1 - t0)
             nc.vector.tensor_tensor(total[:], parts[0][:], parts[1][:], ALU.add)
             nc.sync.dma_start(out=out[last * P : (last + 1) * P, t0:t1], in_=total[:])

@@ -7,6 +7,7 @@ K, T, E, C, H, N = 512, 768, 12, 128, 512, 512
 S = E * C
 P = 128
 PACK = 4
+PER_COLUMN = 16
 FLOPS = 2 * S * (2 * K * H + H * N)
 
 F32 = mybir.dt.float32
@@ -22,24 +23,33 @@ ALU = mybir.AluOpType
 
 PAIR = 2
 GROUP = 4
-CAST_BESIDE_GATHERS = 192
+SORTS = 4
+
+CAST_FIRST = 128
+CAST_BESIDE_GATHERS = 256
+CAST_ALONE = 384
+
 W2_SCALES_AFTER = 8
-CAST_ALONE = 320
+ADDED_ON_TENSOR = 2
+HALF = T // 2
+LAST_SPLIT = 640
+
 BANK = 2048
 PRE_BANKS, TURNED_BANKS, Y_BANKS = (0, 1, 2), (3, 4), (5, 6, 7)
-HALF = T // 2
-LAST_SPLIT = 512
+
 REGION = PACK * H * 4
-RELU_AT, HIDDEN_AT, GATHERED_AT = 0, 2048, 3072
+RELU_AT, HIDDEN_AT, GATHERED_AT, H_WORDS_AT, H_SCALES_AT = 0, 2048, 3072, 5120, 5632
 
 
-def load_scale_rows(nc, plane, rows):
-    by_row = rows.bitcast(I32).rearrange("m (q r) w -> r q m w", r=4)
-    for r in range(4):
-        nc.sync.dma_start(out=plane.bitcast(I32)[r:P:32, :, :], in_=by_row[r])
+def load_scale_rows(nc, scale_tile, rows):
+    by_place = rows.bitcast(I32).rearrange("m (q j) w -> j q m w", j=4)
+    for j in range(4):
+        nc.sync.dma_start(out=scale_tile.bitcast(I32)[j:P:32, :, :], in_=by_place[j])
 
 
-def tile_moe_duo_relu2_kernel(tc, x_words, x_scales, w1_words, w1_scales, wp, w2_words, w2_scales, gate, offs, pos1, pos2, offs2, out):
+def tile_moe_duo_relu2_kernel(
+    tc, x_words, x_scales, w1_words, w1_scales, wp, w2_words, w2_scales, gate, offs, pos1, pos2, offs2, out
+):
     nc = tc.nc
     with ExitStack() as ctx:
         keep = ctx.enter_context(tc.tile_pool(name="keep", bufs=1))
@@ -47,28 +57,29 @@ def tile_moe_duo_relu2_kernel(tc, x_words, x_scales, w1_words, w1_scales, wp, w2
         stage = ctx.enter_context(tc.tile_pool(name="stage", bufs=1))
         psum = ctx.enter_context(tc.psum_pool(name="psum", bufs=1))
 
-        token_list = keep.tile([P, S // 16], U16, name="token_list")
-        partner_list = keep.tile([P, S // 16], U16, name="partner_list")
-        slot_lists = [keep.tile([P, T // 16], U16, name="slot_list%d" % r) for r in range(2)]
+        token_list = keep.tile([P, S // PER_COLUMN], U16, name="token_list")
+        partner_list = keep.tile([P, S // PER_COLUMN], U16, name="partner_list")
+        slot_lists = [keep.tile([P, T // PER_COLUMN], U16, name="slot_list%d" % r) for r in range(2)]
         x_w = keep.tile([P, T], I32, name="x_w", align_bytes=64)
         x_s = keep.tile([P, 1, T], U8, name="x_s", align_bytes=64)
         w1_s = [keep.tile([P, GROUP, H], U8, name="w1_s%d" % g, align_bytes=64) for g in range(E // GROUP)]
-        w2_s = [keep.tile([P, E, N // 2], U8, name="w2_s%d" % h, align_bytes=64) for h in range(2)]
-        w1_w = [keep.tile([P, PAIR, 2 * H], U8, name="w1_w%d" % i, align_bytes=64) for i in range(E // PAIR)]
-        w2_w = [[keep.tile([P, GROUP, N], U8, name="w2_w%d_%d" % (h, g), align_bytes=64) for g in range(E // GROUP)] for h in range(2)]
+        w2_s = [keep.tile([P, E, N // 2], U8, name="w2_s%d" % side, align_bytes=64) for side in range(2)]
+        w1_w = [keep.tile([P, PAIR, 2 * H], U8, name="w1_w%d" % pair, align_bytes=64) for pair in range(E // PAIR)]
+        w2_w = [
+            [keep.tile([P, GROUP, N], U8, name="w2_w%d_%d" % (side, g), align_bytes=64) for g in range(E // GROUP)]
+            for side in range(2)
+        ]
         wp_raw = [stage.tile([P, PACK, H], F32, name="wp_raw%d" % e, align_bytes=64, offset=e * REGION) for e in range(E)]
         gates = [keep.tile([P, T], F32, name="gate%d" % r) for r in range(2)]
         ident = keep.tile([P, P], F32, name="ident")
-        h_w = keep.tile([P, S], U32, name="h_w", align_bytes=64)
-        h_s = keep.tile([P, S], U8, name="h_s", align_bytes=64)
         y = [keep.tile([P, S], F32, name="y%d" % b) for b in range(N // P)]
 
         nc.gpsimd.memset(x_s[:].bitcast(I32), 0)
-        for plane in w1_s:
-            nc.vector.memset(plane[:].bitcast(I32), 0)
+        for scale_tile in w1_s:
+            nc.vector.memset(scale_tile[:].bitcast(I32), 0)
         make_identity(nc, ident[:])
-        for plane in w2_s:
-            nc.gpsimd.memset(plane[:].bitcast(I32), 0)
+        for scale_tile in w2_s:
+            nc.gpsimd.memset(scale_tile[:].bitcast(I32), 0)
 
         def staged(name, shape, dtype, step, at):
             if 0 <= step < E:
@@ -78,16 +89,16 @@ def tile_moe_duo_relu2_kernel(tc, x_words, x_scales, w1_words, w1_scales, wp, w2
         def in_bank(name, shape, bank):
             return psum.tile(shape, F32, name=name, offset=bank * BANK)
 
-        def load_packed(tile, words):
-            nc.sync.dma_start(out=tile[:].bitcast(I32), in_=words.bitcast(I32).rearrange("e p w -> p e w"))
+        def load_packed(word_tile, hbm_words):
+            nc.sync.dma_start(out=word_tile[:].bitcast(I32), in_=hbm_words.bitcast(I32).rearrange("e p w -> p e w"))
 
         nc.sync.dma_start(token_list[:], offs)
         nc.sync.dma_start(out=x_w[:], in_=x_words[0].rearrange("p t d -> p (t d)").bitcast(I32))
         load_scale_rows(nc, x_s[:], x_scales)
         nc.sync.dma_start(partner_list[:], offs2)
         for e in range(E):
-            nc.sync.dma_start(out=wp_raw[e][:], in_=wp[e].rearrange("(p j) c -> p j c", j=PACK))
-            if e % GROUP == 2 and e + 2 < E or e == 0:
+            nc.sync.dma_start(out=wp_raw[e][:], in_=wp[e].rearrange("(p d) c -> p d c", d=PACK))
+            if e == 0 or ((e + 2) % GROUP == 0 and e + 2 < E):
                 g = (e + 2) // GROUP
                 load_scale_rows(nc, w1_s[g][:], w1_scales[g * GROUP : (g + 1) * GROUP, 0])
             if e % PAIR == 0:
@@ -104,86 +115,106 @@ def tile_moe_duo_relu2_kernel(tc, x_words, x_scales, w1_words, w1_scales, wp, w2
         for g in range(E // GROUP):
             load_packed(w2_w[1][g], w2_words[g * GROUP : (g + 1) * GROUP, 0, :, N : 2 * N])
 
-        gathered = {}
+        gathered, wp_bf, wp_q, pre, turned, h_bf, h_q = {}, {}, {}, {}, {}, {}, {}
 
         def gather(g, sort, step):
-            which, is_scale = divmod(sort, 2)
-            lst = (token_list, partner_list)[which][:, g * GROUP * C // 16 : (g + 1) * GROUP * C // 16]
+            is_partner, is_scale = divmod(sort, 2)
+            columns = GROUP * C // PER_COLUMN
+            entries = (partner_list if is_partner else token_list)[:, g * columns : (g + 1) * columns]
             window = x_s[:, 0, :] if is_scale else x_w[:].bitcast(U32)
             picked = staged("gathered%d_%d" % (g, sort), [P, GROUP * C], U8 if is_scale else U32, step, GATHERED_AT)
-            nc.vector.tensor_copy(picked[:], window.indirect(lst))
+            nc.vector.tensor_copy(picked[:], window.indirect(entries))
             gathered[(g, sort)] = picked
 
-        wp_bf, wp_q, pre, relu, turned, h_bf = {}, {}, {}, {}, {}, {}
+        def has_gather(step):
+            return step + GROUP < E
 
         def cast(e):
             wp_bf[e] = ring.tile([P, H, PACK], BF16, name="wp_bf", align_bytes=64)
-            split = 0 if e == 0 else CAST_BESIDE_GATHERS if e + GROUP < E else CAST_ALONE
-            shares = [(nc.scalar.copy, split, H), (nc.vector.tensor_copy, 0, split)]
-            for engine_copy, c0, c1 in shares[: 2 if split else 1]:
+            split = CAST_FIRST if e == 0 else CAST_BESIDE_GATHERS if has_gather(e) else CAST_ALONE
+            for engine_copy, c0, c1 in ((nc.scalar.copy, split, H), (nc.vector.tensor_copy, 0, split)):
                 engine_copy(
-                    wp_bf[e][:, c0:c1, :].rearrange("p (c i) j -> p c j i", i=4),
-                    wp_raw[e][:, :, c0:c1].rearrange("p j (c i) -> p c j i", i=4),
+                    wp_bf[e][:, c0:c1, :].rearrange("p (c w) d -> p c d w", w=4),
+                    wp_raw[e][:, :, c0:c1].rearrange("p d (c w) -> p c d w", w=4),
                 )
 
         def quantize_wp(e):
-            words = ring.tile([P, H], U32, name="wp_w", align_bytes=64)
-            scales = ring.tile([P, H], U8, name="wp_s", align_bytes=64)
-            nc.vector.quantize_mx(out=words[:].bitcast(FP8X4), scales=scales[:], in_=wp_bf[e][:].rearrange("p c j -> p (c j)"))
-            wp_q[e] = (words, scales)
+            wp_w = ring.tile([P, H], U32, name="wp_w", align_bytes=64)
+            wp_s = ring.tile([P, H], U8, name="wp_s", align_bytes=64)
+            nc.vector.quantize_mx(out=wp_w[:].bitcast(FP8X4), scales=wp_s[:], in_=wp_bf[e][:].rearrange("p c d -> p (c d)"))
+            wp_q[e] = (wp_w, wp_s)
 
         def first_layer(e):
             pre[e] = in_bank("pre%d" % e, [P, H], PRE_BANKS[e % len(PRE_BANKS)])
-            cols = slice(e % GROUP * C, (e % GROUP + 1) * C)
-            tok_w, tok_s, par_w, par_s = [gathered[(e // GROUP, sort)][:, cols] for sort in range(4)]
+            slots = slice(e % GROUP * C, (e % GROUP + 1) * C)
+            token_w, token_s, partner_w, partner_s = [gathered[(e // GROUP, sort)][:, slots] for sort in range(SORTS)]
             nc.tensor.matmul_mx(
-                out=pre[e][:], lhsT=tok_w.bitcast(FP8X4), lhsT_scale=tok_s,
-                rhs=w1_w[e // PAIR][:, e % PAIR, :].bitcast(FP4X4), rhs_scale=w1_s[e // GROUP][:, e % GROUP, :], start=True, stop=False,
+                out=pre[e][:],
+                lhsT=token_w.bitcast(FP8X4),
+                lhsT_scale=token_s,
+                rhs=w1_w[e // PAIR][:, e % PAIR, :].bitcast(FP4X4),
+                rhs_scale=w1_s[e // GROUP][:, e % GROUP, :],
+                start=True,
+                stop=False,
             )
             nc.tensor.matmul_mx(
-                out=pre[e][:], lhsT=par_w.bitcast(FP8X4), lhsT_scale=par_s,
-                rhs=wp_q[e][0][:].bitcast(FP8X4), rhs_scale=wp_q[e][1][:], start=False, stop=True,
+                out=pre[e][:],
+                lhsT=partner_w.bitcast(FP8X4),
+                lhsT_scale=partner_s,
+                rhs=wp_q[e][0][:].bitcast(FP8X4),
+                rhs_scale=wp_q[e][1][:],
+                start=False,
+                stop=True,
             )
 
         def relu_and_turn(e):
-            relu[e] = staged("relu%d" % e, [P, PACK, P], F32, e + 1, RELU_AT)
-            nc.scalar.activation(relu[e][:], pre[e][:].rearrange("s (p t) -> s t p", t=PACK), ACT.Relu)
+            relu = staged("relu%d" % e, [P, PACK, P], F32, e + 1, RELU_AT)
+            nc.scalar.activation(relu[:], pre[e][:].rearrange("u (p d) -> u d p", d=PACK), ACT.Relu)
             turned[e] = in_bank("turned%d" % e, [P, PACK, C], TURNED_BANKS[e % len(TURNED_BANKS)])
-            for t in range(PACK):
-                nc.tensor.transpose(turned[e][:, t, :], relu[e][:, t, :], ident[:])
+            for d in range(PACK):
+                nc.tensor.transpose(turned[e][:, d, :], relu[:, d, :], ident[:])
 
         def square(e):
             h_bf[e] = staged("h_bf%d" % e, [P, C, PACK], BF16, e + 2, HIDDEN_AT)
-            nc.scalar.activation(h_bf[e][:], turned[e][:].rearrange("p t s -> p s t"), ACT.Square)
+            nc.scalar.activation(h_bf[e][:], turned[e][:].rearrange("p d u -> p u d"), ACT.Square)
 
         def quantize_h(e):
-            cols = slice(e * C, (e + 1) * C)
-            nc.vector.quantize_mx(out=h_w[:, cols].bitcast(FP8X4), scales=h_s[:, cols], in_=h_bf[e][:].rearrange("p s t -> p (s t)"))
+            h_w = staged("h_w%d" % e, [P, C], U32, e + 3, H_WORDS_AT)
+            h_s = staged("h_s%d" % e, [P, C], U8, e + 3, H_SCALES_AT)
+            nc.vector.quantize_mx(out=h_w[:].bitcast(FP8X4), scales=h_s[:], in_=h_bf[e][:].rearrange("p u d -> p (u d)"))
+            h_q[e] = (h_w, h_s)
 
-        for sort in range(4):
+        for sort in range(SORTS):
             gather(0, sort, -1)
-        for step in range(E + 2):
+        for step in range(E + 3):
             if step < E:
                 cast(step)
+            if step >= 3:
+                quantize_h(step - 3)
+            if step < E:
                 quantize_wp(step)
                 first_layer(step)
-            if step + GROUP < E:
+            if has_gather(step):
                 gather(step // GROUP + 1, step % GROUP, step)
             if 0 <= step - 1 < E:
                 relu_and_turn(step - 1)
             if 0 <= step - 2 < E:
                 square(step - 2)
-                quantize_h(step - 2)
 
         def second_layer(turn, b, experts, engine_copy):
-            bank = in_bank("y_bank%d" % turn, [P, len(experts) * C], Y_BANKS[turn % len(Y_BANKS)])
-            for u, e in enumerate(experts):
+            bank_tile = in_bank("y_bank%d" % turn, [P, len(experts) * C], Y_BANKS[turn % len(Y_BANKS)])
+            side, within = divmod(b, 2)
+            for place, e in enumerate(experts):
                 nc.tensor.matmul_mx(
-                    out=bank[:, u * C : (u + 1) * C],
-                    lhsT=w2_w[b // 2][e // GROUP][:, e % GROUP, 2 * P * (b % 2) : 2 * P * (b % 2 + 1)].bitcast(FP4X4), lhsT_scale=w2_s[b // 2][:, e, P * (b % 2) : P * (b % 2 + 1)],
-                    rhs=h_w[:, e * C : (e + 1) * C].bitcast(FP8X4), rhs_scale=h_s[:, e * C : (e + 1) * C], start=True, stop=True,
+                    out=bank_tile[:, place * C : (place + 1) * C],
+                    lhsT=w2_w[side][e // GROUP][:, e % GROUP, 2 * P * within : 2 * P * (within + 1)].bitcast(FP4X4),
+                    lhsT_scale=w2_s[side][:, e, P * within : P * (within + 1)],
+                    rhs=h_q[e][0][:].bitcast(FP8X4),
+                    rhs_scale=h_q[e][1][:],
+                    start=True,
+                    stop=True,
                 )
-            engine_copy(y[b][:, experts[0] * C : (experts[-1] + 1) * C], bank[:])
+            engine_copy(y[b][:, experts[0] * C : (experts[-1] + 1) * C], bank_tile[:])
 
         products = [
             (0, range(0, GROUP), nc.vector.tensor_copy),
@@ -195,39 +226,56 @@ def tile_moe_duo_relu2_kernel(tc, x_words, x_scales, w1_words, w1_scales, wp, w2
         for turn, product in enumerate(products):
             second_layer(turn, *product)
 
-        taken = [0]
+        used = [0] * E
 
         def spare(name, width):
-            tile = stage.tile([P, width], F32, name=name, align_bytes=64, offset=sum(taken))
-            taken.append(4 * width)
-            return tile
+            region = min(e for e in range(E) if used[e] + 4 * width <= H_WORDS_AT)
+            at = region * REGION + used[region]
+            used[region] = used[region] + 4 * width
+            return stage.tile([P, width], F32, name=name, align_bytes=64, offset=at)
 
         def weigh(b, r, t0, t1):
             part = spare("part%d_%d_%d" % (b, r, t0), t1 - t0)
-            nc.vector.tensor_tensor(part[:], y[b][:].indirect(slot_lists[r][:, t0 // 16 : t1 // 16]), gates[r][:, t0:t1], ALU.mult)
+            entries = slot_lists[r][:, t0 // PER_COLUMN : t1 // PER_COLUMN]
+            nc.vector.tensor_tensor(part[:], y[b][:].indirect(entries), gates[r][:, t0:t1], ALU.mult)
             return part
 
         def add_on_tensor(b, parts):
-            total = spare("total%d" % b, T)
             for t0 in range(0, T, HALF):
-                bank = Y_BANKS[(len(products) - 2 + t0 // HALF) % len(Y_BANKS)]
-                sum_bank = in_bank("sum%d_%d" % (b, t0), [P, HALF], bank)
-                for c in range(0, HALF, P):
+                sum_bank = in_bank("sum%d_%d" % (b, t0), [P, HALF], Y_BANKS[(len(products) - 2 + t0 // HALF) % len(Y_BANKS)])
+                for col in range(0, HALF, P):
                     for r in range(2):
-                        nc.tensor.matmul(sum_bank[:, c : c + P], parts[r][:, t0 + c : t0 + c + P], ident[:], start=(r == 0), stop=(r == 1), is_transpose=True)
+                        nc.tensor.matmul(
+                            sum_bank[:, col : col + P],
+                            parts[r][:, t0 + col : t0 + col + P],
+                            ident[:],
+                            start=(r == 0),
+                            stop=(r == 1),
+                            is_transpose=True,
+                        )
                 by_token = spare("by_token%d_%d" % (b, t0), HALF)
                 nc.scalar.copy(by_token[:], sum_bank[:])
-                back_bank = in_bank("back%d_%d" % (b, t0), [P, HALF], bank)
-                for c in range(0, HALF, P):
-                    nc.tensor.transpose(back_bank[:, c : c + P], by_token[:, c : c + P], ident[:])
-                nc.scalar.copy(total[:, t0 : t0 + HALF], back_bank[:])
-            nc.sync.dma_start(out=out[b * P : (b + 1) * P, :], in_=total[:])
+                back_bank = in_bank("back%d_%d" % (b, t0), [P, HALF], TURNED_BANKS[t0 // HALF])
+                for col in range(0, HALF, P):
+                    nc.tensor.transpose(back_bank[:, col : col + P], by_token[:, col : col + P], ident[:])
+                total = spare("total%d_%d" % (b, t0), HALF)
+                nc.scalar.copy(total[:], back_bank[:])
+                nc.scalar.dma_start(out=out[b * P : (b + 1) * P, t0 : t0 + HALF], in_=total[:])
 
-        last = N // P - 1
-        for b in range(last):
-            add_on_tensor(b, [weigh(b, r, 0, T) for r in range(2)])
-        for t0, t1 in ((0, LAST_SPLIT), (LAST_SPLIT, T)):
-            parts = [weigh(last, r, t0, t1) for r in range(2)]
-            total = spare("total%d_%d" % (last, t0), t1 - t0)
+        def add_on_vector(b, t0, t1, parts):
+            total = spare("total%d_%d" % (b, t0), t1 - t0)
             nc.vector.tensor_tensor(total[:], parts[0][:], parts[1][:], ALU.add)
-            nc.sync.dma_start(out=out[last * P : (last + 1) * P, t0:t1], in_=total[:])
+            nc.sync.dma_start(out=out[b * P : (b + 1) * P, t0:t1], in_=total[:])
+
+        for b in range(ADDED_ON_TENSOR):
+            add_on_tensor(b, [weigh(b, r, 0, T) for r in range(2)])
+        last = N // P - 1
+        pieces = [(b, 0, T) for b in range(ADDED_ON_TENSOR, last)] + [(last, 0, LAST_SPLIT), (last, LAST_SPLIT, T)]
+        waiting = None
+        for b, t0, t1 in pieces:
+            parts = [weigh(b, 0, t0, t1)]
+            if waiting:
+                add_on_vector(*waiting)
+            parts.append(weigh(b, 1, t0, t1))
+            waiting = (b, t0, t1, parts)
+        add_on_vector(*waiting)

@@ -21,24 +21,24 @@ FP4X4 = mybir.dt.float4_e2m1fn_x4
 ACT = mybir.ActivationFunctionType
 ALU = mybir.AluOpType
 
-PAIR = 2
 GROUP = 4
 SORTS = 4
 
-CAST_FIRST = 128
-CAST_BESIDE_GATHERS = 256
-CAST_ALONE = 384
+CAST_FIRST = (0, 128)
+CAST_BESIDE_GATHERS = 192
+CAST_ALONE = 320
 
-W2_SCALES_AFTER = 8
-ADDED_ON_TENSOR = 2
 HALF = T // 2
+WEIGHED_WHOLE = 2
 LAST_SPLIT = 640
 
 BANK = 2048
 PRE_BANKS, TURNED_BANKS, Y_BANKS = (0, 1, 2), (3, 4), (5, 6, 7)
 
 REGION = PACK * H * 4
-RELU_AT, HIDDEN_AT, GATHERED_AT, H_WORDS_AT, H_SCALES_AT = 0, 2048, 3072, 5120, 5632
+RELU_AT, H_WORDS_AT, H_SCALES_AT, LAST_WORDS_AT = 0, 5120, 5632, 6144
+W1_REGION = 3072
+HIDDEN_AT, W1_AT, GATHERED_AT = 0, 512, 1024
 
 
 def load_scale_rows(nc, scale_tile, rows):
@@ -64,7 +64,7 @@ def tile_moe_duo_relu2_kernel(
         x_s = keep.tile([P, 1, T], U8, name="x_s", align_bytes=64)
         w1_s = [keep.tile([P, GROUP, H], U8, name="w1_s%d" % g, align_bytes=64) for g in range(E // GROUP)]
         w2_s = [keep.tile([P, E, N // 2], U8, name="w2_s%d" % side, align_bytes=64) for side in range(2)]
-        w1_w = [keep.tile([P, PAIR, 2 * H], U8, name="w1_w%d" % pair, align_bytes=64) for pair in range(E // PAIR)]
+        w1_w = [stage.tile([P, 1, 2 * H], U8, name="w1_w%d" % e, align_bytes=64, offset=E * REGION + e * W1_REGION + W1_AT) for e in range(E)]
         w2_w = [
             [keep.tile([P, GROUP, N], U8, name="w2_w%d_%d" % (side, g), align_bytes=64) for g in range(E // GROUP)]
             for side in range(2)
@@ -86,6 +86,11 @@ def tile_moe_duo_relu2_kernel(
                 return stage.tile(shape, dtype, name=name, align_bytes=64, offset=step * REGION + at)
             return keep.tile(shape, dtype, name=name, align_bytes=64)
 
+        def behind_w1(name, shape, dtype, e, at):
+            if 0 <= e < E:
+                return stage.tile(shape, dtype, name=name, align_bytes=64, offset=E * REGION + e * W1_REGION + at)
+            return keep.tile(shape, dtype, name=name, align_bytes=64)
+
         def in_bank(name, shape, bank):
             return psum.tile(shape, F32, name=name, offset=bank * BANK)
 
@@ -101,14 +106,14 @@ def tile_moe_duo_relu2_kernel(
             if e == 0 or ((e + 2) % GROUP == 0 and e + 2 < E):
                 g = (e + 2) // GROUP
                 load_scale_rows(nc, w1_s[g][:], w1_scales[g * GROUP : (g + 1) * GROUP, 0])
-            if e % PAIR == 0:
-                load_packed(w1_w[e // PAIR], w1_words[e : e + PAIR, 0])
-            if e == W2_SCALES_AFTER:
-                load_scale_rows(nc, w2_s[0][:], w2_scales[:, 0, :, 0 : N // 2])
-        nc.sync.dma_start(slot_lists[0][:], pos1)
-        nc.sync.dma_start(slot_lists[1][:], pos2)
+            if e > 0:
+                load_packed(w1_w[e - 1], w1_words[e - 1 : e, 0])
+        load_packed(w1_w[E - 1], w1_words[E - 1 : E, 0])
+        load_scale_rows(nc, w2_s[0][:], w2_scales[:, 0, :, 0 : N // 2])
         for g in range(E // GROUP):
             load_packed(w2_w[0][g], w2_words[g * GROUP : (g + 1) * GROUP, 0, :, 0:N])
+        nc.sync.dma_start(slot_lists[0][:], pos1)
+        nc.sync.dma_start(slot_lists[1][:], pos2)
         for r in range(2):
             nc.sync.dma_start(out=gates[r][:], in_=gate[r])
         load_scale_rows(nc, w2_s[1][:], w2_scales[:, 0, :, N // 2 : N])
@@ -122,24 +127,28 @@ def tile_moe_duo_relu2_kernel(
             columns = GROUP * C // PER_COLUMN
             entries = (partner_list if is_partner else token_list)[:, g * columns : (g + 1) * columns]
             window = x_s[:, 0, :] if is_scale else x_w[:].bitcast(U32)
-            picked = staged("gathered%d_%d" % (g, sort), [P, GROUP * C], U8 if is_scale else U32, step, GATHERED_AT)
+            picked = behind_w1("gathered%d_%d" % (g, sort), [P, GROUP * C], U8 if is_scale else U32, step - 1, GATHERED_AT)
             nc.vector.tensor_copy(picked[:], window.indirect(entries))
             gathered[(g, sort)] = picked
 
         def has_gather(step):
-            return step + GROUP < E
+            return 1 <= step <= E - GROUP
 
         def cast(e):
             wp_bf[e] = ring.tile([P, H, PACK], BF16, name="wp_bf", align_bytes=64)
-            split = CAST_FIRST if e == 0 else CAST_BESIDE_GATHERS if has_gather(e) else CAST_ALONE
-            for engine_copy, c0, c1 in ((nc.scalar.copy, split, H), (nc.vector.tensor_copy, 0, split)):
+            split = CAST_FIRST[e] if e < len(CAST_FIRST) else CAST_BESIDE_GATHERS if has_gather(e) else CAST_ALONE
+            shares = [(nc.scalar.copy, split, H), (nc.vector.tensor_copy, 0, split)]
+            for engine_copy, c0, c1 in shares[: 2 if split else 1]:
                 engine_copy(
                     wp_bf[e][:, c0:c1, :].rearrange("p (c w) d -> p c d w", w=4),
                     wp_raw[e][:, :, c0:c1].rearrange("p d (c w) -> p c d w", w=4),
                 )
 
         def quantize_wp(e):
-            wp_w = ring.tile([P, H], U32, name="wp_w", align_bytes=64)
+            if e + 1 < E:
+                wp_w = ring.tile([P, H], U32, name="wp_w", align_bytes=64)
+            else:
+                wp_w = staged("wp_w_last", [P, H], U32, e - 1, LAST_WORDS_AT)
             wp_s = ring.tile([P, H], U8, name="wp_s", align_bytes=64)
             nc.vector.quantize_mx(out=wp_w[:].bitcast(FP8X4), scales=wp_s[:], in_=wp_bf[e][:].rearrange("p c d -> p (c d)"))
             wp_q[e] = (wp_w, wp_s)
@@ -148,61 +157,65 @@ def tile_moe_duo_relu2_kernel(
             pre[e] = in_bank("pre%d" % e, [P, H], PRE_BANKS[e % len(PRE_BANKS)])
             slots = slice(e % GROUP * C, (e % GROUP + 1) * C)
             token_w, token_s, partner_w, partner_s = [gathered[(e // GROUP, sort)][:, slots] for sort in range(SORTS)]
-            nc.tensor.matmul_mx(
-                out=pre[e][:],
-                lhsT=token_w.bitcast(FP8X4),
-                lhsT_scale=token_s,
-                rhs=w1_w[e // PAIR][:, e % PAIR, :].bitcast(FP4X4),
-                rhs_scale=w1_s[e // GROUP][:, e % GROUP, :],
-                start=True,
-                stop=False,
-            )
-            nc.tensor.matmul_mx(
-                out=pre[e][:],
-                lhsT=partner_w.bitcast(FP8X4),
-                lhsT_scale=partner_s,
-                rhs=wp_q[e][0][:].bitcast(FP8X4),
-                rhs_scale=wp_q[e][1][:],
-                start=False,
-                stop=True,
-            )
+            passes = [
+                (token_w, token_s, w1_w[e][:, 0, :].bitcast(FP4X4), w1_s[e // GROUP][:, e % GROUP, :]),
+                (partner_w, partner_s, wp_q[e][0][:].bitcast(FP8X4), wp_q[e][1][:]),
+            ]
+            if not has_gather(e + 1) and e + 1 < E:
+                passes = [passes[1], passes[0]]
+            for place, (slot_w, slot_s, weight_w, weight_s) in enumerate(passes):
+                nc.tensor.matmul_mx(
+                    out=pre[e][:],
+                    lhsT=slot_w.bitcast(FP8X4),
+                    lhsT_scale=slot_s,
+                    rhs=weight_w,
+                    rhs_scale=weight_s,
+                    start=(place == 0),
+                    stop=(place == 1),
+                )
 
         def relu_and_turn(e):
-            relu = staged("relu%d" % e, [P, PACK, P], F32, e + 1, RELU_AT)
+            relu = staged("relu%d" % e, [P, PACK, P], F32, e, RELU_AT)
             nc.scalar.activation(relu[:], pre[e][:].rearrange("u (p d) -> u d p", d=PACK), ACT.Relu)
             turned[e] = in_bank("turned%d" % e, [P, PACK, C], TURNED_BANKS[e % len(TURNED_BANKS)])
             for d in range(PACK):
                 nc.tensor.transpose(turned[e][:, d, :], relu[:, d, :], ident[:])
 
         def square(e):
-            h_bf[e] = staged("h_bf%d" % e, [P, C, PACK], BF16, e + 2, HIDDEN_AT)
+            if e + 2 == E:
+                h_bf[e] = staged("h_bf%d" % e, [P, C, PACK], BF16, e, LAST_WORDS_AT)
+            else:
+                h_bf[e] = behind_w1("h_bf%d" % e, [P, C, PACK], BF16, e + 1, HIDDEN_AT)
             nc.scalar.activation(h_bf[e][:], turned[e][:].rearrange("p d u -> p u d"), ACT.Square)
 
         def quantize_h(e):
-            h_w = staged("h_w%d" % e, [P, C], U32, e + 3, H_WORDS_AT)
-            h_s = staged("h_s%d" % e, [P, C], U8, e + 3, H_SCALES_AT)
+            h_w = staged("h_w%d" % e, [P, C], U32, e, H_WORDS_AT)
+            h_s = staged("h_s%d" % e, [P, C], U8, e, H_SCALES_AT)
             nc.vector.quantize_mx(out=h_w[:].bitcast(FP8X4), scales=h_s[:], in_=h_bf[e][:].rearrange("p u d -> p (u d)"))
             h_q[e] = (h_w, h_s)
 
         for sort in range(SORTS):
-            gather(0, sort, -1)
-        for step in range(E + 3):
+            gather(0, sort, 0)
+        for step in range(E + 2):
             if step < E:
                 cast(step)
-            if step >= 3:
-                quantize_h(step - 3)
+            if 0 <= step - 1 < E:
+                first_layer(step - 1)
+            if has_gather(step):
+                gather((step - 1) // GROUP + 1, (step - 1) % GROUP, step)
             if step < E:
                 quantize_wp(step)
-                first_layer(step)
-            if has_gather(step):
-                gather(step // GROUP + 1, step % GROUP, step)
+            if 0 <= step - 2 < E and step != E:
+                square(step - 2)
             if 0 <= step - 1 < E:
                 relu_and_turn(step - 1)
-            if 0 <= step - 2 < E:
+            if step == E:
                 square(step - 2)
+            if 0 <= step - 2 < E:
+                quantize_h(step - 2)
 
-        def second_layer(turn, b, experts, engine_copy):
-            bank_tile = in_bank("y_bank%d" % turn, [P, len(experts) * C], Y_BANKS[turn % len(Y_BANKS)])
+        def second_layer(turn, bank, b, experts, engine_copy):
+            bank_tile = in_bank("y_bank%d" % turn, [P, len(experts) * C], bank)
             side, within = divmod(b, 2)
             for place, e in enumerate(experts):
                 nc.tensor.matmul_mx(
@@ -217,22 +230,29 @@ def tile_moe_duo_relu2_kernel(
             engine_copy(y[b][:, experts[0] * C : (experts[-1] + 1) * C], bank_tile[:])
 
         products = [
-            (0, range(0, GROUP), nc.vector.tensor_copy),
-            (0, range(GROUP, 2 * GROUP), nc.scalar.copy),
-            (0, range(2 * GROUP, E - 1), nc.vector.tensor_copy),
-            (0, range(E - 1, E), nc.scalar.copy),
+            (Y_BANKS[0], 0, range(0, GROUP), nc.scalar.copy),
+            (Y_BANKS[1], 0, range(GROUP, 2 * GROUP), nc.vector.tensor_copy),
+            (Y_BANKS[2], 0, range(2 * GROUP, E - 1), nc.scalar.copy),
+            (PRE_BANKS[0], 0, range(E - 1, E), nc.vector.tensor_copy),
         ]
-        products.extend((b, range(e0, e0 + GROUP), nc.scalar.copy) for b in range(1, N // P) for e0 in range(0, E, GROUP))
+        products.extend(
+            (Y_BANKS[g], b, range(g * GROUP, (g + 1) * GROUP), nc.scalar.copy) for b in range(1, N // P) for g in range(E // GROUP)
+        )
         for turn, product in enumerate(products):
             second_layer(turn, *product)
 
         used = [0] * E
 
-        def spare(name, width):
-            region = min(e for e in range(E) if used[e] + 4 * width <= H_WORDS_AT)
-            at = region * REGION + used[region]
-            used[region] = used[region] + 4 * width
-            return stage.tile([P, width], F32, name=name, align_bytes=64, offset=at)
+        places = {}
+
+        def spare(name, width, on=None, at=0):
+            if on is None:
+                region = min(e for e in range(E) if used[e] + 4 * width <= H_WORDS_AT)
+                places[name] = region * REGION + used[region]
+                used[region] = used[region] + 4 * width
+            else:
+                places[name] = places[on] + 4 * at
+            return stage.tile([P, width], F32, name=name, align_bytes=64, offset=places[name])
 
         def weigh(b, r, t0, t1):
             part = spare("part%d_%d_%d" % (b, r, t0), t1 - t0)
@@ -240,42 +260,46 @@ def tile_moe_duo_relu2_kernel(
             nc.vector.tensor_tensor(part[:], y[b][:].indirect(entries), gates[r][:, t0:t1], ALU.mult)
             return part
 
-        def add_on_tensor(b, parts):
-            for t0 in range(0, T, HALF):
-                sum_bank = in_bank("sum%d_%d" % (b, t0), [P, HALF], Y_BANKS[(len(products) - 2 + t0 // HALF) % len(Y_BANKS)])
-                for col in range(0, HALF, P):
-                    for r in range(2):
-                        nc.tensor.matmul(
-                            sum_bank[:, col : col + P],
-                            parts[r][:, t0 + col : t0 + col + P],
-                            ident[:],
-                            start=(r == 0),
-                            stop=(r == 1),
-                            is_transpose=True,
-                        )
-                by_token = spare("by_token%d_%d" % (b, t0), HALF)
-                nc.scalar.copy(by_token[:], sum_bank[:])
-                back_bank = in_bank("back%d_%d" % (b, t0), [P, HALF], TURNED_BANKS[t0 // HALF])
-                for col in range(0, HALF, P):
-                    nc.tensor.transpose(back_bank[:, col : col + P], by_token[:, col : col + P], ident[:])
-                total = spare("total%d_%d" % (b, t0), HALF)
-                nc.scalar.copy(total[:], back_bank[:])
-                nc.scalar.dma_start(out=out[b * P : (b + 1) * P, t0 : t0 + HALF], in_=total[:])
+        def add_on_tensor(turn, b, t0, parts, at):
+            sum_bank = in_bank("sum%d" % turn, [P, HALF], Y_BANKS[1 + turn % 2])
+            for col in range(0, HALF, P):
+                for r in range(2):
+                    nc.tensor.matmul(
+                        sum_bank[:, col : col + P],
+                        parts[r][:, at + col : at + col + P],
+                        ident[:],
+                        start=(r == 0),
+                        stop=(r == 1),
+                        is_transpose=True,
+                    )
+            by_token = spare("by_token%d" % turn, HALF)
+            nc.scalar.copy(by_token[:], sum_bank[:])
+            back_bank = in_bank("back%d" % turn, [P, HALF], TURNED_BANKS[turn % 2])
+            for col in range(0, HALF, P):
+                nc.tensor.transpose(back_bank[:, col : col + P], by_token[:, col : col + P], ident[:])
+            total = spare("total%d" % turn, HALF)
+            nc.scalar.copy(total[:], back_bank[:])
+            nc.sync.dma_start(out=out[b * P : (b + 1) * P, t0 : t0 + HALF], in_=total[:])
 
-        def add_on_vector(b, t0, t1, parts):
-            total = spare("total%d_%d" % (b, t0), t1 - t0)
+        def add_on_vector(b, t0, t1, parts, on, at):
+            total = spare("total%d_%d" % (b, t0), t1 - t0, on, at)
             nc.vector.tensor_tensor(total[:], parts[0][:], parts[1][:], ALU.add)
             nc.sync.dma_start(out=out[b * P : (b + 1) * P, t0:t1], in_=total[:])
 
-        for b in range(ADDED_ON_TENSOR):
-            add_on_tensor(b, [weigh(b, r, 0, T) for r in range(2)])
         last = N // P - 1
-        pieces = [(b, 0, T) for b in range(ADDED_ON_TENSOR, last)] + [(last, 0, LAST_SPLIT), (last, LAST_SPLIT, T)]
+        for b in range(WEIGHED_WHOLE):
+            parts = [weigh(b, r, 0, T) for r in range(2)]
+            for half in range(2):
+                add_on_tensor(2 * b + half, b, half * HALF, parts, half * HALF)
+        for turn in range(2 * WEIGHED_WHOLE, 2 * last):
+            b, half = divmod(turn, 2)
+            add_on_tensor(turn, b, half * HALF, [weigh(b, r, half * HALF, (half + 1) * HALF) for r in range(2)], 0)
+        pieces = [(0, HALF, "by_token5", 0), (HALF, LAST_SPLIT, "total4", 0), (LAST_SPLIT, T, "total4", LAST_SPLIT - HALF)]
         waiting = None
-        for b, t0, t1 in pieces:
-            parts = [weigh(b, 0, t0, t1)]
+        for t0, t1, on, at in pieces:
+            parts = [weigh(last, 0, t0, t1)]
             if waiting:
                 add_on_vector(*waiting)
-            parts.append(weigh(b, 1, t0, t1))
-            waiting = (b, t0, t1, parts)
+            parts.append(weigh(last, 1, t0, t1))
+            waiting = (last, t0, t1, parts, on, at)
         add_on_vector(*waiting)

@@ -30,6 +30,7 @@ CAST_ALONE = 320
 
 HALF = T // 2
 WEIGHED_WHOLE = 2
+ADDED_ON_TENSOR = 5
 LAST_SPLIT = 640
 
 BANK = 2048
@@ -243,16 +244,11 @@ def tile_moe_duo_relu2_kernel(
 
         used = [0] * E
 
-        places = {}
-
-        def spare(name, width, on=None, at=0):
-            if on is None:
-                region = min(e for e in range(E) if used[e] + 4 * width <= H_WORDS_AT)
-                places[name] = region * REGION + used[region]
-                used[region] = used[region] + 4 * width
-            else:
-                places[name] = places[on] + 4 * at
-            return stage.tile([P, width], F32, name=name, align_bytes=64, offset=places[name])
+        def spare(name, width):
+            region = min(e for e in range(E) if used[e] + 4 * width <= H_WORDS_AT)
+            at = region * REGION + used[region]
+            used[region] = used[region] + 4 * width
+            return stage.tile([P, width], F32, name=name, align_bytes=64, offset=at)
 
         def weigh(b, r, t0, t1):
             part = spare("part%d_%d_%d" % (b, r, t0), t1 - t0)
@@ -279,10 +275,10 @@ def tile_moe_duo_relu2_kernel(
                 nc.tensor.transpose(back_bank[:, col : col + P], by_token[:, col : col + P], ident[:])
             total = spare("total%d" % turn, HALF)
             nc.scalar.copy(total[:], back_bank[:])
-            nc.sync.dma_start(out=out[b * P : (b + 1) * P, t0 : t0 + HALF], in_=total[:])
+            nc.scalar.dma_start(out=out[b * P : (b + 1) * P, t0 : t0 + HALF], in_=total[:])
 
-        def add_on_vector(b, t0, t1, parts, on, at):
-            total = spare("total%d_%d" % (b, t0), t1 - t0, on, at)
+        def add_on_vector(b, t0, t1, parts):
+            total = spare("total%d_%d" % (b, t0), t1 - t0)
             nc.vector.tensor_tensor(total[:], parts[0][:], parts[1][:], ALU.add)
             nc.sync.dma_start(out=out[b * P : (b + 1) * P, t0:t1], in_=total[:])
 
@@ -291,15 +287,15 @@ def tile_moe_duo_relu2_kernel(
             parts = [weigh(b, r, 0, T) for r in range(2)]
             for half in range(2):
                 add_on_tensor(2 * b + half, b, half * HALF, parts, half * HALF)
-        for turn in range(2 * WEIGHED_WHOLE, 2 * last):
+        for turn in range(2 * WEIGHED_WHOLE, ADDED_ON_TENSOR):
             b, half = divmod(turn, 2)
             add_on_tensor(turn, b, half * HALF, [weigh(b, r, half * HALF, (half + 1) * HALF) for r in range(2)], 0)
-        pieces = [(0, HALF, "by_token5", 0), (HALF, LAST_SPLIT, "total4", 0), (LAST_SPLIT, T, "total4", LAST_SPLIT - HALF)]
+        pieces = [(last - 1, HALF, T), (last, 0, HALF), (last, HALF, LAST_SPLIT), (last, LAST_SPLIT, T)]
         waiting = None
-        for t0, t1, on, at in pieces:
-            parts = [weigh(last, 0, t0, t1)]
+        for b, t0, t1 in pieces:
+            parts = [weigh(b, 0, t0, t1)]
             if waiting:
                 add_on_vector(*waiting)
-            parts.append(weigh(last, 1, t0, t1))
-            waiting = (last, t0, t1, parts, on, at)
+            parts.append(weigh(b, 1, t0, t1))
+            waiting = (b, t0, t1, parts)
         add_on_vector(*waiting)

@@ -26,7 +26,7 @@ SORTS = 4
 
 CAST_FIRST = (0, 128)
 CAST_BESIDE_GATHERS = 192
-CAST_ALONE = 320
+CAST_ALONE = 384
 
 HALF = T // 2
 WEIGHED_WHOLE = 2
@@ -145,39 +145,47 @@ def tile_moe_duo_relu2_kernel(
                     wp_raw[e][:, :, c0:c1].rearrange("p d (c w) -> p c d w", w=4),
                 )
 
+        def column_pieces(e):
+            return [(0, H // 2), (H // 2, H)] if e + 1 == E else [(0, H)]
+
         def quantize_wp(e):
             if e + 1 < E:
                 wp_w = ring.tile([P, H], U32, name="wp_w", align_bytes=64)
             else:
                 wp_w = staged("wp_w_last", [P, H], U32, e - 1, LAST_WORDS_AT)
             wp_s = ring.tile([P, H], U8, name="wp_s", align_bytes=64)
-            nc.vector.quantize_mx(out=wp_w[:].bitcast(FP8X4), scales=wp_s[:], in_=wp_bf[e][:].rearrange("p c d -> p (c d)"))
+            for c0, c1 in column_pieces(e):
+                nc.vector.quantize_mx(
+                    out=wp_w[:, c0:c1].bitcast(FP8X4), scales=wp_s[:, c0:c1], in_=wp_bf[e][:, c0:c1, :].rearrange("p c d -> p (c d)")
+                )
             wp_q[e] = (wp_w, wp_s)
 
         def first_layer(e):
             pre[e] = in_bank("pre%d" % e, [P, H], PRE_BANKS[e % len(PRE_BANKS)])
             slots = slice(e % GROUP * C, (e % GROUP + 1) * C)
             token_w, token_s, partner_w, partner_s = [gathered[(e // GROUP, sort)][:, slots] for sort in range(SORTS)]
-            passes = [
-                (token_w, token_s, w1_w[e][:, 0, :].bitcast(FP4X4), w1_s[e // GROUP][:, e % GROUP, :]),
-                (partner_w, partner_s, wp_q[e][0][:].bitcast(FP8X4), wp_q[e][1][:]),
-            ]
+            passes = [(0, H, token_w, token_s, w1_w[e][:, 0, :].bitcast(FP4X4), w1_s[e // GROUP][:, e % GROUP, :])]
+            passes.extend(
+                (c0, c1, partner_w, partner_s, wp_q[e][0][:, c0:c1].bitcast(FP8X4), wp_q[e][1][:, c0:c1]) for c0, c1 in column_pieces(e)
+            )
             if not has_gather(e + 1) and e + 1 < E:
                 passes = [passes[1], passes[0]]
-            for place, (slot_w, slot_s, weight_w, weight_s) in enumerate(passes):
+            for place, (c0, c1, slot_w, slot_s, weight_w, weight_s) in enumerate(passes):
                 nc.tensor.matmul_mx(
-                    out=pre[e][:],
+                    out=pre[e][:, c0:c1],
                     lhsT=slot_w.bitcast(FP8X4),
                     lhsT_scale=slot_s,
                     rhs=weight_w,
                     rhs_scale=weight_s,
                     start=(place == 0),
-                    stop=(place == 1),
+                    stop=(place + 1 == len(passes)),
                 )
 
         def relu_and_turn(e):
             relu = staged("relu%d" % e, [P, PACK, P], F32, e, RELU_AT)
-            nc.scalar.activation(relu[:], pre[e][:].rearrange("u (p d) -> u d p", d=PACK), ACT.Relu)
+            for c0, c1 in column_pieces(e):
+                planes = slice(c0 // P, c1 // P)
+                nc.scalar.activation(relu[:, planes, :], pre[e][:].rearrange("u (p d) -> u d p", d=PACK)[:, planes, :], ACT.Relu)
             turned[e] = in_bank("turned%d" % e, [P, PACK, C], TURNED_BANKS[e % len(TURNED_BANKS)])
             for d in range(PACK):
                 nc.tensor.transpose(turned[e][:, d, :], relu[:, d, :], ident[:])
@@ -206,11 +214,9 @@ def tile_moe_duo_relu2_kernel(
                 gather((step - 1) // GROUP + 1, (step - 1) % GROUP, step)
             if step < E:
                 quantize_wp(step)
-            if 0 <= step - 2 < E and step != E:
-                square(step - 2)
             if 0 <= step - 1 < E:
                 relu_and_turn(step - 1)
-            if step == E:
+            if 0 <= step - 2 < E:
                 square(step - 2)
             if 0 <= step - 2 < E:
                 quantize_h(step - 2)

@@ -27,6 +27,7 @@ SORTS = 4
 CAST_FIRST = (0, 128)
 CAST_BESIDE_GATHERS = 192
 CAST_ALONE = 384
+CAST_LAST = 320
 
 HALF = T // 2
 WEIGHED_WHOLE = 2
@@ -137,16 +138,16 @@ def tile_moe_duo_relu2_kernel(
 
         def cast(e):
             wp_bf[e] = ring.tile([P, H, PACK], BF16, name="wp_bf", align_bytes=64)
-            split = CAST_FIRST[e] if e < len(CAST_FIRST) else CAST_BESIDE_GATHERS if has_gather(e) else CAST_ALONE
-            shares = [(nc.scalar.copy, split, H), (nc.vector.tensor_copy, 0, split)]
-            for engine_copy, c0, c1 in shares[: 2 if split else 1]:
+            split = CAST_FIRST[e] if e < len(CAST_FIRST) else CAST_BESIDE_GATHERS if has_gather(e) else CAST_LAST if e + 1 == E else CAST_ALONE
+            shares = [(nc.scalar.copy, split, H), (nc.vector.tensor_copy, 0, min(split, H // 2)), (nc.vector.tensor_copy, H // 2, split)]
+            for engine_copy, c0, c1 in [share for share in shares if share[1] < share[2]]:
                 engine_copy(
-                    wp_bf[e][:, c0:c1, :].rearrange("p (c w) d -> p c d w", w=4),
-                    wp_raw[e][:, :, c0:c1].rearrange("p d (c w) -> p c d w", w=4),
+                    wp_bf[e][:, c0:c1, :].rearrange("p (c w) d -> p c d w", w=2),
+                    wp_raw[e][:, :, c0:c1].rearrange("p d (c w) -> p c d w", w=2),
                 )
 
         def column_pieces(e):
-            return [(0, H // 2), (H // 2, H)] if e + 1 == E else [(0, H)]
+            return [(0, H)] if e == 0 or has_gather(e) else [(0, H // 2), (H // 2, H)]
 
         def quantize_wp(e):
             if e + 1 < E:
@@ -166,7 +167,8 @@ def tile_moe_duo_relu2_kernel(
             token_w, token_s, partner_w, partner_s = [gathered[(e // GROUP, sort)][:, slots] for sort in range(SORTS)]
             passes = [(0, H, token_w, token_s, w1_w[e][:, 0, :].bitcast(FP4X4), w1_s[e // GROUP][:, e % GROUP, :])]
             passes.extend(
-                (c0, c1, partner_w, partner_s, wp_q[e][0][:, c0:c1].bitcast(FP8X4), wp_q[e][1][:, c0:c1]) for c0, c1 in column_pieces(e)
+                (c0, c1, partner_w, partner_s, wp_q[e][0][:, c0:c1].bitcast(FP8X4), wp_q[e][1][:, c0:c1])
+                for c0, c1 in (column_pieces(e) if e + 1 == E else [(0, H)])
             )
             if not has_gather(e + 1) and e + 1 < E:
                 passes = [passes[1], passes[0]]
@@ -183,7 +185,7 @@ def tile_moe_duo_relu2_kernel(
 
         def relu_and_turn(e):
             relu = staged("relu%d" % e, [P, PACK, P], F32, e, RELU_AT)
-            for c0, c1 in column_pieces(e):
+            for c0, c1 in column_pieces(e) if e + 1 == E else [(0, H)]:
                 planes = slice(c0 // P, c1 // P)
                 nc.scalar.activation(relu[:, planes, :], pre[e][:].rearrange("u (p d) -> u d p", d=PACK)[:, planes, :], ACT.Relu)
             turned[e] = in_bank("turned%d" % e, [P, PACK, C], TURNED_BANKS[e % len(TURNED_BANKS)])

@@ -30,9 +30,9 @@ CAST_ALONE = 384
 CAST_LAST = 320
 
 HALF = T // 2
-WEIGHED_WHOLE = 2
-ADDED_ON_TENSOR = 5
-LAST_SPLIT = 640
+LAST_PIECES = ((0, HALF), (HALF, 640), (640, T))
+
+W2_PARTS = ((0, P), (P, 2 * P), (2 * P, N))
 
 BANK = 2048
 PRE_BANKS, TURNED_BANKS, Y_BANKS = (0, 1, 2), (3, 4), (5, 6, 7)
@@ -57,6 +57,7 @@ def tile_moe_duo_relu2_kernel(
         keep = ctx.enter_context(tc.tile_pool(name="keep", bufs=1))
         ring = ctx.enter_context(tc.tile_pool(name="ring", bufs=3))
         stage = ctx.enter_context(tc.tile_pool(name="stage", bufs=1))
+        rounded = ctx.enter_context(tc.tile_pool(name="rounded", bufs=1))
         psum = ctx.enter_context(tc.psum_pool(name="psum", bufs=1))
 
         token_list = keep.tile([P, S // PER_COLUMN], U16, name="token_list")
@@ -65,11 +66,11 @@ def tile_moe_duo_relu2_kernel(
         x_w = keep.tile([P, T], I32, name="x_w", align_bytes=64)
         x_s = keep.tile([P, 1, T], U8, name="x_s", align_bytes=64)
         w1_s = [keep.tile([P, GROUP, H], U8, name="w1_s%d" % g, align_bytes=64) for g in range(E // GROUP)]
-        w2_s = [keep.tile([P, E, N // 2], U8, name="w2_s%d" % side, align_bytes=64) for side in range(2)]
+        w2_s = [keep.tile([P, E, c1 - c0], U8, name="w2_s%d" % c0, align_bytes=64) for c0, c1 in W2_PARTS]
         w1_w = [stage.tile([P, 1, 2 * H], U8, name="w1_w%d" % e, align_bytes=64, offset=E * REGION + e * W1_REGION + W1_AT) for e in range(E)]
         w2_w = [
-            [keep.tile([P, GROUP, N], U8, name="w2_w%d_%d" % (side, g), align_bytes=64) for g in range(E // GROUP)]
-            for side in range(2)
+            [keep.tile([P, GROUP, 2 * (c1 - c0)], U8, name="w2_w%d_%d" % (c0, g), align_bytes=64) for g in range(E // GROUP)]
+            for c0, c1 in W2_PARTS
         ]
         wp_raw = [stage.tile([P, PACK, H], F32, name="wp_raw%d" % e, align_bytes=64, offset=e * REGION) for e in range(E)]
         gates = [keep.tile([P, T], F32, name="gate%d" % r) for r in range(2)]
@@ -99,6 +100,12 @@ def tile_moe_duo_relu2_kernel(
         def load_packed(word_tile, hbm_words):
             nc.sync.dma_start(out=word_tile[:].bitcast(I32), in_=hbm_words.bitcast(I32).rearrange("e p w -> p e w"))
 
+        def load_w2(part):
+            c0, c1 = W2_PARTS[part]
+            load_scale_rows(nc, w2_s[part][:], w2_scales[:, 0, :, c0:c1])
+            for g in range(E // GROUP):
+                load_packed(w2_w[part][g], w2_words[g * GROUP : (g + 1) * GROUP, 0, :, 2 * c0 : 2 * c1])
+
         nc.sync.dma_start(token_list[:], offs)
         nc.sync.dma_start(out=x_w[:], in_=x_words[0].rearrange("p t d -> p (t d)").bitcast(I32))
         load_scale_rows(nc, x_s[:], x_scales)
@@ -111,16 +118,13 @@ def tile_moe_duo_relu2_kernel(
             if e > 0:
                 load_packed(w1_w[e - 1], w1_words[e - 1 : e, 0])
         load_packed(w1_w[E - 1], w1_words[E - 1 : E, 0])
-        load_scale_rows(nc, w2_s[0][:], w2_scales[:, 0, :, 0 : N // 2])
-        for g in range(E // GROUP):
-            load_packed(w2_w[0][g], w2_words[g * GROUP : (g + 1) * GROUP, 0, :, 0:N])
+        load_w2(0)
         nc.sync.dma_start(slot_lists[0][:], pos1)
         nc.sync.dma_start(slot_lists[1][:], pos2)
         for r in range(2):
             nc.sync.dma_start(out=gates[r][:], in_=gate[r])
-        load_scale_rows(nc, w2_s[1][:], w2_scales[:, 0, :, N // 2 : N])
-        for g in range(E // GROUP):
-            load_packed(w2_w[1][g], w2_words[g * GROUP : (g + 1) * GROUP, 0, :, N : 2 * N])
+        load_w2(1)
+        load_w2(2)
 
         gathered, wp_bf, wp_q, pre, turned, h_bf, h_q = {}, {}, {}, {}, {}, {}, {}
 
@@ -137,13 +141,14 @@ def tile_moe_duo_relu2_kernel(
             return 1 <= step <= E - GROUP
 
         def cast(e):
-            wp_bf[e] = ring.tile([P, H, PACK], BF16, name="wp_bf", align_bytes=64)
+            at = min(e, E - 3) % 3 * 2 * H * PACK
+            wp_bf[e] = rounded.tile([P, H, PACK], BF16, name="wp_bf%d" % e, align_bytes=64, offset=at)
             split = CAST_FIRST[e] if e < len(CAST_FIRST) else CAST_BESIDE_GATHERS if has_gather(e) else CAST_LAST if e + 1 == E else CAST_ALONE
             shares = [(nc.scalar.copy, split, H), (nc.vector.tensor_copy, 0, min(split, H // 2)), (nc.vector.tensor_copy, H // 2, split)]
             for engine_copy, c0, c1 in [share for share in shares if share[1] < share[2]]:
                 engine_copy(
-                    wp_bf[e][:, c0:c1, :].rearrange("p (c w) d -> p c d w", w=2),
-                    wp_raw[e][:, :, c0:c1].rearrange("p d (c w) -> p c d w", w=2),
+                    wp_bf[e][:, c0:c1, :].rearrange("p (c w) d -> p c d w", w=4),
+                    wp_raw[e][:, :, c0:c1].rearrange("p d (c w) -> p c d w", w=4),
                 )
 
         def column_pieces(e):
@@ -225,12 +230,13 @@ def tile_moe_duo_relu2_kernel(
 
         def second_layer(turn, bank, b, experts, engine_copy):
             bank_tile = in_bank("y_bank%d" % turn, [P, len(experts) * C], bank)
-            side, within = divmod(b, 2)
+            part = min(b, len(W2_PARTS) - 1)
+            c0 = b * P - W2_PARTS[part][0]
             for place, e in enumerate(experts):
                 nc.tensor.matmul_mx(
                     out=bank_tile[:, place * C : (place + 1) * C],
-                    lhsT=w2_w[side][e // GROUP][:, e % GROUP, 2 * P * within : 2 * P * (within + 1)].bitcast(FP4X4),
-                    lhsT_scale=w2_s[side][:, e, P * within : P * (within + 1)],
+                    lhsT=w2_w[part][e // GROUP][:, e % GROUP, 2 * c0 : 2 * (c0 + P)].bitcast(FP4X4),
+                    lhsT_scale=w2_s[part][:, e, c0 : c0 + P],
                     rhs=h_q[e][0][:].bitcast(FP8X4),
                     rhs_scale=h_q[e][1][:],
                     start=True,
@@ -264,13 +270,13 @@ def tile_moe_duo_relu2_kernel(
             nc.vector.tensor_tensor(part[:], y[b][:].indirect(entries), gates[r][:, t0:t1], ALU.mult)
             return part
 
-        def add_on_tensor(turn, b, t0, parts, at):
+        def add_on_tensor(turn, b, t0, parts):
             sum_bank = in_bank("sum%d" % turn, [P, HALF], Y_BANKS[1 + turn % 2])
             for col in range(0, HALF, P):
                 for r in range(2):
                     nc.tensor.matmul(
                         sum_bank[:, col : col + P],
-                        parts[r][:, at + col : at + col + P],
+                        parts[r][:, t0 + col : t0 + col + P],
                         ident[:],
                         start=(r == 0),
                         stop=(r == 1),
@@ -287,23 +293,21 @@ def tile_moe_duo_relu2_kernel(
 
         def add_on_vector(b, t0, t1, parts):
             total = spare("total%d_%d" % (b, t0), t1 - t0)
-            nc.vector.tensor_tensor(total[:], parts[0][:], parts[1][:], ALU.add)
+            nc.vector.tensor_tensor(total[:], parts[0], parts[1], ALU.add)
             nc.sync.dma_start(out=out[b * P : (b + 1) * P, t0:t1], in_=total[:])
 
         last = N // P - 1
-        for b in range(WEIGHED_WHOLE):
-            parts = [weigh(b, r, 0, T) for r in range(2)]
-            for half in range(2):
-                add_on_tensor(2 * b + half, b, half * HALF, parts, half * HALF)
-        for turn in range(2 * WEIGHED_WHOLE, ADDED_ON_TENSOR):
-            b, half = divmod(turn, 2)
-            add_on_tensor(turn, b, half * HALF, [weigh(b, r, half * HALF, (half + 1) * HALF) for r in range(2)], 0)
-        pieces = [(last - 1, HALF, T), (last, 0, HALF), (last, HALF, LAST_SPLIT), (last, LAST_SPLIT, T)]
         waiting = None
-        for b, t0, t1 in pieces:
-            parts = [weigh(b, 0, t0, t1)]
-            if waiting:
-                add_on_vector(*waiting)
-            parts.append(weigh(b, 1, t0, t1))
-            waiting = (b, t0, t1, parts)
+        for b in range(last):
+            parts = [weigh(b, r, 0, T) for r in range(2)]
+            add_on_tensor(2 * b, b, 0, parts)
+            if b + 1 < last:
+                add_on_tensor(2 * b + 1, b, HALF, parts)
+            else:
+                waiting = (b, HALF, T, [part[:, HALF:T] for part in parts])
+        for t0, t1 in LAST_PIECES:
+            parts = [weigh(last, 0, t0, t1)]
+            add_on_vector(*waiting)
+            parts.append(weigh(last, 1, t0, t1))
+            waiting = (last, t0, t1, [part[:] for part in parts])
         add_on_vector(*waiting)

@@ -34,6 +34,10 @@ LAST_PIECES = ((0, HALF), (HALF, 640), (640, T))
 
 W2_PARTS = ((0, P), (P, 2 * P), (2 * P, N))
 
+GATE_PIECES, GATE_STEP = 2 * T // P, 133
+GATE_STEPS, GATE_AT = (9, 10), 2048
+GATE_LOAD_BEHIND = 4
+
 BANK = 2048
 PRE_BANKS, TURNED_BANKS, Y_BANKS = (0, 1, 2), (3, 4), (5, 6, 7)
 
@@ -73,10 +77,13 @@ def tile_moe_duo_relu2_kernel(
             for c0, c1 in W2_PARTS
         ]
         wp_raw = [stage.tile([P, PACK, H], F32, name="wp_raw%d" % e, align_bytes=64, offset=e * REGION) for e in range(E)]
-        gates = [keep.tile([P, T], F32, name="gate%d" % r) for r in range(2)]
+        gates = [stage.tile([P, T], F32, name="gate%d" % r, align_bytes=64, offset=step * REGION + GATE_AT) for r, step in enumerate(GATE_STEPS)]
         ident = keep.tile([P, P], F32, name="ident")
+        gate_rows = keep.tile([P, P], F32, name="gate_rows")
+        gate_columns = keep.tile([P, GATE_PIECES], F32, name="gate_columns")
         y = [keep.tile([P, S], F32, name="y%d" % b) for b in range(N // P)]
 
+        nc.gpsimd.memset(gate_rows[:], 0.0)
         nc.gpsimd.memset(x_s[:].bitcast(I32), 0)
         for scale_tile in w1_s:
             nc.vector.memset(scale_tile[:].bitcast(I32), 0)
@@ -117,14 +124,28 @@ def tile_moe_duo_relu2_kernel(
                 load_scale_rows(nc, w1_s[g][:], w1_scales[g * GROUP : (g + 1) * GROUP, 0])
             if e > 0:
                 load_packed(w1_w[e - 1], w1_words[e - 1 : e, 0])
+            if e == GATE_LOAD_BEHIND:
+                nc.sync.dma_start(out=gate_rows[0:GATE_PIECES, :], in_=gate.rearrange("r p (c j) -> (r p c) j", j=P)[0 : GATE_PIECES * GATE_STEP - GATE_STEP + 1 : GATE_STEP, :])
         load_packed(w1_w[E - 1], w1_words[E - 1 : E, 0])
         load_w2(0)
         nc.sync.dma_start(slot_lists[0][:], pos1)
         nc.sync.dma_start(slot_lists[1][:], pos2)
-        for r in range(2):
-            nc.sync.dma_start(out=gates[r][:], in_=gate[r])
         load_w2(1)
         load_w2(2)
+
+        piece_bank = in_bank("piece_bank", [P, P], Y_BANKS[2])
+        nc.tensor.transpose(piece_bank[:], gate_rows[:], ident[:])
+        nc.scalar.copy(gate_columns[:], piece_bank[:, 0:GATE_PIECES])
+
+        spread = [in_bank("spread%d" % n, [P, H], bank) for n, bank in enumerate(Y_BANKS)]
+        for q in range(GATE_PIECES):
+            col = q % PACK * P
+            nc.tensor.transpose(spread[q // PACK][:, col : col + P], gate_columns[:, q : q + 1].to_broadcast([P, P]), ident[:])
+
+        def take_gate(r):
+            whole, rest = (slice(0, H), slice(H, T)) if r == 0 else (slice(T - H, T), slice(0, T - H))
+            nc.vector.tensor_copy(gates[r][:, whole], spread[2 * r][:])
+            nc.scalar.copy(gates[r][:, rest], spread[1][:, r * (T - H) : (r + 1) * (T - H)])
 
         gathered, wp_bf, wp_q, pre, turned, h_bf, h_q = {}, {}, {}, {}, {}, {}, {}
 
@@ -227,6 +248,8 @@ def tile_moe_duo_relu2_kernel(
                 square(step - 2)
             if 0 <= step - 2 < E:
                 quantize_h(step - 2)
+            if step in GATE_STEPS:
+                take_gate(GATE_STEPS.index(step))
 
         def second_layer(turn, bank, b, experts, engine_copy):
             bank_tile = in_bank("y_bank%d" % turn, [P, len(experts) * C], bank)
@@ -256,7 +279,7 @@ def tile_moe_duo_relu2_kernel(
         for turn, product in enumerate(products):
             second_layer(turn, *product)
 
-        used = [0] * E
+        used = [H_WORDS_AT if e in GATE_STEPS else 0 for e in range(E)]
 
         def spare(name, width):
             region = min(e for e in range(E) if used[e] + 4 * width <= H_WORDS_AT)

@@ -24,27 +24,23 @@ ALU = mybir.AluOpType
 GROUP = 4
 SORTS = 4
 
-CAST_FIRST = (0, 128)
-CAST_BESIDE_GATHERS = 192
-CAST_ALONE = 384
-CAST_LAST = 320
+CAST_ON_VECTOR = (0, 0, 0, 0, 0, 512, 512, 512, 336, 336, 336, 320)
+W1_LOADS = ((0, 4, 3), (4, 8, 5), (8, 10, 8), (10, 11, 11), (11, 12, 11))
+BF_BUFFERS = 6
 
 HALF = T // 2
 LAST_PIECES = ((0, HALF), (HALF, 640), (640, T))
 
 W2_PARTS = ((0, P), (P, 2 * P), (2 * P, N))
 
-GATE_PIECES, GATE_STEP = 2 * T // P, 133
-GATE_STEPS, GATE_AT = (9, 10), 2048
-GATE_LOAD_BEHIND = 4
-
 BANK = 2048
 PRE_BANKS, TURNED_BANKS, Y_BANKS = (0, 1, 2), (3, 4), (5, 6, 7)
 
 REGION = PACK * H * 4
-RELU_AT, H_WORDS_AT, H_SCALES_AT, LAST_WORDS_AT = 0, 5120, 5632, 6144
-W1_REGION = 3072
-HIDDEN_AT, W1_AT, GATHERED_AT = 0, 512, 1024
+WORDS_AT, SCALES_AT, H_WORDS_AT, RELU_AT = 0, 2048, 4864, 6144
+HIDDEN_AT = 3072
+SHARED_FROM = 8
+H_BYTES = 5 * C
 
 
 def load_scale_rows(nc, scale_tile, rows):
@@ -59,7 +55,6 @@ def tile_moe_duo_relu2_kernel(
     nc = tc.nc
     with ExitStack() as ctx:
         keep = ctx.enter_context(tc.tile_pool(name="keep", bufs=1))
-        ring = ctx.enter_context(tc.tile_pool(name="ring", bufs=3))
         stage = ctx.enter_context(tc.tile_pool(name="stage", bufs=1))
         rounded = ctx.enter_context(tc.tile_pool(name="rounded", bufs=1))
         psum = ctx.enter_context(tc.psum_pool(name="psum", bufs=1))
@@ -69,24 +64,20 @@ def tile_moe_duo_relu2_kernel(
         slot_lists = [keep.tile([P, T // PER_COLUMN], U16, name="slot_list%d" % r) for r in range(2)]
         x_w = keep.tile([P, T], I32, name="x_w", align_bytes=64)
         x_s = keep.tile([P, 1, T], U8, name="x_s", align_bytes=64)
-        w1_s = [keep.tile([P, GROUP, H], U8, name="w1_s%d" % g, align_bytes=64) for g in range(E // GROUP)]
+        w1_s = keep.tile([P, E, H], U8, name="w1_s", align_bytes=64)
         w2_s = [keep.tile([P, E, c1 - c0], U8, name="w2_s%d" % c0, align_bytes=64) for c0, c1 in W2_PARTS]
-        w1_w = [stage.tile([P, 1, 2 * H], U8, name="w1_w%d" % e, align_bytes=64, offset=E * REGION + e * W1_REGION + W1_AT) for e in range(E)]
+        w1_w = [keep.tile([P, e1 - e0, 2 * H], U8, name="w1_w%d" % e0, align_bytes=64) for e0, e1, behind in W1_LOADS]
         w2_w = [
             [keep.tile([P, GROUP, 2 * (c1 - c0)], U8, name="w2_w%d_%d" % (c0, g), align_bytes=64) for g in range(E // GROUP)]
             for c0, c1 in W2_PARTS
         ]
         wp_raw = [stage.tile([P, PACK, H], F32, name="wp_raw%d" % e, align_bytes=64, offset=e * REGION) for e in range(E)]
-        gates = [stage.tile([P, T], F32, name="gate%d" % r, align_bytes=64, offset=step * REGION + GATE_AT) for r, step in enumerate(GATE_STEPS)]
+        gates = [keep.tile([P, T], F32, name="gate%d" % r) for r in range(2)]
         ident = keep.tile([P, P], F32, name="ident")
-        gate_rows = keep.tile([P, P], F32, name="gate_rows")
-        gate_columns = keep.tile([P, GATE_PIECES], F32, name="gate_columns")
         y = [keep.tile([P, S], F32, name="y%d" % b) for b in range(N // P)]
 
-        nc.gpsimd.memset(gate_rows[:], 0.0)
         nc.gpsimd.memset(x_s[:].bitcast(I32), 0)
-        for scale_tile in w1_s:
-            nc.vector.memset(scale_tile[:].bitcast(I32), 0)
+        nc.vector.memset(w1_s[:].bitcast(I32), 0)
         make_identity(nc, ident[:])
         for scale_tile in w2_s:
             nc.gpsimd.memset(scale_tile[:].bitcast(I32), 0)
@@ -94,11 +85,6 @@ def tile_moe_duo_relu2_kernel(
         def staged(name, shape, dtype, step, at):
             if 0 <= step < E:
                 return stage.tile(shape, dtype, name=name, align_bytes=64, offset=step * REGION + at)
-            return keep.tile(shape, dtype, name=name, align_bytes=64)
-
-        def behind_w1(name, shape, dtype, e, at):
-            if 0 <= e < E:
-                return stage.tile(shape, dtype, name=name, align_bytes=64, offset=E * REGION + e * W1_REGION + at)
             return keep.tile(shape, dtype, name=name, align_bytes=64)
 
         def in_bank(name, shape, bank):
@@ -115,56 +101,38 @@ def tile_moe_duo_relu2_kernel(
 
         nc.sync.dma_start(token_list[:], offs)
         nc.sync.dma_start(out=x_w[:], in_=x_words[0].rearrange("p t d -> p (t d)").bitcast(I32))
-        load_scale_rows(nc, x_s[:], x_scales)
         nc.sync.dma_start(partner_list[:], offs2)
+        load_scale_rows(nc, x_s[:], x_scales)
         for e in range(E):
             nc.sync.dma_start(out=wp_raw[e][:], in_=wp[e].rearrange("(p d) c -> p d c", d=PACK))
-            if e == 0 or ((e + 2) % GROUP == 0 and e + 2 < E):
-                g = (e + 2) // GROUP
-                load_scale_rows(nc, w1_s[g][:], w1_scales[g * GROUP : (g + 1) * GROUP, 0])
-            if e > 0:
-                load_packed(w1_w[e - 1], w1_words[e - 1 : e, 0])
-            if e == GATE_LOAD_BEHIND:
-                nc.sync.dma_start(out=gate_rows[0:GATE_PIECES, :], in_=gate.rearrange("r p (c j) -> (r p c) j", j=P)[0 : GATE_PIECES * GATE_STEP - GATE_STEP + 1 : GATE_STEP, :])
-        load_packed(w1_w[E - 1], w1_words[E - 1 : E, 0])
+            if e == W1_LOADS[0][2]:
+                load_scale_rows(nc, w1_s[:], w1_scales[:, 0])
+            for part, (e0, e1, behind) in enumerate(W1_LOADS):
+                if behind == e:
+                    load_packed(w1_w[part], w1_words[e0:e1, 0])
         load_w2(0)
         nc.sync.dma_start(slot_lists[0][:], pos1)
         nc.sync.dma_start(slot_lists[1][:], pos2)
+        for r in range(2):
+            nc.sync.dma_start(out=gates[r][:], in_=gate[r])
         load_w2(1)
         load_w2(2)
 
-        piece_bank = in_bank("piece_bank", [P, P], Y_BANKS[2])
-        nc.tensor.transpose(piece_bank[:], gate_rows[:], ident[:])
-        nc.scalar.copy(gate_columns[:], piece_bank[:, 0:GATE_PIECES])
+        gathered, wp_bf, wp_q, pre, rectified, turned, h_bf, h_q = {}, {}, {}, {}, {}, {}, {}, {}
+        alone = len([columns for columns in CAST_ON_VECTOR if columns == 0])
 
-        spread = [in_bank("spread%d" % n, [P, H], bank) for n, bank in enumerate(Y_BANKS)]
-        for q in range(GATE_PIECES):
-            col = q % PACK * P
-            nc.tensor.transpose(spread[q // PACK][:, col : col + P], gate_columns[:, q : q + 1].to_broadcast([P, P]), ident[:])
-
-        def take_gate(r):
-            whole, rest = (slice(0, H), slice(H, T)) if r == 0 else (slice(T - H, T), slice(0, T - H))
-            nc.vector.tensor_copy(gates[r][:, whole], spread[2 * r][:])
-            nc.scalar.copy(gates[r][:, rest], spread[1][:, r * (T - H) : (r + 1) * (T - H)])
-
-        gathered, wp_bf, wp_q, pre, turned, h_bf, h_q = {}, {}, {}, {}, {}, {}, {}
-
-        def gather(g, sort, step):
-            is_partner, is_scale = divmod(sort, 2)
+        def gather(g, sort):
+            is_scale, is_partner = divmod(sort, 2)
             columns = GROUP * C // PER_COLUMN
             entries = (partner_list if is_partner else token_list)[:, g * columns : (g + 1) * columns]
             window = x_s[:, 0, :] if is_scale else x_w[:].bitcast(U32)
-            picked = behind_w1("gathered%d_%d" % (g, sort), [P, GROUP * C], U8 if is_scale else U32, step - 1, GATHERED_AT)
+            picked = keep.tile([P, GROUP * C], U8 if is_scale else U32, name="gathered%d_%d" % (g, sort), align_bytes=64)
             nc.vector.tensor_copy(picked[:], window.indirect(entries))
             gathered[(g, sort)] = picked
 
-        def has_gather(step):
-            return 1 <= step <= E - GROUP
-
         def cast(e):
-            at = min(e, E - 3) % 3 * 2 * H * PACK
-            wp_bf[e] = rounded.tile([P, H, PACK], BF16, name="wp_bf%d" % e, align_bytes=64, offset=at)
-            split = CAST_FIRST[e] if e < len(CAST_FIRST) else CAST_BESIDE_GATHERS if has_gather(e) else CAST_LAST if e + 1 == E else CAST_ALONE
+            wp_bf[e] = rounded.tile([P, H, PACK], BF16, name="wp_bf%d" % e, align_bytes=64, offset=e % BF_BUFFERS * 2 * H * PACK)
+            split = CAST_ON_VECTOR[e]
             shares = [(nc.scalar.copy, split, H), (nc.vector.tensor_copy, 0, min(split, H // 2)), (nc.vector.tensor_copy, H // 2, split)]
             for engine_copy, c0, c1 in [share for share in shares if share[1] < share[2]]:
                 engine_copy(
@@ -173,31 +141,29 @@ def tile_moe_duo_relu2_kernel(
                 )
 
         def column_pieces(e):
-            return [(0, H)] if e == 0 or has_gather(e) else [(0, H // 2), (H // 2, H)]
+            return [(0, H // 2), (H // 2, H)] if CAST_ON_VECTOR[e] else [(0, H)]
 
-        def quantize_wp(e):
-            if e + 1 < E:
-                wp_w = ring.tile([P, H], U32, name="wp_w", align_bytes=64)
-            else:
-                wp_w = staged("wp_w_last", [P, H], U32, e - 1, LAST_WORDS_AT)
-            wp_s = ring.tile([P, H], U8, name="wp_s", align_bytes=64)
-            for c0, c1 in column_pieces(e):
+        def quantize_wp(e, pieces):
+            if e not in wp_q:
+                wp_q[e] = (staged("wp_w%d" % e, [P, H], U32, e - 2, WORDS_AT), staged("wp_s%d" % e, [P, H], U8, e - 2, SCALES_AT))
+            wp_w, wp_s = wp_q[e]
+            for c0, c1 in pieces:
                 nc.vector.quantize_mx(
                     out=wp_w[:, c0:c1].bitcast(FP8X4), scales=wp_s[:, c0:c1], in_=wp_bf[e][:, c0:c1, :].rearrange("p c d -> p (c d)")
                 )
-            wp_q[e] = (wp_w, wp_s)
 
         def first_layer(e):
             pre[e] = in_bank("pre%d" % e, [P, H], PRE_BANKS[e % len(PRE_BANKS)])
             slots = slice(e % GROUP * C, (e % GROUP + 1) * C)
-            token_w, token_s, partner_w, partner_s = [gathered[(e // GROUP, sort)][:, slots] for sort in range(SORTS)]
-            passes = [(0, H, token_w, token_s, w1_w[e][:, 0, :].bitcast(FP4X4), w1_s[e // GROUP][:, e % GROUP, :])]
+            token_w, partner_w, token_s, partner_s = [gathered[(e // GROUP, sort)][:, slots] for sort in range(SORTS)]
+            part = min(n for n, load in enumerate(W1_LOADS) if e < load[1])
+            passes = [(0, H, token_w, token_s, w1_w[part][:, e - W1_LOADS[part][0], :].bitcast(FP4X4), w1_s[:, e, :])]
             passes.extend(
                 (c0, c1, partner_w, partner_s, wp_q[e][0][:, c0:c1].bitcast(FP8X4), wp_q[e][1][:, c0:c1])
                 for c0, c1 in (column_pieces(e) if e + 1 == E else [(0, H)])
             )
-            if not has_gather(e + 1) and e + 1 < E:
-                passes = [passes[1], passes[0]]
+            if W1_LOADS[part][2] > e:
+                passes.reverse()
             for place, (c0, c1, slot_w, slot_s, weight_w, weight_s) in enumerate(passes):
                 nc.tensor.matmul_mx(
                     out=pre[e][:, c0:c1],
@@ -209,47 +175,69 @@ def tile_moe_duo_relu2_kernel(
                     stop=(place + 1 == len(passes)),
                 )
 
-        def relu_and_turn(e):
-            relu = staged("relu%d" % e, [P, PACK, P], F32, e, RELU_AT)
+        def rectify(e):
+            if e < len(PRE_BANKS):
+                place = (alone - 1, (RELU_AT, WORDS_AT, SCALES_AT)[e])
+            else:
+                place = (e if e + 1 < SHARED_FROM and e + 1 != alone else e - 1 if e < alone else e + 1, RELU_AT)
+            relu = staged("relu%d" % e, [P, PACK, P], F32, *place)
+            rectified[e] = relu
             for c0, c1 in column_pieces(e) if e + 1 == E else [(0, H)]:
                 planes = slice(c0 // P, c1 // P)
                 nc.scalar.activation(relu[:, planes, :], pre[e][:].rearrange("u (p d) -> u d p", d=PACK)[:, planes, :], ACT.Relu)
+
+        def turn(e):
+            relu = rectified[e]
             turned[e] = in_bank("turned%d" % e, [P, PACK, C], TURNED_BANKS[e % len(TURNED_BANKS)])
             for d in range(PACK):
                 nc.tensor.transpose(turned[e][:, d, :], relu[:, d, :], ident[:])
 
         def square(e):
-            if e + 2 == E:
-                h_bf[e] = staged("h_bf%d" % e, [P, C, PACK], BF16, e, LAST_WORDS_AT)
-            else:
-                h_bf[e] = behind_w1("h_bf%d" % e, [P, C, PACK], BF16, e + 1, HIDDEN_AT)
+            h_bf[e] = staged("h_bf%d" % e, [P, C, PACK], BF16, e if e + 2 < SHARED_FROM else e + 2, HIDDEN_AT)
             nc.scalar.activation(h_bf[e][:], turned[e][:].rearrange("p d u -> p u d"), ACT.Square)
 
-        def quantize_h(e):
-            h_w = staged("h_w%d" % e, [P, C], U32, e, H_WORDS_AT)
-            h_s = staged("h_s%d" % e, [P, C], U8, e, H_SCALES_AT)
+        def quantize_h(e, step):
+            h_w = staged("h_w%d" % e, [P, C], U32, step, H_WORDS_AT + e % 2 * H_BYTES)
+            h_s = staged("h_s%d" % e, [P, C], U8, step, H_WORDS_AT + e % 2 * H_BYTES + PACK * C)
             nc.vector.quantize_mx(out=h_w[:].bitcast(FP8X4), scales=h_s[:], in_=h_bf[e][:].rearrange("p u d -> p (u d)"))
             h_q[e] = (h_w, h_s)
 
         for sort in range(SORTS):
-            gather(0, sort, 0)
+            for g in range(E // GROUP):
+                gather(g, sort)
+        h_step = [max(7 + e // 2, e + 2) for e in range(E)]
         for step in range(E + 2):
+            early = column_pieces(step)[: 1 if step + 1 < E else 2] if step < E else []
             if step < E:
                 cast(step)
-            if 0 <= step - 1 < E:
-                first_layer(step - 1)
-            if has_gather(step):
-                gather((step - 1) // GROUP + 1, (step - 1) % GROUP, step)
+                quantize_wp(step, early)
+            for e in [e for e in range(E) if h_step[e] == step and e not in (E - 4, E - 3)]:
+                quantize_h(e, step)
             if step < E:
-                quantize_wp(step)
-            if 0 <= step - 1 < E:
-                relu_and_turn(step - 1)
-            if 0 <= step - 2 < E:
-                square(step - 2)
-            if 0 <= step - 2 < E:
-                quantize_h(step - 2)
-            if step in GATE_STEPS:
-                take_gate(GATE_STEPS.index(step))
+                quantize_wp(step, column_pieces(step)[len(early) :])
+            lag = len(PRE_BANKS) if step < SHARED_FROM else 1
+            if lag <= step < SHARED_FROM:
+                rectify(step - lag)
+            if step < E:
+                first_layer(step)
+            if SHARED_FROM <= step < E:
+                rectify(step - lag)
+            if lag <= step < E:
+                turn(step - lag)
+            if lag < step < E:
+                square(step - lag - 1)
+            if step + 1 == SHARED_FROM:
+                for e in (step - 2, step - 1):
+                    rectify(e)
+                    turn(e)
+                    square(e - 1)
+            if step + 1 == E:
+                quantize_h(step - 3, step)
+                quantize_h(step - 2, step)
+                rectify(step)
+                turn(step)
+                square(step - 1)
+                square(step)
 
         def second_layer(turn, bank, b, experts, engine_copy):
             bank_tile = in_bank("y_bank%d" % turn, [P, len(experts) * C], bank)
@@ -279,7 +267,7 @@ def tile_moe_duo_relu2_kernel(
         for turn, product in enumerate(products):
             second_layer(turn, *product)
 
-        used = [H_WORDS_AT if e in GATE_STEPS else 0 for e in range(E)]
+        used = [0] * E
 
         def spare(name, width):
             region = min(e for e in range(E) if used[e] + 4 * width <= H_WORDS_AT)

@@ -25,7 +25,7 @@ GROUP = 4
 SORTS = 4
 
 CAST_ON_VECTOR = (0, 0, 0, 0, 0, 512, 512, 512, 336, 336, 336, 320)
-W1_LOADS = ((0, 4, 3), (4, 8, 5), (8, 10, 8), (10, 11, 11), (11, 12, 11))
+W1_LOADS = ((0, 4, 4), (4, 8, 5), (8, 10, 8), (10, 11, 11), (11, 12, 11))
 BF_BUFFERS = 6
 
 HALF = T // 2
@@ -99,8 +99,8 @@ def tile_moe_duo_relu2_kernel(
             for g in range(E // GROUP):
                 load_packed(w2_w[part][g], w2_words[g * GROUP : (g + 1) * GROUP, 0, :, 2 * c0 : 2 * c1])
 
-        nc.sync.dma_start(token_list[:], offs)
         nc.sync.dma_start(out=x_w[:], in_=x_words[0].rearrange("p t d -> p (t d)").bitcast(I32))
+        nc.sync.dma_start(token_list[:], offs)
         nc.sync.dma_start(partner_list[:], offs2)
         load_scale_rows(nc, x_s[:], x_scales)
         for e in range(E):
@@ -162,7 +162,7 @@ def tile_moe_duo_relu2_kernel(
                 (c0, c1, partner_w, partner_s, wp_q[e][0][:, c0:c1].bitcast(FP8X4), wp_q[e][1][:, c0:c1])
                 for c0, c1 in (column_pieces(e) if e + 1 == E else [(0, H)])
             )
-            if W1_LOADS[part][2] > e:
+            if W1_LOADS[part][2] > e and (e == 0 or e >= alone):
                 passes.reverse()
             for place, (c0, c1, slot_w, slot_s, weight_w, weight_s) in enumerate(passes):
                 nc.tensor.matmul_mx(
@@ -281,13 +281,13 @@ def tile_moe_duo_relu2_kernel(
             nc.vector.tensor_tensor(part[:], y[b][:].indirect(entries), gates[r][:, t0:t1], ALU.mult)
             return part
 
-        def add_on_tensor(turn, b, t0, parts):
+        def add_on_tensor(turn, parts, total):
             sum_bank = in_bank("sum%d" % turn, [P, HALF], Y_BANKS[1 + turn % 2])
             for col in range(0, HALF, P):
                 for r in range(2):
                     nc.tensor.matmul(
                         sum_bank[:, col : col + P],
-                        parts[r][:, t0 + col : t0 + col + P],
+                        parts[r][:, col : col + P],
                         ident[:],
                         start=(r == 0),
                         stop=(r == 1),
@@ -298,9 +298,7 @@ def tile_moe_duo_relu2_kernel(
             back_bank = in_bank("back%d" % turn, [P, HALF], TURNED_BANKS[turn % 2])
             for col in range(0, HALF, P):
                 nc.tensor.transpose(back_bank[:, col : col + P], by_token[:, col : col + P], ident[:])
-            total = spare("total%d" % turn, HALF)
-            nc.scalar.copy(total[:], back_bank[:])
-            nc.scalar.dma_start(out=out[b * P : (b + 1) * P, t0 : t0 + HALF], in_=total[:])
+            nc.scalar.copy(total, back_bank[:])
 
         def add_on_vector(b, t0, t1, parts):
             total = spare("total%d_%d" % (b, t0), t1 - t0)
@@ -308,14 +306,18 @@ def tile_moe_duo_relu2_kernel(
             nc.sync.dma_start(out=out[b * P : (b + 1) * P, t0:t1], in_=total[:])
 
         last = N // P - 1
-        waiting = None
-        for b in range(last):
+        for b in range(last - 1):
             parts = [weigh(b, r, 0, T) for r in range(2)]
-            add_on_tensor(2 * b, b, 0, parts)
-            if b + 1 < last:
-                add_on_tensor(2 * b + 1, b, HALF, parts)
-            else:
-                waiting = (b, HALF, T, [part[:, HALF:T] for part in parts])
+            total = spare("total%d" % b, T)
+            for half in range(2):
+                tokens = slice(half * HALF, (half + 1) * HALF)
+                add_on_tensor(2 * b + half, [part[:, tokens] for part in parts], total[:, tokens])
+            nc.scalar.dma_start(out=out[b * P : (b + 1) * P, :], in_=total[:])
+        parts = [weigh(last - 1, r, 0, HALF)[:] for r in range(2)]
+        total = spare("total%d" % (last - 1), HALF)
+        add_on_tensor(2 * (last - 1), parts, total[:])
+        nc.scalar.dma_start(out=out[(last - 1) * P : last * P, 0:HALF], in_=total[:])
+        waiting = (last - 1, HALF, T, [weigh(last - 1, r, HALF, T)[:] for r in range(2)])
         for t0, t1 in LAST_PIECES:
             parts = [weigh(last, 0, t0, t1)]
             add_on_vector(*waiting)

@@ -24,8 +24,8 @@ ALU = mybir.AluOpType
 GROUP = 4
 SORTS = 4
 
-CAST_ON_VECTOR = (0, 0, 0, 0, 0, 512, 512, 512, 336, 336, 336, 320)
-W1_LOADS = ((0, 4, 4), (4, 8, 5), (8, 10, 8), (10, 11, 11), (11, 12, 11))
+CAST_ON_VECTOR = (0, 0, 0, 0, 0, 512, 512, 512, 512, 512, 512, 320)
+W1_LOADS = ((0, 4, 3), (4, 8, 5), (8, 10, 8), (10, 11, 11), (11, 12, 11))
 BF_BUFFERS = 6
 
 HALF = T // 2
@@ -39,8 +39,10 @@ PRE_BANKS, TURNED_BANKS, Y_BANKS = (0, 1, 2), (3, 4), (5, 6, 7)
 REGION = PACK * H * 4
 WORDS_AT, SCALES_AT, H_WORDS_AT, RELU_AT = 0, 2048, 4864, 6144
 HIDDEN_AT = 3072
-SHARED_FROM = 8
-H_BYTES = 5 * C
+GATHERED_AT, UNDER_GATHERED = (0, 2048, 4096, 4608), (1024, 4352)
+LAST_GATHERS_STEP = 3
+CAUGHT_UP = 8
+H_GROUPS = ((0, 2),) + tuple((e, e + 1) for e in range(2, E))
 
 
 def load_scale_rows(nc, scale_tile, rows):
@@ -119,14 +121,15 @@ def tile_moe_duo_relu2_kernel(
         load_w2(2)
 
         gathered, wp_bf, wp_q, pre, rectified, turned, h_bf, h_q = {}, {}, {}, {}, {}, {}, {}, {}
-        alone = len([columns for columns in CAST_ON_VECTOR if columns == 0])
+        alone = CAST_ON_VECTOR.index(H)
 
         def gather(g, sort):
             is_scale, is_partner = divmod(sort, 2)
             columns = GROUP * C // PER_COLUMN
             entries = (partner_list if is_partner else token_list)[:, g * columns : (g + 1) * columns]
             window = x_s[:, 0, :] if is_scale else x_w[:].bitcast(U32)
-            picked = keep.tile([P, GROUP * C], U8 if is_scale else U32, name="gathered%d_%d" % (g, sort), align_bytes=64)
+            region = 0 if g + 1 == E // GROUP else E
+            picked = staged("gathered%d_%d" % (g, sort), [P, GROUP * C], U8 if is_scale else U32, region, GATHERED_AT[sort])
             nc.vector.tensor_copy(picked[:], window.indirect(entries))
             gathered[(g, sort)] = picked
 
@@ -145,7 +148,9 @@ def tile_moe_duo_relu2_kernel(
 
         def quantize_wp(e, pieces):
             if e not in wp_q:
-                wp_q[e] = (staged("wp_w%d" % e, [P, H], U32, e - 2, WORDS_AT), staged("wp_s%d" % e, [P, H], U8, e - 2, SCALES_AT))
+                words_at, scales_at = UNDER_GATHERED if e == 0 else (WORDS_AT, SCALES_AT)
+                region = 0 if e == 0 else E if e == 2 else e - 2
+                wp_q[e] = (staged("wp_w%d" % e, [P, H], U32, region, words_at), staged("wp_s%d" % e, [P, H], U8, region, scales_at))
             wp_w, wp_s = wp_q[e]
             for c0, c1 in pieces:
                 nc.vector.quantize_mx(
@@ -162,7 +167,7 @@ def tile_moe_duo_relu2_kernel(
                 (c0, c1, partner_w, partner_s, wp_q[e][0][:, c0:c1].bitcast(FP8X4), wp_q[e][1][:, c0:c1])
                 for c0, c1 in (column_pieces(e) if e + 1 == E else [(0, H)])
             )
-            if W1_LOADS[part][2] > e and (e == 0 or e >= alone):
+            if W1_LOADS[part][2] > e >= alone:
                 passes.reverse()
             for place, (c0, c1, slot_w, slot_s, weight_w, weight_s) in enumerate(passes):
                 nc.tensor.matmul_mx(
@@ -176,11 +181,8 @@ def tile_moe_duo_relu2_kernel(
                 )
 
         def rectify(e):
-            if e < len(PRE_BANKS):
-                place = (alone - 1, (RELU_AT, WORDS_AT, SCALES_AT)[e])
-            else:
-                place = (e if e + 1 < SHARED_FROM and e + 1 != alone else e - 1 if e < alone else e + 1, RELU_AT)
-            relu = staged("relu%d" % e, [P, PACK, P], F32, *place)
+            region = E if e + 3 == E else e + 1 if e + 1 >= alone else alone - 1 if e == 2 else e
+            relu = staged("relu%d" % e, [P, PACK, P], F32, region, RELU_AT)
             rectified[e] = relu
             for c0, c1 in column_pieces(e) if e + 1 == E else [(0, H)]:
                 planes = slice(c0 // P, c1 // P)
@@ -192,52 +194,63 @@ def tile_moe_duo_relu2_kernel(
             for d in range(PACK):
                 nc.tensor.transpose(turned[e][:, d, :], relu[:, d, :], ident[:])
 
+        def hidden_place(e):
+            if e < 2 or e in (E - 4, E - 2, E - 1):
+                return E, 0
+            return (e + 3, HIDDEN_AT) if e + 3 <= CAUGHT_UP else (e + 2, HIDDEN_AT + 2 * C * PACK)
+
         def square(e):
-            h_bf[e] = staged("h_bf%d" % e, [P, C, PACK], BF16, e if e + 2 < SHARED_FROM else e + 2, HIDDEN_AT)
-            nc.scalar.activation(h_bf[e][:], turned[e][:].rearrange("p d u -> p u d"), ACT.Square)
+            e0, e1 = min(group for group in H_GROUPS if e < group[1])
+            if e == e0:
+                h_bf[e0] = staged("h_bf%d" % e, [P, e1 - e0, C, PACK], BF16, *hidden_place(e))
+            nc.scalar.activation(h_bf[e0][:, e - e0, :, :], turned[e][:].rearrange("p d u -> p u d"), ACT.Square)
 
-        def quantize_h(e, step):
-            h_w = staged("h_w%d" % e, [P, C], U32, step, H_WORDS_AT + e % 2 * H_BYTES)
-            h_s = staged("h_s%d" % e, [P, C], U8, step, H_WORDS_AT + e % 2 * H_BYTES + PACK * C)
-            nc.vector.quantize_mx(out=h_w[:].bitcast(FP8X4), scales=h_s[:], in_=h_bf[e][:].rearrange("p u d -> p (u d)"))
-            h_q[e] = (h_w, h_s)
+        def quantize_h(e0, e1):
+            h_w = keep.tile([P, (e1 - e0) * C], U32, name="h_w%d" % e0, align_bytes=64)
+            h_s = staged("h_s%d" % e0, [P, (e1 - e0) * C], U8, E - 3, WORDS_AT + e0 * C)
+            nc.vector.quantize_mx(out=h_w[:].bitcast(FP8X4), scales=h_s[:], in_=h_bf[e0][:].rearrange("p e u d -> p (e u d)"))
+            for e in range(e0, e1):
+                h_q[e] = (h_w[:, (e - e0) * C : (e - e0 + 1) * C], h_s[:, (e - e0) * C : (e - e0 + 1) * C])
 
-        for sort in range(SORTS):
-            for g in range(E // GROUP):
-                gather(g, sort)
-        h_step = [max(7 + e // 2, e + 2) for e in range(E)]
-        for step in range(E + 2):
-            early = column_pieces(step)[: 1 if step + 1 < E else 2] if step < E else []
-            if step < E:
-                cast(step)
-                quantize_wp(step, early)
-            for e in [e for e in range(E) if h_step[e] == step and e not in (E - 4, E - 3)]:
-                quantize_h(e, step)
-            if step < E:
-                quantize_wp(step, column_pieces(step)[len(early) :])
-            lag = len(PRE_BANKS) if step < SHARED_FROM else 1
-            if lag <= step < SHARED_FROM:
-                rectify(step - lag)
-            if step < E:
-                first_layer(step)
-            if SHARED_FROM <= step < E:
-                rectify(step - lag)
-            if lag <= step < E:
-                turn(step - lag)
-            if lag < step < E:
-                square(step - lag - 1)
-            if step + 1 == SHARED_FROM:
-                for e in (step - 2, step - 1):
-                    rectify(e)
-                    turn(e)
-                    square(e - 1)
-            if step + 1 == E:
-                quantize_h(step - 3, step)
-                quantize_h(step - 2, step)
+        for g, sort in ((0, 0), (1, 0), (0, 1), (0, 2), (0, 3), (1, 1), (1, 2), (1, 3)):
+            gather(g, sort)
+        for step in range(E):
+            cast(step)
+            quantize_wp(step, column_pieces(step))
+            if step == LAST_GATHERS_STEP:
+                for sort in range(SORTS):
+                    gather(E // GROUP - 1, sort)
+            if step == len(PRE_BANKS):
+                rectify(0)
+            if step == alone - 1:
+                rectify(1)
+            first_layer(step)
+            if step == len(PRE_BANKS):
+                turn(0)
+            if step == alone - 1:
+                turn(1)
+                square(0)
+                rectify(2)
+                turn(2)
+                square(1)
+                rectify(3)
+                turn(3)
+            if step >= alone and step + 2 != E:
+                square(step - 3 if step <= CAUGHT_UP else step - 2)
+                rectify(step - 1)
+                turn(step - 1)
+            if step == CAUGHT_UP:
+                square(step - 2)
+            if step + 3 == E:
                 rectify(step)
                 turn(step)
                 square(step - 1)
-                square(step)
+        rectify(E - 1)
+        turn(E - 1)
+        square(E - 2)
+        square(E - 1)
+        for group in H_GROUPS:
+            quantize_h(*group)
 
         def second_layer(turn, bank, b, experts, engine_copy):
             bank_tile = in_bank("y_bank%d" % turn, [P, len(experts) * C], bank)
@@ -248,8 +261,8 @@ def tile_moe_duo_relu2_kernel(
                     out=bank_tile[:, place * C : (place + 1) * C],
                     lhsT=w2_w[part][e // GROUP][:, e % GROUP, 2 * c0 : 2 * (c0 + P)].bitcast(FP4X4),
                     lhsT_scale=w2_s[part][:, e, c0 : c0 + P],
-                    rhs=h_q[e][0][:].bitcast(FP8X4),
-                    rhs_scale=h_q[e][1][:],
+                    rhs=h_q[e][0].bitcast(FP8X4),
+                    rhs_scale=h_q[e][1],
                     start=True,
                     stop=True,
                 )
@@ -267,7 +280,7 @@ def tile_moe_duo_relu2_kernel(
         for turn, product in enumerate(products):
             second_layer(turn, *product)
 
-        used = [0] * E
+        used = [H_WORDS_AT if e == E - 3 else 0 for e in range(E)]
 
         def spare(name, width):
             region = min(e for e in range(E) if used[e] + 4 * width <= H_WORDS_AT)

@@ -29,9 +29,11 @@ W1_LOADS = ((0, 4, 3), (4, 8, 5), (8, 10, 8), (10, 11, 11), (11, 12, 11))
 BF_BUFFERS = 6
 
 HALF = T // 2
-LAST_PIECES = ((0, HALF), (HALF, 640), (640, T))
+PIECES = HALF // P
+HALVES = ((0, HALF), (HALF, T))
+LAST_SHARE = 256
 
-W2_PARTS = ((0, P), (P, 2 * P), (2 * P, N))
+W2_PARTS = ((0, 2 * P), (2 * P, N))
 
 BANK = 2048
 PRE_BANKS, TURNED_BANKS, Y_BANKS = (0, 1, 2), (3, 4), (5, 6, 7)
@@ -69,10 +71,7 @@ def tile_moe_duo_relu2_kernel(
         w1_s = keep.tile([P, E, H], U8, name="w1_s", align_bytes=64)
         w2_s = [keep.tile([P, E, c1 - c0], U8, name="w2_s%d" % c0, align_bytes=64) for c0, c1 in W2_PARTS]
         w1_w = [keep.tile([P, e1 - e0, 2 * H], U8, name="w1_w%d" % e0, align_bytes=64) for e0, e1, behind in W1_LOADS]
-        w2_w = [
-            [keep.tile([P, GROUP, 2 * (c1 - c0)], U8, name="w2_w%d_%d" % (c0, g), align_bytes=64) for g in range(E // GROUP)]
-            for c0, c1 in W2_PARTS
-        ]
+        w2_w = [keep.tile([P, E, 2 * (c1 - c0)], U8, name="w2_w%d" % c0, align_bytes=64) for c0, c1 in W2_PARTS]
         wp_raw = [stage.tile([P, PACK, H], F32, name="wp_raw%d" % e, align_bytes=64, offset=e * REGION) for e in range(E)]
         gates = [keep.tile([P, T], F32, name="gate%d" % r) for r in range(2)]
         ident = keep.tile([P, P], F32, name="ident")
@@ -98,8 +97,7 @@ def tile_moe_duo_relu2_kernel(
         def load_w2(part):
             c0, c1 = W2_PARTS[part]
             load_scale_rows(nc, w2_s[part][:], w2_scales[:, 0, :, c0:c1])
-            for g in range(E // GROUP):
-                load_packed(w2_w[part][g], w2_words[g * GROUP : (g + 1) * GROUP, 0, :, 2 * c0 : 2 * c1])
+            load_packed(w2_w[part], w2_words[:, 0, :, 2 * c0 : 2 * c1])
 
         nc.sync.dma_start(out=x_w[:], in_=x_words[0].rearrange("p t d -> p (t d)").bitcast(I32))
         nc.sync.dma_start(token_list[:], offs)
@@ -114,11 +112,10 @@ def tile_moe_duo_relu2_kernel(
                     load_packed(w1_w[part], w1_words[e0:e1, 0])
         load_w2(0)
         nc.sync.dma_start(slot_lists[0][:], pos1)
+        nc.sync.dma_start(out=gates[0][:], in_=gate[0])
         nc.sync.dma_start(slot_lists[1][:], pos2)
-        for r in range(2):
-            nc.sync.dma_start(out=gates[r][:], in_=gate[r])
         load_w2(1)
-        load_w2(2)
+        nc.sync.dma_start(out=gates[1][:], in_=gate[1])
 
         gathered, wp_bf, wp_q, pre, rectified, turned, h_bf, h_q = {}, {}, {}, {}, {}, {}, {}, {}
         alone = CAST_ON_VECTOR.index(H)
@@ -252,14 +249,14 @@ def tile_moe_duo_relu2_kernel(
         for group in H_GROUPS:
             quantize_h(*group)
 
-        def second_layer(turn, bank, b, experts, engine_copy):
-            bank_tile = in_bank("y_bank%d" % turn, [P, len(experts) * C], bank)
-            part = min(b, len(W2_PARTS) - 1)
+        def second_layer(b, bank, experts, engine_copy):
+            bank_tile = in_bank("y_bank%d_%d" % (b, experts[0]), [P, len(experts) * C], bank)
+            part = min(n for n, cols in enumerate(W2_PARTS) if b * P < cols[1])
             c0 = b * P - W2_PARTS[part][0]
             for place, e in enumerate(experts):
                 nc.tensor.matmul_mx(
                     out=bank_tile[:, place * C : (place + 1) * C],
-                    lhsT=w2_w[part][e // GROUP][:, e % GROUP, 2 * c0 : 2 * (c0 + P)].bitcast(FP4X4),
+                    lhsT=w2_w[part][:, e, 2 * c0 : 2 * (c0 + P)].bitcast(FP4X4),
                     lhsT_scale=w2_s[part][:, e, c0 : c0 + P],
                     rhs=h_q[e][0].bitcast(FP8X4),
                     rhs_scale=h_q[e][1],
@@ -267,18 +264,6 @@ def tile_moe_duo_relu2_kernel(
                     stop=True,
                 )
             engine_copy(y[b][:, experts[0] * C : (experts[-1] + 1) * C], bank_tile[:])
-
-        products = [
-            (Y_BANKS[0], 0, range(0, GROUP), nc.scalar.copy),
-            (Y_BANKS[1], 0, range(GROUP, 2 * GROUP), nc.vector.tensor_copy),
-            (Y_BANKS[2], 0, range(2 * GROUP, E - 1), nc.scalar.copy),
-            (PRE_BANKS[0], 0, range(E - 1, E), nc.vector.tensor_copy),
-        ]
-        products.extend(
-            (Y_BANKS[g], b, range(g * GROUP, (g + 1) * GROUP), nc.scalar.copy) for b in range(1, N // P) for g in range(E // GROUP)
-        )
-        for turn, product in enumerate(products):
-            second_layer(turn, *product)
 
         used = [H_WORDS_AT if e == E - 3 else 0 for e in range(E)]
 
@@ -294,46 +279,67 @@ def tile_moe_duo_relu2_kernel(
             nc.vector.tensor_tensor(part[:], y[b][:].indirect(entries), gates[r][:, t0:t1], ALU.mult)
             return part
 
-        def add_on_tensor(turn, parts, total):
-            sum_bank = in_bank("sum%d" % turn, [P, HALF], Y_BANKS[1 + turn % 2])
-            for col in range(0, HALF, P):
-                for r in range(2):
-                    nc.tensor.matmul(
-                        sum_bank[:, col : col + P],
-                        parts[r][:, col : col + P],
-                        ident[:],
-                        start=(r == 0),
-                        stop=(r == 1),
-                        is_transpose=True,
-                    )
-            by_token = spare("by_token%d" % turn, HALF)
-            nc.scalar.copy(by_token[:], sum_bank[:])
-            back_bank = in_bank("back%d" % turn, [P, HALF], TURNED_BANKS[turn % 2])
-            for col in range(0, HALF, P):
-                nc.tensor.transpose(back_bank[:, col : col + P], by_token[:, col : col + P], ident[:])
-            nc.scalar.copy(total, back_bank[:])
-
-        def add_on_vector(b, t0, t1, parts):
+        def add_and_store(b, t0, t1, first, second):
             total = spare("total%d_%d" % (b, t0), t1 - t0)
-            nc.vector.tensor_tensor(total[:], parts[0], parts[1], ALU.add)
+            nc.vector.tensor_tensor(total[:], first, second, ALU.add)
             nc.sync.dma_start(out=out[b * P : (b + 1) * P, t0:t1], in_=total[:])
 
-        last = N // P - 1
-        for b in range(last - 1):
-            parts = [weigh(b, r, 0, T) for r in range(2)]
-            total = spare("total%d" % b, T)
-            for half in range(2):
-                tokens = slice(half * HALF, (half + 1) * HALF)
-                add_on_tensor(2 * b + half, [part[:, tokens] for part in parts], total[:, tokens])
-            nc.scalar.dma_start(out=out[b * P : (b + 1) * P, :], in_=total[:])
-        parts = [weigh(last - 1, r, 0, HALF)[:] for r in range(2)]
-        total = spare("total%d" % (last - 1), HALF)
-        add_on_tensor(2 * (last - 1), parts, total[:])
-        nc.scalar.dma_start(out=out[(last - 1) * P : last * P, 0:HALF], in_=total[:])
-        waiting = (last - 1, HALF, T, [weigh(last - 1, r, HALF, T)[:] for r in range(2)])
-        for t0, t1 in LAST_PIECES:
-            parts = [weigh(last, 0, t0, t1)]
-            add_on_vector(*waiting)
-            parts.append(weigh(last, 1, t0, t1))
-            waiting = (last, t0, t1, [part[:] for part in parts])
-        add_on_vector(*waiting)
+        def products(b, banks):
+            for g, bank in enumerate(banks):
+                second_layer(b, bank, range(g * GROUP, (g + 1) * GROUP), nc.scalar.copy)
+
+        def turn_gate(banks):
+            for half, bank in enumerate(banks):
+                gate_bank = in_bank("gate_bank%d" % half, [P, PIECES, P], bank)
+                for piece in range(PIECES):
+                    t0 = half * HALF + piece * P
+                    nc.tensor.transpose(gate_bank[:, piece, :], gates[1][:, t0 : t0 + P], ident[:])
+                nc.scalar.copy(gate_by_token[:, half * PIECES : (half + 1) * PIECES], gate_bank[:, :, 0])
+
+        def pick(b, t0, t1, bank):
+            picked = spare("picked%d_%d" % (b, t0), t1 - t0)
+            nc.scalar.activation(picked[:], y[b][:].indirect(slot_lists[1][:, t0 // PER_COLUMN : t1 // PER_COLUMN]), ACT.Copy)
+            there = in_bank("there%d_%d" % (b, t0), [P, t1 - t0], bank)
+            for col in range(0, t1 - t0, P):
+                nc.tensor.transpose(there[:, col : col + P], picked[:, col : col + P], ident[:])
+            return there
+
+        def turn_back(b, t0, t1, there, bank):
+            scaled = spare("scaled%d_%d" % (b, t0), t1 - t0)
+            for col in range(0, t1 - t0, P):
+                chunk = (t0 + col) // P
+                nc.scalar.activation(
+                    scaled[:, col : col + P], there[:, col : col + P], ACT.Copy, scale=gate_by_token[:, chunk : chunk + 1]
+                )
+            back = in_bank("back%d_%d" % (b, t0), [P, t1 - t0], bank)
+            for col in range(0, t1 - t0, P):
+                nc.tensor.transpose(back[:, col : col + P], scaled[:, col : col + P], ident[:])
+            return back
+
+        def add_in_place(b, first, backs):
+            for (t0, t1), back in zip(HALVES, backs):
+                nc.vector.tensor_tensor(first[:, t0:t1], back[:], first[:, t0:t1], ALU.add)
+            nc.sync.dma_start(out=out[b * P : (b + 1) * P, :], in_=first[:])
+
+        gate_by_token = keep.tile([P, T // P], F32, name="gate_by_token")
+        second_layer(0, 5, range(0, GROUP), nc.scalar.copy)
+        second_layer(0, 6, range(GROUP, 2 * GROUP), nc.vector.tensor_copy)
+        second_layer(0, 7, range(2 * GROUP, E - 1), nc.scalar.copy)
+        second_layer(0, 0, range(E - 1, E), nc.vector.tensor_copy)
+        products(1, (1, 2, 3))
+        firsts = [weigh(b, 0, 0, T) for b in range(2)]
+        theres = [pick(1, *tokens, bank) for tokens, bank in zip(HALVES, (4, 0))]
+        products(2, (5, 6, 7))
+        products(3, (1, 2, 3))
+        turn_gate((5, 6))
+        add_and_store(0, 0, T, firsts[0][:], weigh(0, 1, 0, T)[:])
+        firsts.extend(weigh(b, 0, 0, T) for b in (2, 3))
+        backs = [turn_back(1, *tokens, there, bank) for tokens, there, bank in zip(HALVES, theres, (7, 1))]
+        theres = [pick(2, *tokens, bank) for tokens, bank in zip(HALVES, (2, 3))]
+        add_and_store(3, LAST_SHARE, T, firsts[3][:, LAST_SHARE:T], weigh(3, 1, LAST_SHARE, T)[:])
+        add_in_place(1, firsts[1], backs)
+        backs = [turn_back(2, *tokens, there, bank) for tokens, there, bank in zip(HALVES, theres, (5, 6))]
+        there = pick(3, 0, LAST_SHARE, 4)
+        for (t0, t1), back in zip(HALVES, backs):
+            add_and_store(2, t0, t1, back[:], firsts[2][:, t0:t1])
+        add_and_store(3, 0, LAST_SHARE, turn_back(3, 0, LAST_SHARE, there, 0)[:], firsts[3][:, 0:LAST_SHARE])

@@ -101,10 +101,11 @@ def tile_moe_duo_relu2_kernel(
 
         nc.sync.dma_start(out=x_w[:], in_=x_words[0].rearrange("p t d -> p (t d)").bitcast(I32))
         nc.sync.dma_start(token_list[:], offs)
-        nc.sync.dma_start(partner_list[:], offs2)
-        load_scale_rows(nc, x_s[:], x_scales)
         for e in range(E):
             nc.sync.dma_start(out=wp_raw[e][:], in_=wp[e].rearrange("(p d) c -> p d c", d=PACK))
+            if e == 0:
+                nc.sync.dma_start(partner_list[:], offs2)
+                load_scale_rows(nc, x_s[:], x_scales)
             if e == W1_LOADS[0][2]:
                 load_scale_rows(nc, w1_s[:], w1_scales[:, 0])
             for part, (e0, e1, behind) in enumerate(W1_LOADS):

@@ -29,11 +29,12 @@ W1_LOADS = ((0, 4, 3), (4, 8, 5), (8, 10, 8), (10, 11, 11), (11, 12, 11))
 BF_BUFFERS = 6
 
 HALF = T // 2
-PIECES = HALF // P
 HALVES = ((0, HALF), (HALF, T))
 LAST_SHARE = 256
 
 W2_PARTS = ((0, 2 * P), (2 * P, N))
+W2_EXPERTS = (GROUP, E)
+W2_SCALE_PARTS = ((0, P), (P, 2 * P), (2 * P, N))
 
 BANK = 2048
 PRE_BANKS, TURNED_BANKS, Y_BANKS = (0, 1, 2), (3, 4), (5, 6, 7)
@@ -43,6 +44,7 @@ WORDS_AT, SCALES_AT, H_WORDS_AT, RELU_AT = 0, 2048, 4864, 6144
 HIDDEN_AT = 3072
 GATHERED_AT, UNDER_GATHERED = (0, 2048, 4096, 4608), (1024, 4352)
 LAST_GATHERS_STEP = 3
+SPREAD_STEP, SPREAD_AT = 3, 2560
 CAUGHT_UP = 8
 H_GROUPS = ((0, 2),) + tuple((e, e + 1) for e in range(2, E))
 
@@ -69,14 +71,20 @@ def tile_moe_duo_relu2_kernel(
         x_w = keep.tile([P, T], I32, name="x_w", align_bytes=64)
         x_s = keep.tile([P, 1, T], U8, name="x_s", align_bytes=64)
         w1_s = keep.tile([P, E, H], U8, name="w1_s", align_bytes=64)
-        w2_s = [keep.tile([P, E, c1 - c0], U8, name="w2_s%d" % c0, align_bytes=64) for c0, c1 in W2_PARTS]
+        w2_s = [keep.tile([P, E, c1 - c0], U8, name="w2_s%d" % c0, align_bytes=64) for c0, c1 in W2_SCALE_PARTS]
         w1_w = [keep.tile([P, e1 - e0, 2 * H], U8, name="w1_w%d" % e0, align_bytes=64) for e0, e1, behind in W1_LOADS]
-        w2_w = [keep.tile([P, E, 2 * (c1 - c0)], U8, name="w2_w%d" % c0, align_bytes=64) for c0, c1 in W2_PARTS]
+        w2_w = [
+            [keep.tile([P, size, 2 * (c1 - c0)], U8, name="w2_w%d_%d" % (c0, e0), align_bytes=64) for e0 in range(0, E, size)]
+            for (c0, c1), size in zip(W2_PARTS, W2_EXPERTS)
+        ]
         wp_raw = [stage.tile([P, PACK, H], F32, name="wp_raw%d" % e, align_bytes=64, offset=e * REGION) for e in range(E)]
-        gates = [keep.tile([P, T], F32, name="gate%d" % r) for r in range(2)]
+        gates = [keep.tile([P, T], F32, name="gate0")]
+        gate_rows = keep.tile([P, P], F32, name="gate_rows")
+        gate_by_token = keep.tile([P, T // P], F32, name="gate_by_token")
         ident = keep.tile([P, P], F32, name="ident")
         y = [keep.tile([P, S], F32, name="y%d" % b) for b in range(N // P)]
 
+        nc.vector.memset(gate_rows[:], 0.0)
         nc.gpsimd.memset(x_s[:].bitcast(I32), 0)
         nc.vector.memset(w1_s[:].bitcast(I32), 0)
         make_identity(nc, ident[:])
@@ -94,13 +102,19 @@ def tile_moe_duo_relu2_kernel(
         def load_packed(word_tile, hbm_words):
             nc.sync.dma_start(out=word_tile[:].bitcast(I32), in_=hbm_words.bitcast(I32).rearrange("e p w -> p e w"))
 
+        def load_w2_scales(part):
+            c0, c1 = W2_SCALE_PARTS[part]
+            load_scale_rows(nc, w2_s[part][:], w2_scales[:, 0, :, c0:c1])
+
         def load_w2(part):
             c0, c1 = W2_PARTS[part]
-            load_scale_rows(nc, w2_s[part][:], w2_scales[:, 0, :, c0:c1])
-            load_packed(w2_w[part], w2_words[:, 0, :, 2 * c0 : 2 * c1])
+            size = W2_EXPERTS[part]
+            for e0 in range(0, E, size):
+                load_packed(w2_w[part][e0 // size], w2_words[e0 : e0 + size, 0, :, 2 * c0 : 2 * c1])
 
         nc.sync.dma_start(out=x_w[:], in_=x_words[0].rearrange("p t d -> p (t d)").bitcast(I32))
         nc.sync.dma_start(token_list[:], offs)
+        nc.sync.dma_start(out=gate_rows[0 : T // P, :], in_=gate[1, 0, :].rearrange("(c t) -> c t", t=P))
         for e in range(E):
             nc.sync.dma_start(out=wp_raw[e][:], in_=wp[e].rearrange("(p d) c -> p d c", d=PACK))
             if e == 0:
@@ -111,12 +125,23 @@ def tile_moe_duo_relu2_kernel(
             for part, (e0, e1, behind) in enumerate(W1_LOADS):
                 if behind == e:
                     load_packed(w1_w[part], w1_words[e0:e1, 0])
+        load_w2_scales(0)
         load_w2(0)
+        load_w2_scales(1)
         nc.sync.dma_start(slot_lists[0][:], pos1)
         nc.sync.dma_start(out=gates[0][:], in_=gate[0])
         nc.sync.dma_start(slot_lists[1][:], pos2)
+        load_w2_scales(2)
         load_w2(1)
-        nc.sync.dma_start(out=gates[1][:], in_=gate[1])
+
+        turned_rows = in_bank("turned_rows", [P, P], Y_BANKS[0])
+        nc.tensor.transpose(turned_rows[:], gate_rows[:], ident[:])
+        nc.scalar.copy(gate_by_token[:], turned_rows[:, 0 : T // P])
+        spreads = [in_bank("spread%d" % t0, [P, HALF], bank) for (t0, t1), bank in zip(HALVES, Y_BANKS[1:])]
+        for (t0, t1), spread in zip(HALVES, spreads):
+            for col in range(0, HALF, P):
+                chunk = (t0 + col) // P
+                nc.tensor.transpose(spread[:, col : col + P], gate_by_token[:, chunk : chunk + 1].to_broadcast([P, P]), ident[:])
 
         gathered, wp_bf, wp_q, pre, rectified, turned, h_bf, h_q = {}, {}, {}, {}, {}, {}, {}, {}
         alone = CAST_ON_VECTOR.index(H)
@@ -218,6 +243,10 @@ def tile_moe_duo_relu2_kernel(
             if step == LAST_GATHERS_STEP:
                 for sort in range(SORTS):
                     gather(E // GROUP - 1, sort)
+            if step == SPREAD_STEP:
+                gates.append(staged("gate1", [P, T], F32, step, SPREAD_AT))
+                for (t0, t1), spread in zip(HALVES, spreads):
+                    nc.scalar.copy(gates[1][:, t0:t1], spread[:])
             if step == len(PRE_BANKS):
                 rectify(0)
             if step == alone - 1:
@@ -254,11 +283,13 @@ def tile_moe_duo_relu2_kernel(
             bank_tile = in_bank("y_bank%d_%d" % (b, experts[0]), [P, len(experts) * C], bank)
             part = min(n for n, cols in enumerate(W2_PARTS) if b * P < cols[1])
             c0 = b * P - W2_PARTS[part][0]
+            scale_part = min(b, len(W2_SCALE_PARTS) - 1)
+            s0 = b * P - W2_SCALE_PARTS[scale_part][0]
             for place, e in enumerate(experts):
                 nc.tensor.matmul_mx(
                     out=bank_tile[:, place * C : (place + 1) * C],
-                    lhsT=w2_w[part][:, e, 2 * c0 : 2 * (c0 + P)].bitcast(FP4X4),
-                    lhsT_scale=w2_s[part][:, e, c0 : c0 + P],
+                    lhsT=w2_w[part][e // W2_EXPERTS[part]][:, e % W2_EXPERTS[part], 2 * c0 : 2 * (c0 + P)].bitcast(FP4X4),
+                    lhsT_scale=w2_s[scale_part][:, e, s0 : s0 + P],
                     rhs=h_q[e][0].bitcast(FP8X4),
                     rhs_scale=h_q[e][1],
                     start=True,
@@ -269,7 +300,7 @@ def tile_moe_duo_relu2_kernel(
         used = [H_WORDS_AT if e == E - 3 else 0 for e in range(E)]
 
         def spare(name, width):
-            region = min(e for e in range(E) if used[e] + 4 * width <= H_WORDS_AT)
+            region = min(e for e in range(E) if used[e] + 4 * width <= (SPREAD_AT if e == SPREAD_STEP else H_WORDS_AT))
             at = region * REGION + used[region]
             used[region] = used[region] + 4 * width
             return stage.tile([P, width], F32, name=name, align_bytes=64, offset=at)
@@ -285,17 +316,9 @@ def tile_moe_duo_relu2_kernel(
             nc.vector.tensor_tensor(total[:], first, second, ALU.add)
             nc.sync.dma_start(out=out[b * P : (b + 1) * P, t0:t1], in_=total[:])
 
-        def products(b, banks):
-            for g, bank in enumerate(banks):
+        def products(b, groups, banks):
+            for g, bank in zip(groups, banks):
                 second_layer(b, bank, range(g * GROUP, (g + 1) * GROUP), nc.scalar.copy)
-
-        def turn_gate(banks):
-            for half, bank in enumerate(banks):
-                gate_bank = in_bank("gate_bank%d" % half, [P, PIECES, P], bank)
-                for piece in range(PIECES):
-                    t0 = half * HALF + piece * P
-                    nc.tensor.transpose(gate_bank[:, piece, :], gates[1][:, t0 : t0 + P], ident[:])
-                nc.scalar.copy(gate_by_token[:, half * PIECES : (half + 1) * PIECES], gate_bank[:, :, 0])
 
         def pick(b, t0, t1, bank):
             picked = spare("picked%d_%d" % (b, t0), t1 - t0)
@@ -305,13 +328,16 @@ def tile_moe_duo_relu2_kernel(
                 nc.tensor.transpose(there[:, col : col + P], picked[:, col : col + P], ident[:])
             return there
 
-        def turn_back(b, t0, t1, there, bank):
+        def scale(b, t0, t1, there):
             scaled = spare("scaled%d_%d" % (b, t0), t1 - t0)
             for col in range(0, t1 - t0, P):
                 chunk = (t0 + col) // P
                 nc.scalar.activation(
                     scaled[:, col : col + P], there[:, col : col + P], ACT.Copy, scale=gate_by_token[:, chunk : chunk + 1]
                 )
+            return scaled
+
+        def turn_back(b, t0, t1, scaled, bank):
             back = in_bank("back%d_%d" % (b, t0), [P, t1 - t0], bank)
             for col in range(0, t1 - t0, P):
                 nc.tensor.transpose(back[:, col : col + P], scaled[:, col : col + P], ident[:])
@@ -322,25 +348,30 @@ def tile_moe_duo_relu2_kernel(
                 nc.vector.tensor_tensor(first[:, t0:t1], back[:], first[:, t0:t1], ALU.add)
             nc.sync.dma_start(out=out[b * P : (b + 1) * P, :], in_=first[:])
 
-        gate_by_token = keep.tile([P, T // P], F32, name="gate_by_token")
         second_layer(0, 5, range(0, GROUP), nc.scalar.copy)
         second_layer(0, 6, range(GROUP, 2 * GROUP), nc.vector.tensor_copy)
         second_layer(0, 7, range(2 * GROUP, E - 1), nc.scalar.copy)
         second_layer(0, 0, range(E - 1, E), nc.vector.tensor_copy)
-        products(1, (1, 2, 3))
-        firsts = [weigh(b, 0, 0, T) for b in range(2)]
+        products(1, (0, 1, 2), (1, 2, 3))
+        firsts = [weigh(0, 0, 0, T)]
+        second = weigh(0, 1, 0, T)
+        firsts.append(weigh(1, 0, 0, T))
         theres = [pick(1, *tokens, bank) for tokens, bank in zip(HALVES, (4, 0))]
-        products(2, (5, 6, 7))
-        products(3, (1, 2, 3))
-        turn_gate((5, 6))
-        add_and_store(0, 0, T, firsts[0][:], weigh(0, 1, 0, T)[:])
-        firsts.extend(weigh(b, 0, 0, T) for b in (2, 3))
-        backs = [turn_back(1, *tokens, there, bank) for tokens, there, bank in zip(HALVES, theres, (7, 1))]
-        theres = [pick(2, *tokens, bank) for tokens, bank in zip(HALVES, (2, 3))]
-        add_and_store(3, LAST_SHARE, T, firsts[3][:, LAST_SHARE:T], weigh(3, 1, LAST_SHARE, T)[:])
+        add_and_store(0, 0, T, firsts[0][:], second[:])
+        scaled = [scale(1, *tokens, there) for tokens, there in zip(HALVES, theres)]
+        products(2, (0, 1, 2), (5, 6, 7))
+        products(3, (0, 1, 2), (1, 2, 3))
+        backs = [turn_back(1, *tokens, part, bank) for tokens, part, bank in zip(HALVES, scaled, (5, 6))]
         add_in_place(1, firsts[1], backs)
-        backs = [turn_back(2, *tokens, there, bank) for tokens, there, bank in zip(HALVES, theres, (5, 6))]
-        there = pick(3, 0, LAST_SHARE, 4)
+        firsts.append(weigh(2, 0, 0, T))
+        parts = [weigh(3, r, LAST_SHARE, T) for r in range(2)]
+        firsts.append(weigh(3, 0, 0, LAST_SHARE))
+        theres = [pick(2, *tokens, bank) for tokens, bank in zip(HALVES, (7, 4))]
+        add_and_store(3, LAST_SHARE, T, parts[0][:], parts[1][:])
+        backs = [turn_back(2, *HALVES[0], scale(2, *HALVES[0], theres[0]), 0)]
+        there = pick(3, 0, LAST_SHARE, 2)
+        backs.append(turn_back(2, *HALVES[1], scale(2, *HALVES[1], theres[1]), 1))
         for (t0, t1), back in zip(HALVES, backs):
             add_and_store(2, t0, t1, back[:], firsts[2][:, t0:t1])
-        add_and_store(3, 0, LAST_SHARE, turn_back(3, 0, LAST_SHARE, there, 0)[:], firsts[3][:, 0:LAST_SHARE])
+        back = turn_back(3, 0, LAST_SHARE, scale(3, 0, LAST_SHARE, there), 3)
+        add_and_store(3, 0, LAST_SHARE, back[:], firsts[3][:])

@@ -44,7 +44,7 @@ WORDS_AT, SCALES_AT, H_WORDS_AT, RELU_AT = 0, 2048, 4864, 6144
 HIDDEN_AT = 3072
 GATHERED_AT, UNDER_GATHERED = (0, 2048, 4096, 4608), (1024, 4352)
 LAST_GATHERS_STEP = 3
-SPREAD_STEP, SPREAD_AT = 3, 2560
+LISTS_BEHIND = 6
 CAUGHT_UP = 8
 H_GROUPS = ((0, 2),) + tuple((e, e + 1) for e in range(2, E))
 
@@ -78,13 +78,11 @@ def tile_moe_duo_relu2_kernel(
             for (c0, c1), size in zip(W2_PARTS, W2_EXPERTS)
         ]
         wp_raw = [stage.tile([P, PACK, H], F32, name="wp_raw%d" % e, align_bytes=64, offset=e * REGION) for e in range(E)]
-        gates = [keep.tile([P, T], F32, name="gate0")]
-        gate_rows = keep.tile([P, P], F32, name="gate_rows")
+        gates = [keep.tile([P, T], F32, name="gate%d" % r) for r in range(2)]
         gate_by_token = keep.tile([P, T // P], F32, name="gate_by_token")
         ident = keep.tile([P, P], F32, name="ident")
         y = [keep.tile([P, S], F32, name="y%d" % b) for b in range(N // P)]
 
-        nc.vector.memset(gate_rows[:], 0.0)
         nc.gpsimd.memset(x_s[:].bitcast(I32), 0)
         nc.vector.memset(w1_s[:].bitcast(I32), 0)
         make_identity(nc, ident[:])
@@ -114,12 +112,13 @@ def tile_moe_duo_relu2_kernel(
 
         nc.sync.dma_start(out=x_w[:], in_=x_words[0].rearrange("p t d -> p (t d)").bitcast(I32))
         nc.sync.dma_start(token_list[:], offs)
-        nc.sync.dma_start(out=gate_rows[0 : T // P, :], in_=gate[1, 0, :].rearrange("(c t) -> c t", t=P))
+        nc.sync.dma_start(partner_list[:], offs2)
+        load_scale_rows(nc, x_s[:], x_scales)
         for e in range(E):
             nc.sync.dma_start(out=wp_raw[e][:], in_=wp[e].rearrange("(p d) c -> p d c", d=PACK))
-            if e == 0:
-                nc.sync.dma_start(partner_list[:], offs2)
-                load_scale_rows(nc, x_s[:], x_scales)
+            if e == LISTS_BEHIND:
+                nc.sync.dma_start(slot_lists[0][:], pos1)
+                nc.sync.dma_start(slot_lists[1][:], pos2)
             if e == W1_LOADS[0][2]:
                 load_scale_rows(nc, w1_s[:], w1_scales[:, 0])
             for part, (e0, e1, behind) in enumerate(W1_LOADS):
@@ -128,20 +127,10 @@ def tile_moe_duo_relu2_kernel(
         load_w2_scales(0)
         load_w2(0)
         load_w2_scales(1)
-        nc.sync.dma_start(slot_lists[0][:], pos1)
-        nc.sync.dma_start(out=gates[0][:], in_=gate[0])
-        nc.sync.dma_start(slot_lists[1][:], pos2)
+        for r in range(2):
+            nc.sync.dma_start(out=gates[r][:], in_=gate[r])
         load_w2_scales(2)
         load_w2(1)
-
-        turned_rows = in_bank("turned_rows", [P, P], Y_BANKS[0])
-        nc.tensor.transpose(turned_rows[:], gate_rows[:], ident[:])
-        nc.scalar.copy(gate_by_token[:], turned_rows[:, 0 : T // P])
-        spreads = [in_bank("spread%d" % t0, [P, HALF], bank) for (t0, t1), bank in zip(HALVES, Y_BANKS[1:])]
-        for (t0, t1), spread in zip(HALVES, spreads):
-            for col in range(0, HALF, P):
-                chunk = (t0 + col) // P
-                nc.tensor.transpose(spread[:, col : col + P], gate_by_token[:, chunk : chunk + 1].to_broadcast([P, P]), ident[:])
 
         gathered, wp_bf, wp_q, pre, rectified, turned, h_bf, h_q = {}, {}, {}, {}, {}, {}, {}, {}
         alone = CAST_ON_VECTOR.index(H)
@@ -243,10 +232,6 @@ def tile_moe_duo_relu2_kernel(
             if step == LAST_GATHERS_STEP:
                 for sort in range(SORTS):
                     gather(E // GROUP - 1, sort)
-            if step == SPREAD_STEP:
-                gates.append(staged("gate1", [P, T], F32, step, SPREAD_AT))
-                for (t0, t1), spread in zip(HALVES, spreads):
-                    nc.scalar.copy(gates[1][:, t0:t1], spread[:])
             if step == len(PRE_BANKS):
                 rectify(0)
             if step == alone - 1:
@@ -300,7 +285,7 @@ def tile_moe_duo_relu2_kernel(
         used = [H_WORDS_AT if e == E - 3 else 0 for e in range(E)]
 
         def spare(name, width):
-            region = min(e for e in range(E) if used[e] + 4 * width <= (SPREAD_AT if e == SPREAD_STEP else H_WORDS_AT))
+            region = min(e for e in range(E) if used[e] + 4 * width <= H_WORDS_AT)
             at = region * REGION + used[region]
             used[region] = used[region] + 4 * width
             return stage.tile([P, width], F32, name=name, align_bytes=64, offset=at)
@@ -319,6 +304,13 @@ def tile_moe_duo_relu2_kernel(
         def products(b, groups, banks):
             for g, bank in zip(groups, banks):
                 second_layer(b, bank, range(g * GROUP, (g + 1) * GROUP), nc.scalar.copy)
+
+        def turn_gate(banks):
+            for (t0, t1), bank in zip(HALVES, banks):
+                gate_bank = in_bank("gate_bank%d" % t0, [P, HALF // P, P], bank)
+                for col in range(t0, t1, P):
+                    nc.tensor.transpose(gate_bank[:, (col - t0) // P, :], gates[1][:, col : col + P], ident[:])
+                nc.scalar.copy(gate_by_token[:, t0 // P : t1 // P], gate_bank[:, :, 0])
 
         def pick(b, t0, t1, bank):
             picked = spare("picked%d_%d" % (b, t0), t1 - t0)
@@ -357,6 +349,7 @@ def tile_moe_duo_relu2_kernel(
         second = weigh(0, 1, 0, T)
         firsts.append(weigh(1, 0, 0, T))
         theres = [pick(1, *tokens, bank) for tokens, bank in zip(HALVES, (4, 0))]
+        turn_gate((5, 6))
         add_and_store(0, 0, T, firsts[0][:], second[:])
         scaled = [scale(1, *tokens, there) for tokens, there in zip(HALVES, theres)]
         products(2, (0, 1, 2), (5, 6, 7))

@@ -30,7 +30,7 @@ BF_BUFFERS = 6
 
 HALF = T // 2
 HALVES = ((0, HALF), (HALF, T))
-LAST_SHARE = 256
+LAST_SHARE = 384
 
 W2_PARTS = ((0, 2 * P), (2 * P, N))
 W2_EXPERTS = (GROUP, E)
@@ -343,7 +343,7 @@ def tile_moe_duo_relu2_kernel(
         second_layer(0, 5, range(0, GROUP), nc.scalar.copy)
         second_layer(0, 6, range(GROUP, 2 * GROUP), nc.vector.tensor_copy)
         second_layer(0, 7, range(2 * GROUP, E - 1), nc.scalar.copy)
-        second_layer(0, 0, range(E - 1, E), nc.vector.tensor_copy)
+        second_layer(0, 0, range(E - 1, E), nc.scalar.copy)
         products(1, (0, 1, 2), (1, 2, 3))
         firsts = [weigh(0, 0, 0, T)]
         second = weigh(0, 1, 0, T)
@@ -352,19 +352,21 @@ def tile_moe_duo_relu2_kernel(
         turn_gate((5, 6))
         add_and_store(0, 0, T, firsts[0][:], second[:])
         scaled = [scale(1, *tokens, there) for tokens, there in zip(HALVES, theres)]
-        products(2, (0, 1, 2), (5, 6, 7))
-        products(3, (0, 1, 2), (1, 2, 3))
-        backs = [turn_back(1, *tokens, part, bank) for tokens, part, bank in zip(HALVES, scaled, (5, 6))]
-        add_in_place(1, firsts[1], backs)
+        products(2, (0, 1), (5, 6))
+        second_layer(2, 7, range(2 * GROUP, E), nc.vector.tensor_copy)
         firsts.append(weigh(2, 0, 0, T))
+        products(3, (0, 1, 2), (1, 2, 3))
+        backs = [turn_back(1, *tokens, part, bank) for tokens, part, bank in zip(HALVES, scaled, (1, 2))]
+        add_in_place(1, firsts[1], backs)
         parts = [weigh(3, r, LAST_SHARE, T) for r in range(2)]
         firsts.append(weigh(3, 0, 0, LAST_SHARE))
-        theres = [pick(2, *tokens, bank) for tokens, bank in zip(HALVES, (7, 4))]
+        theres = [pick(2, *tokens, bank) for tokens, bank in zip(HALVES, (5, 4))]
         add_and_store(3, LAST_SHARE, T, parts[0][:], parts[1][:])
+        there = pick(3, 0, LAST_SHARE, 6)
         backs = [turn_back(2, *HALVES[0], scale(2, *HALVES[0], theres[0]), 0)]
-        there = pick(3, 0, LAST_SHARE, 2)
-        backs.append(turn_back(2, *HALVES[1], scale(2, *HALVES[1], theres[1]), 1))
+        backs.append(turn_back(2, *HALVES[1], scale(2, *HALVES[1], theres[1]), 7))
         for (t0, t1), back in zip(HALVES, backs):
             add_and_store(2, t0, t1, back[:], firsts[2][:, t0:t1])
-        back = turn_back(3, 0, LAST_SHARE, scale(3, 0, LAST_SHARE, there), 3)
-        add_and_store(3, 0, LAST_SHARE, back[:], firsts[3][:])
+        scaled = scale(3, 0, LAST_SHARE, there)
+        for (t0, t1), bank in zip(((0, LAST_SHARE - P), (LAST_SHARE - P, LAST_SHARE)), (3, 1)):
+            add_and_store(3, t0, t1, turn_back(3, t0, t1, scaled[:, t0:t1], bank)[:], firsts[3][:, t0:t1])

@@ -198,7 +198,11 @@ def tile_moe_duo_relu2_kernel(
             rectified[e] = relu
             for c0, c1 in column_pieces(e) if e + 1 == E else [(0, H)]:
                 planes = slice(c0 // P, c1 // P)
-                nc.scalar.activation(relu[:, planes, :], pre[e][:].rearrange("u (p d) -> u d p", d=PACK)[:, planes, :], ACT.Relu)
+                by_plane = pre[e][:].rearrange("u (p d) -> u d p", d=PACK)[:, planes, :]
+                if e + 2 == E:
+                    nc.vector.tensor_scalar_max(relu[:, planes, :], by_plane, 0.0)
+                else:
+                    nc.scalar.activation(relu[:, planes, :], by_plane, ACT.Relu)
 
         def turn(e):
             relu = rectified[e]
@@ -296,9 +300,9 @@ def tile_moe_duo_relu2_kernel(
             nc.vector.tensor_tensor(part[:], y[b][:].indirect(entries), gates[r][:, t0:t1], ALU.mult)
             return part
 
-        def add_and_store(b, t0, t1, first, second):
+        def add_and_store(b, t0, t1, first, second, engine=nc.vector):
             total = spare("total%d_%d" % (b, t0), t1 - t0)
-            nc.vector.tensor_tensor(total[:], first, second, ALU.add)
+            engine.tensor_tensor(total[:], first, second, ALU.add)
             nc.sync.dma_start(out=out[b * P : (b + 1) * P, t0:t1], in_=total[:])
 
         def products(b, groups, banks):
@@ -337,14 +341,15 @@ def tile_moe_duo_relu2_kernel(
 
         def add_in_place(b, first, backs):
             for (t0, t1), back in zip(HALVES, backs):
-                nc.vector.tensor_tensor(first[:, t0:t1], back[:], first[:, t0:t1], ALU.add)
+                nc.vector.tensor_tensor(first[:, t0:t1], first[:, t0:t1], back[:], ALU.add)
             nc.sync.dma_start(out=out[b * P : (b + 1) * P, :], in_=first[:])
 
         second_layer(0, 5, range(0, GROUP), nc.scalar.copy)
         second_layer(0, 6, range(GROUP, 2 * GROUP), nc.vector.tensor_copy)
         second_layer(0, 7, range(2 * GROUP, E - 1), nc.scalar.copy)
         second_layer(0, 0, range(E - 1, E), nc.scalar.copy)
-        products(1, (0, 1, 2), (1, 2, 3))
+        second_layer(1, 1, range(0, GROUP), nc.vector.tensor_copy)
+        products(1, (1, 2), (2, 3))
         firsts = [weigh(0, 0, 0, T)]
         second = weigh(0, 1, 0, T)
         firsts.append(weigh(1, 0, 0, T))
@@ -361,12 +366,12 @@ def tile_moe_duo_relu2_kernel(
         parts = [weigh(3, r, LAST_SHARE, T) for r in range(2)]
         firsts.append(weigh(3, 0, 0, LAST_SHARE))
         theres = [pick(2, *tokens, bank) for tokens, bank in zip(HALVES, (5, 4))]
-        add_and_store(3, LAST_SHARE, T, parts[0][:], parts[1][:])
+        add_and_store(3, LAST_SHARE, T, parts[0][:], parts[1][:], nc.gpsimd)
         there = pick(3, 0, LAST_SHARE, 6)
         backs = [turn_back(2, *HALVES[0], scale(2, *HALVES[0], theres[0]), 0)]
         backs.append(turn_back(2, *HALVES[1], scale(2, *HALVES[1], theres[1]), 7))
         for (t0, t1), back in zip(HALVES, backs):
-            add_and_store(2, t0, t1, back[:], firsts[2][:, t0:t1])
+            add_and_store(2, t0, t1, firsts[2][:, t0:t1], back[:])
         scaled = scale(3, 0, LAST_SHARE, there)
         for (t0, t1), bank in zip(((0, LAST_SHARE - P), (LAST_SHARE - P, LAST_SHARE)), (3, 1)):
-            add_and_store(3, t0, t1, turn_back(3, t0, t1, scaled[:, t0:t1], bank)[:], firsts[3][:, t0:t1])
+            add_and_store(3, t0, t1, firsts[3][:, t0:t1], turn_back(3, t0, t1, scaled[:, t0:t1], bank)[:])

@@ -44,6 +44,7 @@ WORDS_AT, SCALES_AT, H_WORDS_AT, RELU_AT = 0, 2048, 4864, 6144
 HIDDEN_AT = 3072
 GATHERED_AT, UNDER_GATHERED = (0, 2048, 4096, 4608), (1024, 4352)
 LAST_GATHERS_STEP = 3
+GATE_ROW_LOADS = ((0, 4), (4, 6))
 LISTS_BEHIND = 6
 CAUGHT_UP = 8
 H_GROUPS = ((0, 2),) + tuple((e, e + 1) for e in range(2, E))
@@ -80,12 +81,14 @@ def tile_moe_duo_relu2_kernel(
         wp_raw = [stage.tile([P, PACK, H], F32, name="wp_raw%d" % e, align_bytes=64, offset=e * REGION) for e in range(E)]
         gates = [keep.tile([P, T], F32, name="gate%d" % r) for r in range(2)]
         gate_by_token = keep.tile([P, T // P], F32, name="gate_by_token")
+        gate_rows = keep.tile([P, P], F32, name="gate_rows")
         ident = keep.tile([P, P], F32, name="ident")
         y = [keep.tile([P, S], F32, name="y%d" % b) for b in range(N // P)]
 
         nc.gpsimd.memset(x_s[:].bitcast(I32), 0)
         nc.vector.memset(w1_s[:].bitcast(I32), 0)
         make_identity(nc, ident[:])
+        nc.gpsimd.memset(gate_rows[:], 0.0)
         for scale_tile in w2_s:
             nc.gpsimd.memset(scale_tile[:].bitcast(I32), 0)
 
@@ -116,6 +119,9 @@ def tile_moe_duo_relu2_kernel(
         load_scale_rows(nc, x_s[:], x_scales)
         for e in range(E):
             nc.sync.dma_start(out=wp_raw[e][:], in_=wp[e].rearrange("(p d) c -> p d c", d=PACK))
+            if e == 1:
+                for c0, c1 in GATE_ROW_LOADS:
+                    nc.sync.dma_start(out=gate_rows[c0:c1, :], in_=gate[1, 0, c0 * P : c1 * P].rearrange("(c t) -> c t", t=P))
             if e == LISTS_BEHIND:
                 nc.sync.dma_start(slot_lists[0][:], pos1)
                 nc.sync.dma_start(slot_lists[1][:], pos2)
@@ -127,10 +133,13 @@ def tile_moe_duo_relu2_kernel(
         load_w2_scales(0)
         load_w2(0)
         load_w2_scales(1)
-        for r in range(2):
-            nc.sync.dma_start(out=gates[r][:], in_=gate[r])
+        nc.sync.dma_start(out=gates[0][:], in_=gate[0])
         load_w2_scales(2)
         load_w2(1)
+
+        turned_rows = in_bank("turned_rows", [P, P], Y_BANKS[0])
+        nc.tensor.transpose(turned_rows[:], gate_rows[:], ident[:])
+        nc.scalar.copy(gate_by_token[:], turned_rows[:, 0 : T // P])
 
         gathered, wp_bf, wp_q, pre, rectified, turned, h_bf, h_q = {}, {}, {}, {}, {}, {}, {}, {}
         alone = CAST_ON_VECTOR.index(H)
@@ -309,12 +318,13 @@ def tile_moe_duo_relu2_kernel(
             for g, bank in zip(groups, banks):
                 second_layer(b, bank, range(g * GROUP, (g + 1) * GROUP), nc.scalar.copy)
 
-        def turn_gate(banks):
+        def spread_gate(banks):
             for (t0, t1), bank in zip(HALVES, banks):
-                gate_bank = in_bank("gate_bank%d" % t0, [P, HALF // P, P], bank)
+                spread = in_bank("spread%d" % t0, [P, HALF], bank)
                 for col in range(t0, t1, P):
-                    nc.tensor.transpose(gate_bank[:, (col - t0) // P, :], gates[1][:, col : col + P], ident[:])
-                nc.scalar.copy(gate_by_token[:, t0 // P : t1 // P], gate_bank[:, :, 0])
+                    column = gate_by_token[:, col // P : col // P + 1]
+                    nc.tensor.transpose(spread[:, col - t0 : col - t0 + P], column.to_broadcast([P, P]), ident[:])
+                nc.scalar.copy(gates[1][:, t0:t1], spread[:])
 
         def pick(b, t0, t1, bank):
             picked = spare("picked%d_%d" % (b, t0), t1 - t0)
@@ -350,15 +360,14 @@ def tile_moe_duo_relu2_kernel(
         second_layer(0, 0, range(E - 1, E), nc.scalar.copy)
         second_layer(1, 1, range(0, GROUP), nc.vector.tensor_copy)
         products(1, (1, 2), (2, 3))
-        firsts = [weigh(0, 0, 0, T)]
+        spread_gate((1, 2))
+        firsts = [weigh(b, 0, 0, T) for b in range(2)]
         second = weigh(0, 1, 0, T)
-        firsts.append(weigh(1, 0, 0, T))
         theres = [pick(1, *tokens, bank) for tokens, bank in zip(HALVES, (4, 0))]
-        turn_gate((5, 6))
-        add_and_store(0, 0, T, firsts[0][:], second[:])
         scaled = [scale(1, *tokens, there) for tokens, there in zip(HALVES, theres)]
         products(2, (0, 1), (5, 6))
         second_layer(2, 7, range(2 * GROUP, E), nc.vector.tensor_copy)
+        add_and_store(0, 0, T, firsts[0][:], second[:])
         firsts.append(weigh(2, 0, 0, T))
         products(3, (0, 1, 2), (1, 2, 3))
         backs = [turn_back(1, *tokens, part, bank) for tokens, part, bank in zip(HALVES, scaled, (1, 2))]
@@ -366,7 +375,7 @@ def tile_moe_duo_relu2_kernel(
         parts = [weigh(3, r, LAST_SHARE, T) for r in range(2)]
         firsts.append(weigh(3, 0, 0, LAST_SHARE))
         theres = [pick(2, *tokens, bank) for tokens, bank in zip(HALVES, (5, 4))]
-        add_and_store(3, LAST_SHARE, T, parts[0][:], parts[1][:], nc.gpsimd)
+        add_and_store(3, LAST_SHARE, T, parts[0][:], parts[1][:])
         there = pick(3, 0, LAST_SHARE, 6)
         backs = [turn_back(2, *HALVES[0], scale(2, *HALVES[0], theres[0]), 0)]
         backs.append(turn_back(2, *HALVES[1], scale(2, *HALVES[1], theres[1]), 7))

from contextlib import ExitStack

import concourse.mybir as mybir
from concourse.masks import make_identity

K, T, E, C, H, N = 512, 768, 12, 128, 512, 512
S = E * C
P = 128
PACK = 4
PER_COLUMN = 16
FLOPS = 2 * S * (2 * K * H + H * N)

F32 = mybir.dt.float32
BF16 = mybir.dt.bfloat16
I32 = mybir.dt.int32
U32 = mybir.dt.uint32
U16 = mybir.dt.uint16
U8 = mybir.dt.uint8
FP8X4 = mybir.dt.float8_e4m3fn_x4
FP4X4 = mybir.dt.float4_e2m1fn_x4
ACT = mybir.ActivationFunctionType
ALU = mybir.AluOpType

GROUP = 4
SORTS = 4

CAST_ON_VECTOR = (0, 0, 0, 0, 0, 512, 512, 512, 512, 512, 512, 320)
W1_LOADS = ((0, 4, 3), (4, 8, 5), (8, 10, 8), (10, 11, 11), (11, 12, 11))
BF_BUFFERS = 6

HALF = T // 2
HALVES = ((0, HALF), (HALF, T))
LAST_SHARE = 384

W2_PARTS = ((0, 2 * P), (2 * P, N))
W2_EXPERTS = (GROUP, E)
W2_SCALE_PARTS = ((0, P), (P, 2 * P), (2 * P, N))

BANK = 2048
PRE_BANKS, TURNED_BANKS, Y_BANKS = (0, 1, 2), (3, 4), (5, 6, 7)

REGION = PACK * H * 4
WORDS_AT, SCALES_AT, H_WORDS_AT, RELU_AT = 0, 2048, 4864, 6144
HIDDEN_AT = 3072
GATHERED_AT, UNDER_GATHERED = (0, 2048, 4096, 4608), (1024, 4352)
LAST_GATHERS_STEP = 3
GATE_ROW_LOADS = ((0, 4), (4, 6))
LISTS_BEHIND = 6
CAUGHT_UP = 8
H_GROUPS = ((0, 2),) + tuple((e, e + 1) for e in range(2, E))


def load_scale_rows(nc, scale_tile, rows):
    by_place = rows.bitcast(I32).rearrange("m (q j) w -> j q m w", j=4)
    for j in range(4):
        nc.sync.dma_start(out=scale_tile.bitcast(I32)[j:P:32, :, :], in_=by_place[j])


def tile_moe_duo_relu2_kernel(
    tc, x_words, x_scales, w1_words, w1_scales, wp, w2_words, w2_scales, gate, offs, pos1, pos2, offs2, out
):
    nc = tc.nc
    with ExitStack() as ctx:
        keep = ctx.enter_context(tc.tile_pool(name="keep", bufs=1))
        stage = ctx.enter_context(tc.tile_pool(name="stage", bufs=1))
        rounded = ctx.enter_context(tc.tile_pool(name="rounded", bufs=1))
        psum = ctx.enter_context(tc.psum_pool(name="psum", bufs=1))

        token_list = keep.tile([P, S // PER_COLUMN], U16, name="token_list")
        partner_list = keep.tile([P, S // PER_COLUMN], U16, name="partner_list")
        slot_lists = [keep.tile([P, T // PER_COLUMN], U16, name="slot_list%d" % r) for r in range(2)]
        x_w = keep.tile([P, T], I32, name="x_w", align_bytes=64)
        x_s = keep.tile([P, 1, T], U8, name="x_s", align_bytes=64)
        w1_s = keep.tile([P, E, H], U8, name="w1_s", align_bytes=64)
        w2_s = [keep.tile([P, E, c1 - c0], U8, name="w2_s%d" % c0, align_bytes=64) for c0, c1 in W2_SCALE_PARTS]
        w1_w = [keep.tile([P, e1 - e0, 2 * H], U8, name="w1_w%d" % e0, align_bytes=64) for e0, e1, behind in W1_LOADS]
        w2_w = [
            [keep.tile([P, size, 2 * (c1 - c0)], U8, name="w2_w%d_%d" % (c0, e0), align_bytes=64) for e0 in range(0, E, size)]
            for (c0, c1), size in zip(W2_PARTS, W2_EXPERTS)
        ]
        wp_raw = [stage.tile([P, PACK, H], F32, name="wp_raw%d" % e, align_bytes=64, offset=e * REGION) for e in range(E)]
        gates = [keep.tile([P, T], F32, name="gate%d" % r) for r in range(2)]
        gate_by_token = keep.tile([P, T // P], F32, name="gate_by_token")
        gate_rows = keep.tile([P, P], F32, name="gate_rows")
        ident = keep.tile([P, P], F32, name="ident")
        y = [keep.tile([P, S], F32, name="y%d" % b) for b in range(N // P)]

        nc.gpsimd.memset(x_s[:].bitcast(I32), 0)
        nc.vector.memset(w1_s[:].bitcast(I32), 0)
        make_identity(nc, ident[:])
        nc.gpsimd.memset(gate_rows[:], 0.0)
        for scale_tile in w2_s:
            nc.gpsimd.memset(scale_tile[:].bitcast(I32), 0)

        def staged(name, shape, dtype, step, at):
            if 0 <= step < E:
                return stage.tile(shape, dtype, name=name, align_bytes=64, offset=step * REGION + at)
            return keep.tile(shape, dtype, name=name, align_bytes=64)

        def in_bank(name, shape, bank):
            return psum.tile(shape, F32, name=name, offset=bank * BANK)

        def load_packed(word_tile, hbm_words):
            nc.sync.dma_start(out=word_tile[:].bitcast(I32), in_=hbm_words.bitcast(I32).rearrange("e p w -> p e w"))

        def load_w2_scales(part):
            c0, c1 = W2_SCALE_PARTS[part]
            load_scale_rows(nc, w2_s[part][:], w2_scales[:, 0, :, c0:c1])

        def load_w2(part):
            c0, c1 = W2_PARTS[part]
            size = W2_EXPERTS[part]
            for e0 in range(0, E, size):
                load_packed(w2_w[part][e0 // size], w2_words[e0 : e0 + size, 0, :, 2 * c0 : 2 * c1])

        nc.sync.dma_start(out=x_w[:], in_=x_words[0].rearrange("p t d -> p (t d)").bitcast(I32))
        nc.sync.dma_start(token_list[:], offs)
        nc.sync.dma_start(partner_list[:], offs2)
        load_scale_rows(nc, x_s[:], x_scales)
        for e in range(E):
            nc.sync.dma_start(out=wp_raw[e][:], in_=wp[e].rearrange("(p d) c -> p d c", d=PACK))
            if e == 1:
                for c0, c1 in GATE_ROW_LOADS:
                    nc.sync.dma_start(out=gate_rows[c0:c1, :], in_=gate[1, 0, c0 * P : c1 * P].rearrange("(c t) -> c t", t=P))
            if e == LISTS_BEHIND:
                nc.sync.dma_start(slot_lists[0][:], pos1)
                nc.sync.dma_start(slot_lists[1][:], pos2)
            if e == W1_LOADS[0][2]:
                load_scale_rows(nc, w1_s[:], w1_scales[:, 0])
            for part, (e0, e1, behind) in enumerate(W1_LOADS):
                if behind == e:
                    load_packed(w1_w[part], w1_words[e0:e1, 0])
        load_w2_scales(0)
        load_w2(0)
        load_w2_scales(1)
        nc.sync.dma_start(out=gates[0][:], in_=gate[0])
        load_w2_scales(2)
        load_w2(1)

        turned_rows = in_bank("turned_rows", [P, P], Y_BANKS[0])
        nc.tensor.transpose(turned_rows[:], gate_rows[:], ident[:])
        nc.scalar.copy(gate_by_token[:], turned_rows[:, 0 : T // P])

        gathered, wp_bf, wp_q, pre, rectified, turned, h_bf, h_q = {}, {}, {}, {}, {}, {}, {}, {}
        alone = CAST_ON_VECTOR.index(H)

        def gather(g, sort):
            is_scale, is_partner = divmod(sort, 2)
            columns = GROUP * C // PER_COLUMN
            entries = (partner_list if is_partner else token_list)[:, g * columns : (g + 1) * columns]
            window = x_s[:, 0, :] if is_scale else x_w[:].bitcast(U32)
            region = 0 if g + 1 == E // GROUP else E
            picked = staged("gathered%d_%d" % (g, sort), [P, GROUP * C], U8 if is_scale else U32, region, GATHERED_AT[sort])
            nc.vector.tensor_copy(picked[:], window.indirect(entries))
            gathered[(g, sort)] = picked

        def cast(e):
            wp_bf[e] = rounded.tile([P, H, PACK], BF16, name="wp_bf%d" % e, align_bytes=64, offset=e % BF_BUFFERS * 2 * H * PACK)
            split = CAST_ON_VECTOR[e]
            shares = [(nc.scalar.copy, split, H), (nc.vector.tensor_copy, 0, min(split, H // 2)), (nc.vector.tensor_copy, H // 2, split)]
            for engine_copy, c0, c1 in [share for share in shares if share[1] < share[2]]:
                engine_copy(
                    wp_bf[e][:, c0:c1, :].rearrange("p (c w) d -> p c d w", w=4),
                    wp_raw[e][:, :, c0:c1].rearrange("p d (c w) -> p c d w", w=4),
                )

        def column_pieces(e):
            return [(0, H // 2), (H // 2, H)] if CAST_ON_VECTOR[e] else [(0, H)]

        def quantize_wp(e, pieces):
            if e not in wp_q:
                words_at, scales_at = UNDER_GATHERED if e == 0 else (WORDS_AT, SCALES_AT)
                region = 0 if e == 0 else E if e == 2 else e - 2
                wp_q[e] = (staged("wp_w%d" % e, [P, H], U32, region, words_at), staged("wp_s%d" % e, [P, H], U8, region, scales_at))
            wp_w, wp_s = wp_q[e]
            for c0, c1 in pieces:
                nc.vector.quantize_mx(
                    out=wp_w[:, c0:c1].bitcast(FP8X4), scales=wp_s[:, c0:c1], in_=wp_bf[e][:, c0:c1, :].rearrange("p c d -> p (c d)")
                )

        def first_layer(e):
            pre[e] = in_bank("pre%d" % e, [P, H], PRE_BANKS[e % len(PRE_BANKS)])
            slots = slice(e % GROUP * C, (e % GROUP + 1) * C)
            token_w, partner_w, token_s, partner_s = [gathered[(e // GROUP, sort)][:, slots] for sort in range(SORTS)]
            part = min(n for n, load in enumerate(W1_LOADS) if e < load[1])
            passes = [(0, H, token_w, token_s, w1_w[part][:, e - W1_LOADS[part][0], :].bitcast(FP4X4), w1_s[:, e, :])]
            passes.extend(
                (c0, c1, partner_w, partner_s, wp_q[e][0][:, c0:c1].bitcast(FP8X4), wp_q[e][1][:, c0:c1])
                for c0, c1 in (column_pieces(e) if e + 1 == E else [(0, H)])
            )
            if W1_LOADS[part][2] > e >= alone:
                passes.reverse()
            for place, (c0, c1, slot_w, slot_s, weight_w, weight_s) in enumerate(passes):
                nc.tensor.matmul_mx(
                    out=pre[e][:, c0:c1],
                    lhsT=slot_w.bitcast(FP8X4),
                    lhsT_scale=slot_s,
                    rhs=weight_w,
                    rhs_scale=weight_s,
                    start=(place == 0),
                    stop=(place + 1 == len(passes)),
                )

        def rectify(e):
            region = E if e + 3 == E else e + 1 if e + 1 >= alone else alone - 1 if e == 2 else e
            relu = staged("relu%d" % e, [P, PACK, P], F32, region, RELU_AT)
            rectified[e] = relu
            for c0, c1 in column_pieces(e) if e + 1 == E else [(0, H)]:
                planes = slice(c0 // P, c1 // P)
                by_plane = pre[e][:].rearrange("u (p d) -> u d p", d=PACK)[:, planes, :]
                if e + 2 == E:
                    nc.vector.tensor_scalar_max(relu[:, planes, :], by_plane, 0.0)
                else:
                    nc.scalar.activation(relu[:, planes, :], by_plane, ACT.Relu)

        def turn(e):
            relu = rectified[e]
            turned[e] = in_bank("turned%d" % e, [P, PACK, C], TURNED_BANKS[e % len(TURNED_BANKS)])
            for d in range(PACK):
                nc.tensor.transpose(turned[e][:, d, :], relu[:, d, :], ident[:])

        def hidden_place(e):
            if e < 2 or e in (E - 4, E - 2, E - 1):
                return E, 0
            return (e + 3, HIDDEN_AT) if e + 3 <= CAUGHT_UP else (e + 2, HIDDEN_AT + 2 * C * PACK)

        def square(e):
            e0, e1 = min(group for group in H_GROUPS if e < group[1])
            if e == e0:
                h_bf[e0] = staged("h_bf%d" % e, [P, e1 - e0, C, PACK], BF16, *hidden_place(e))
            nc.scalar.activation(h_bf[e0][:, e - e0, :, :], turned[e][:].rearrange("p d u -> p u d"), ACT.Square)

        def quantize_h(e0, e1):
            h_w = keep.tile([P, (e1 - e0) * C], U32, name="h_w%d" % e0, align_bytes=64)
            h_s = staged("h_s%d" % e0, [P, (e1 - e0) * C], U8, E - 3, WORDS_AT + e0 * C)
            nc.vector.quantize_mx(out=h_w[:].bitcast(FP8X4), scales=h_s[:], in_=h_bf[e0][:].rearrange("p e u d -> p (e u d)"))
            for e in range(e0, e1):
                h_q[e] = (h_w[:, (e - e0) * C : (e - e0 + 1) * C], h_s[:, (e - e0) * C : (e - e0 + 1) * C])

        for g, sort in ((0, 0), (1, 0), (0, 1), (0, 2), (0, 3), (1, 1), (1, 2), (1, 3)):
            gather(g, sort)
        for step in range(E):
            cast(step)
            quantize_wp(step, column_pieces(step))
            if step == LAST_GATHERS_STEP:
                for sort in range(SORTS):
                    gather(E // GROUP - 1, sort)
            if step == len(PRE_BANKS):
                rectify(0)
            if step == alone - 1:
                rectify(1)
            first_layer(step)
            if step == len(PRE_BANKS):
                turn(0)
            if step == alone - 1:
                turn(1)
                square(0)
                rectify(2)
                turn(2)
                square(1)
                rectify(3)
                turn(3)
            if step >= alone and step + 2 != E:
                square(step - 3 if step <= CAUGHT_UP else step - 2)
                rectify(step - 1)
                turn(step - 1)
            if step == CAUGHT_UP:
                square(step - 2)
            if step + 3 == E:
                rectify(step)
                turn(step)
                square(step - 1)
        rectify(E - 1)
        turn(E - 1)
        square(E - 2)
        square(E - 1)
        for group in H_GROUPS:
            quantize_h(*group)

        def second_layer(b, bank, experts, engine_copy):
            bank_tile = in_bank("y_bank%d_%d" % (b, experts[0]), [P, len(experts) * C], bank)
            part = min(n for n, cols in enumerate(W2_PARTS) if b * P < cols[1])
            c0 = b * P - W2_PARTS[part][0]
            scale_part = min(b, len(W2_SCALE_PARTS) - 1)
            s0 = b * P - W2_SCALE_PARTS[scale_part][0]
            for place, e in enumerate(experts):
                nc.tensor.matmul_mx(
                    out=bank_tile[:, place * C : (place + 1) * C],
                    lhsT=w2_w[part][e // W2_EXPERTS[part]][:, e % W2_EXPERTS[part], 2 * c0 : 2 * (c0 + P)].bitcast(FP4X4),
                    lhsT_scale=w2_s[scale_part][:, e, s0 : s0 + P],
                    rhs=h_q[e][0].bitcast(FP8X4),
                    rhs_scale=h_q[e][1],
                    start=True,
                    stop=True,
                )
            engine_copy(y[b][:, experts[0] * C : (experts[-1] + 1) * C], bank_tile[:])

        used = [H_WORDS_AT if e == E - 3 else 0 for e in range(E)]

        def spare(name, width):
            region = min(e for e in range(E) if used[e] + 4 * width <= H_WORDS_AT)
            at = region * REGION + used[region]
            used[region] = used[region] + 4 * width
            return stage.tile([P, width], F32, name=name, align_bytes=64, offset=at)

        def weigh(b, r, t0, t1):
            part = spare("part%d_%d_%d" % (b, r, t0), t1 - t0)
            entries = slot_lists[r][:, t0 // PER_COLUMN : t1 // PER_COLUMN]
            nc.vector.tensor_tensor(part[:], y[b][:].indirect(entries), gates[r][:, t0:t1], ALU.mult)
            return part

        def add_and_store(b, t0, t1, first, second, engine=nc.vector):
            total = spare("total%d_%d" % (b, t0), t1 - t0)
            engine.tensor_tensor(total[:], first, second, ALU.add)
            nc.sync.dma_start(out=out[b * P : (b + 1) * P, t0:t1], in_=total[:])

        def products(b, groups, banks):
            for g, bank in zip(groups, banks):
                second_layer(b, bank, range(g * GROUP, (g + 1) * GROUP), nc.scalar.copy)

        def spread_gate(banks):
            for (t0, t1), bank in zip(HALVES, banks):
                spread = in_bank("spread%d" % t0, [P, HALF], bank)
                for col in range(t0, t1, P):
                    column = gate_by_token[:, col // P : col // P + 1]
                    nc.tensor.transpose(spread[:, col - t0 : col - t0 + P], column.to_broadcast([P, P]), ident[:])
                nc.scalar.copy(gates[1][:, t0:t1], spread[:])

        def pick(b, t0, t1, bank):
            picked = spare("picked%d_%d" % (b, t0), t1 - t0)
            nc.scalar.activation(picked[:], y[b][:].indirect(slot_lists[1][:, t0 // PER_COLUMN : t1 // PER_COLUMN]), ACT.Copy)
            there = in_bank("there%d_%d" % (b, t0), [P, t1 - t0], bank)
            for col in range(0, t1 - t0, P):
                nc.tensor.transpose(there[:, col : col + P], picked[:, col : col + P], ident[:])
            return there

        def scale(b, t0, t1, there):
            scaled = spare("scaled%d_%d" % (b, t0), t1 - t0)
            for col in range(0, t1 - t0, P):
                chunk = (t0 + col) // P
                nc.scalar.activation(
                    scaled[:, col : col + P], there[:, col : col + P], ACT.Copy, scale=gate_by_token[:, chunk : chunk + 1]
                )
            return scaled

        def turn_back(b, t0, t1, scaled, bank):
            back = in_bank("back%d_%d" % (b, t0), [P, t1 - t0], bank)
            for col in range(0, t1 - t0, P):
                nc.tensor.transpose(back[:, col : col + P], scaled[:, col : col + P], ident[:])
            return back

        def add_in_place(b, first, backs):
            for (t0, t1), back in zip(HALVES, backs):
                nc.vector.tensor_tensor(first[:, t0:t1], first[:, t0:t1], back[:], ALU.add)
            nc.sync.dma_start(out=out[b * P : (b + 1) * P, :], in_=first[:])

        second_layer(0, 5, range(0, GROUP), nc.scalar.copy)
        second_layer(0, 6, range(GROUP, 2 * GROUP), nc.vector.tensor_copy)
        second_layer(0, 7, range(2 * GROUP, E - 1), nc.scalar.copy)
        second_layer(0, 0, range(E - 1, E), nc.scalar.copy)
        second_layer(1, 1, range(0, GROUP), nc.vector.tensor_copy)
        products(1, (1, 2), (2, 3))
        spread_gate((1, 2))
        firsts = [weigh(b, 0, 0, T) for b in range(2)]
        second = weigh(0, 1, 0, T)
        theres = [pick(1, *tokens, bank) for tokens, bank in zip(HALVES, (4, 0))]
        scaled = [scale(1, *tokens, there) for tokens, there in zip(HALVES, theres)]
        products(2, (0, 1), (5, 6))
        second_layer(2, 7, range(2 * GROUP, E), nc.vector.tensor_copy)
        add_and_store(0, 0, T, firsts[0][:], second[:])
        firsts.append(weigh(2, 0, 0, T))
        products(3, (0, 1, 2), (1, 2, 3))
        backs = [turn_back(1, *tokens, part, bank) for tokens, part, bank in zip(HALVES, scaled, (1, 2))]
        add_in_place(1, firsts[1], backs)
        parts = [weigh(3, r, LAST_SHARE, T) for r in range(2)]
        firsts.append(weigh(3, 0, 0, LAST_SHARE))
        theres = [pick(2, *tokens, bank) for tokens, bank in zip(HALVES, (5, 4))]
        add_and_store(3, LAST_SHARE, T, parts[0][:], parts[1][:])
        there = pick(3, 0, LAST_SHARE, 6)
        backs = [turn_back(2, *HALVES[0], scale(2, *HALVES[0], theres[0]), 0)]
        backs.append(turn_back(2, *HALVES[1], scale(2, *HALVES[1], theres[1]), 7))
        for (t0, t1), back in zip(HALVES, backs):
            add_and_store(2, t0, t1, firsts[2][:, t0:t1], back[:])
        scaled = scale(3, 0, LAST_SHARE, there)
        for (t0, t1), bank in zip(((0, LAST_SHARE - P), (LAST_SHARE - P, LAST_SHARE)), (3, 1)):
            add_and_store(3, t0, t1, firsts[3][:, t0:t1], turn_back(3, t0, t1, scaled[:, t0:t1], bank)[:])
